import numpy as np
import ml_dtypes


def mxq(x, axis, fmt="e4m3"):
    dtype, down = {"e4m3": (ml_dtypes.float8_e4m3fn, 7), "e5m2": (ml_dtypes.float8_e5m2, 14)}[fmt]
    v = np.moveaxis(np.asarray(x, np.float32).astype(ml_dtypes.bfloat16).astype(np.float64), axis, -1)
    blocks = v.reshape(v.shape[:-1] + (-1, 32))
    amax = np.abs(blocks).max(-1, keepdims=True)
    byte = np.maximum(np.where(amax > 0, np.frexp(amax)[1] - 1 + 127, 0) - down, 1)
    scale = np.exp2(byte - 127.0)
    codes = (blocks / scale).astype(np.float32).astype(dtype).astype(np.float64)
    return np.moveaxis((codes * scale).reshape(v.shape), -1, axis)


WIDE = False


def mx_kscale(k):
    if not WIDE:
        return np.ones(k)
    levels = np.array([10, -10, 5, -5, 0])
    if k % 512:
        return np.exp2(np.random.permutation(np.resize(levels, k // 32))).repeat(32)
    a = np.empty((k // 512, 16))
    for p in range(k // 512):
        a[p, :8] = np.random.permutation(np.resize(levels, 8))
        for g in range(8):
            far = levels[np.abs(levels - a[p, g]) >= 10]
            a[p, g + 8] = far[np.random.randint(len(far))]
    return np.exp2(a.ravel()).repeat(32)


def f64(x):
    return np.asarray(x).astype(np.float64)


def striped(idx):
    return np.tile(idx.reshape(-1, 16).T, (8, 1)).astype(np.uint16)


def unstriped(offs):
    return offs[:16].T.reshape(-1).astype(np.int64)


E2M1 = np.array([0.0, 0.5, 1.0, 1.5, 2.0, 3.0, 4.0, 6.0, -0.0, -0.5, -1.0, -1.5, -2.0, -3.0, -4.0, -6.0])


def pack_weight(w, fmt):
    k, n = w.shape
    w = f64(np.asarray(w, np.float32).astype(ml_dtypes.bfloat16)).reshape(k // 32, 32, n)
    amax = np.abs(w).max(1)
    if fmt == "e4m3":
        byte = np.frexp(amax)[1] - 1 + 127 - 7
    else:
        mant, ex = np.frexp(amax / 6.0)
        byte = np.where(mant > 0.5, ex, ex - 1) + 127
    byte = np.clip(np.where(amax > 0, byte, 1), 1, 254)
    scaled = (w * np.exp2(127.0 - byte)[:, None, :]).reshape(k, n).astype(np.float32)
    by_word = np.ascontiguousarray(scaled.reshape(k // 512, 128, 4, n).transpose(0, 1, 3, 2))
    if fmt == "e4m3":
        words = by_word.astype(ml_dtypes.float8_e4m3fn).view(np.uint8)
    else:
        c = by_word.astype(ml_dtypes.float4_e2m1fn).view(np.uint8) & 0xF
        words = (c[..., 0::2] | (c[..., 1::2] << 4)).reshape(k // 512, 128, 2 * n)
    return np.ascontiguousarray(words), np.ascontiguousarray(byte.astype(np.uint8).reshape(k // 512, 16, n))


def unpack_weight(words, scales, fmt):
    g, _, n = scales.shape
    words = np.ascontiguousarray(words).reshape(g, 128, n, -1)
    if fmt == "e4m3":
        vals = words.view(ml_dtypes.float8_e4m3fn).astype(np.float64)
    else:
        nib = np.empty((g, 128, n, 4), np.uint8)
        nib[..., 0::2] = words & 0xF
        nib[..., 1::2] = words >> 4
        vals = E2M1[nib]
    vals = vals * np.repeat(np.exp2(scales.astype(np.float64) - 127.0), 8, axis=1)[..., None]
    return vals.transpose(0, 1, 3, 2).reshape(g * 512, n)


def d_silu(v):
    s = 1.0 / (1.0 + np.exp(-np.maximum(v, -700.0)))
    return s * (1.0 + v * (1.0 - s))


K, T, G, C1, E, C2, H = 512, 1024, 4, 256, 8, 128, 512
N = 512


def by_expert(wq, xq, E, C):
    return np.concatenate([wq[e].T @ xq[:, e * C:(e + 1) * C] for e in range(E)], axis=1)


def setup_inputs():
    n = np.random.standard_normal
    v = mx_kscale(N)
    u = mx_kscale(H)
    slots1 = np.random.permutation(T)
    slots2 = np.concatenate([q * C1 + np.random.permutation(C1) for q in range(G)])
    dy = pack_weight(n((N, T)) * v[:, None], "e4m3")
    wgt = [pack_weight(m, "e4m3") for m in n((G, H, K)) / np.sqrt(H) / u[None, :, None]]
    return {
        "dy_words": dy[0],
        "dy_scales": dy[1],
        "wet": (n((E, N, H)) / np.sqrt(N) / v[None, :, None] * u).astype(np.float32),
        "wgt_words": np.stack([m[0] for m in wgt]),
        "wgt_scales": np.stack([m[1] for m in wgt]),
        "a": (n((H, T))).astype(np.float32),
        "gate": (np.tile(np.random.uniform(0.2, 1.0, T), (128, 1))).astype(np.float32),
        "offs": striped(slots1),
        "offs2": striped(slots2),
        "dst": striped(slots1[slots2]),
    }


def reference(dy_words, dy_scales, wet, wgt_words, wgt_scales, a, gate, offs, offs2, dst):
    wetq = mxq(f64(wet), 1, "e4m3")
    wgt = np.stack([unpack_weight(wgt_words[e], wgt_scales[e], "e4m3") for e in range(G)])
    gq = unpack_weight(dy_words, dy_scales, "e4m3")[:, unstriped(dst)]
    z = f64(gate[:1]) * by_expert(wetq, gq, E, C2)
    da = np.zeros((H, T))
    da[:, unstriped(offs2)] = z
    dx = by_expert(wgt, mxq(da * d_silu(f64(a)), 0, "e4m3"), G, C1)
    out = np.zeros((K, T))
    out[:, unstriped(offs)] = dx
    return out

@@ -1,0 +1,231 @@
+from contextlib import ExitStack
+
+import concourse.mybir as mybir
+
+F32 = mybir.dt.float32
+BF16 = mybir.dt.bfloat16
+I32 = mybir.dt.int32
+U32 = mybir.dt.uint32
+U16 = mybir.dt.uint16
+U8 = mybir.dt.uint8
+FP8X4 = mybir.dt.float8_e4m3fn_x4
+ACT = mybir.ActivationFunctionType
+ALU = mybir.AluOpType
+
+P = 128
+PACK = 4
+T = 1024
+G, C1 = 4, 256
+E, C2 = 8, 128
+W = 512
+LIST = 16
+FLOPS = 2 * 2 * W * W * T
+
+
+def tile_moe_hib_silu_kernel(
+    tc, dy_words, dy_scales, wet, wgt_words, wgt_scales, a, gate, offs, offs2, dst, out
+):
+    nc = tc.nc
+    with ExitStack() as ctx:
+        held = ctx.enter_context(tc.tile_pool(name="held", bufs=1))
+        ring2 = ctx.enter_context(tc.tile_pool(name="ring2", bufs=2))
+        ring3 = ctx.enter_context(tc.tile_pool(name="ring3", bufs=3))
+        ring4 = ctx.enter_context(tc.tile_pool(name="ring4", bufs=4))
+        psum = ctx.enter_context(tc.psum_pool(name="psum", bufs=2))
+
+        offs_sb = held.tile([P, T // LIST], U16, name="offs_sb")
+        offs2_sb = held.tile([P, T // LIST], U16, name="offs2_sb")
+        dst_sb = held.tile([P, T // LIST], U16, name="dst_sb")
+        dy_w = held.tile([P, T], I32, name="dy_w", align_bytes=64)
+        dy_s = held.tile([P, T // 4], I32, name="dy_s", align_bytes=64)
+        slot_w = held.tile([P, T], U32, name="slot_w", align_bytes=64)
+        slot_s = held.tile([P, T], U8, name="slot_s", align_bytes=64)
+        wgt_s = held.tile([P, W], U8, name="wgt_s", align_bytes=64)
+        wgt_w = [held.tile([P, W], I32, name="wgt_w%d" % f, align_bytes=64) for f in range(G)]
+        gate_sb = [held.tile([P, C1], F32, name="gate%d" % f, align_bytes=64) for f in range(G)]
+        wet_c = [held.tile([P, W], U32, name="wet_c%d" % e, align_bytes=64) for e in range(E)]
+        wet_s = [held.tile([P, W], U8, name="wet_s%d" % e, align_bytes=64) for e in range(E)]
+        z_win = [
+            [held.tile([P, max(2, f + 1) * C1], F32, name="z_win%d_%d" % (f, t), align_bytes=64) for t in range(PACK)]
+            for f in range(G)
+        ]
+        out_sb = [held.tile([P, T], F32, name="out_sb%d" % c, align_bytes=64) for c in range(W // P)]
+
+        raw, grouped, a_sb, tanh_sb, silu_sb, z_sb, half_sb, da_bf, da_c, da_s, dx_sb = ({} for n in range(11))
+
+        def cols(first, count):
+            return slice(first // LIST, (first + count) // LIST)
+
+        def load_wet(e, parts):
+            raw[e] = ring4.tile([P, PACK, W], F32, name="raw", align_bytes=64)
+            rows = wet[e].rearrange("(p j) i -> p j i", j=PACK)
+            for h in range(parts):
+                part = slice(h * W // parts, (h + 1) * W // parts)
+                nc.sync.dma_start(out=raw[e][:, :, part], in_=rows[:, :, part])
+
+        def load_group(f):
+            a_sb[f] = ring3.tile([P, PACK, C1], F32, name="a_sb", align_bytes=64)
+            nc.sync.dma_start(out=a_sb[f][:], in_=a.rearrange("(q t) j -> q t j", t=PACK)[:, :, f * C1 : (f + 1) * C1])
+            nc.sync.dma_start(out=wgt_w[f][:], in_=wgt_words[f, 0].rearrange("p k d -> p (k d)").bitcast(I32))
+
+        def load_gate(f):
+            nc.sync.dma_start(out=gate_sb[f][:], in_=gate[:, f * C1 : (f + 1) * C1])
+
+        def round_wet(e, h, on_vector=False):
+            if h == 0:
+                grouped[e] = ring3.tile([P, PACK, P, PACK], BF16, name="grouped", align_bytes=64)
+            ms = slice(h * P // 2, (h + 1) * P // 2)
+            src = raw[e][:].rearrange("p j (m t) -> p m t j", t=PACK)[:, ms]
+            to = grouped[e][:].rearrange("p t m j -> p m t j")[:, ms]
+            if on_vector:
+                nc.vector.tensor_copy(out=to, in_=src)
+            else:
+                nc.scalar.copy(out=to, in_=src)
+
+        def quantize_wet(e):
+            nc.vector.quantize_mx(
+                out=wet_c[e][:].bitcast(FP8X4), scales=wet_s[e][:], in_=grouped[e][:].rearrange("p t m j -> p (t m j)")
+            )
+
+        def gather(first, count):
+            part = slice(first, first + count)
+            nc.vector.tensor_copy(slot_w[:, part], dy_w[:].bitcast(U32).indirect(dst_sb[:, cols(first, count)]))
+            nc.vector.tensor_copy(slot_s[:, part], dy_s[:].bitcast(U8).indirect(dst_sb[:, cols(first, count)]))
+
+        def expert_product(e):
+            f, u = divmod(e, 2)
+            if u == 0:
+                z_sb[f] = ring2.tile([P, PACK, C1], F32, name="z_sb", align_bytes=64)
+            bank = psum.tile([P, PACK, C2], F32, name="z_bank")
+            slots = slice(e * C2, (e + 1) * C2)
+            for t in range(PACK):
+                nc.tensor.matmul_mx(
+                    out=bank[:, t, :],
+                    lhsT=wet_c[e][:, t * P : (t + 1) * P].bitcast(FP8X4),
+                    lhsT_scale=wet_s[e][:, t * P : (t + 1) * P],
+                    rhs=slot_w[:, slots].bitcast(FP8X4),
+                    rhs_scale=slot_s[:, slots],
+                    start=True,
+                    stop=True,
+                )
+            nc.scalar.activation(out=z_sb[f][:, :, u * C2 : (u + 1) * C2], in_=bank[:], func=ACT.Copy, scale=-0.5)
+
+        def scatter_z(f, first, count):
+            part = slice(first, first + count)
+            for t in range(PACK):
+                nc.vector.tensor_tensor(
+                    z_win[f][t][:].indirect(offs2_sb[:, cols(f * C1 + first, count)]),
+                    z_sb[f][:, t, part],
+                    gate_sb[f][:, part],
+                    ALU.mult,
+                )
+
+        def activations(f):
+            tanh_sb[f] = ring3.tile([P, PACK, C1], F32, name="tanh_sb", align_bytes=64)
+            silu_sb[f] = ring3.tile([P, C1, PACK], F32, name="silu_sb", align_bytes=64)
+            nc.scalar.activation(out=silu_sb[f][:], in_=a_sb[f][:].rearrange("q t j -> q j t"), func=ACT.Silu, scale=-1.0)
+            nc.scalar.activation(out=tanh_sb[f][:], in_=a_sb[f][:], func=ACT.Tanh, scale=0.5)
+
+        def times_sigmoid(f):
+            half_sb[f] = ring2.tile([P, PACK, C1], F32, name="half_sb", align_bytes=64)
+            for t in range(PACK):
+                nc.vector.scalar_tensor_tensor(
+                    half_sb[f][:, t, :], tanh_sb[f][:, t, :], 1.0, z_win[f][t][:, f * C1 : (f + 1) * C1], ALU.add, ALU.mult
+                )
+
+        def finish_da(f):
+            da_bf[f] = ring2.tile([P, C1, PACK], BF16, name="da_bf", align_bytes=64)
+            nc.vector.scalar_tensor_tensor(
+                da_bf[f][:], silu_sb[f][:], 1.0, half_sb[f][:].rearrange("q t j -> q j t"), ALU.subtract, ALU.mult
+            )
+
+        def quantize_da(f):
+            da_c[f] = ring2.tile([P, C1], U32, name="da_c", align_bytes=64)
+            da_s[f] = ring2.tile([P, C1], U8, name="da_s", align_bytes=64)
+            nc.vector.quantize_mx(
+                out=da_c[f][:].bitcast(FP8X4), scales=da_s[f][:], in_=da_bf[f][:].rearrange("q j t -> q (j t)")
+            )
+
+        def group_product(f):
+            dx_sb[f] = ring2.tile([P, W // P, C1], F32, name="dx_sb", align_bytes=64)
+            for b in range(2):
+                bank = psum.tile([P, 2, C1], F32, name="dx_bank")
+                for s in range(2):
+                    ks = slice((2 * b + s) * P, (2 * b + s + 1) * P)
+                    nc.tensor.matmul_mx(
+                        out=bank[:, s, :],
+                        lhsT=wgt_w[f][:, ks].bitcast(FP8X4),
+                        lhsT_scale=wgt_s[PACK * f : P, ks],
+                        rhs=da_c[f][:].bitcast(FP8X4),
+                        rhs_scale=da_s[f][:],
+                        start=True,
+                        stop=True,
+                    )
+                nc.scalar.copy(out=dx_sb[f][:, 2 * b : 2 * b + 2, :], in_=bank[:])
+
+        def scatter_dx(f, c):
+            nc.vector.tensor_copy(out_sb[c][:].indirect(offs_sb[:, cols(f * C1, C1)]), dx_sb[f][:, c, :])
+            if f == G - 1:
+                nc.sync.dma_start(out=out[c * P : (c + 1) * P, :], in_=out_sb[c][:])
+
+        nc.vector.memset(dy_s[:], 0)
+        nc.gpsimd.memset(wgt_s[:].bitcast(I32), 0)
+        nc.sync.dma_start(dst_sb[:], dst)
+        for q in range(4):
+            nc.sync.dma_start(out=dy_s[32 * q : 32 * q + 4, :], in_=dy_scales[0, 4 * q : 4 * q + 4, :].bitcast(I32))
+        load_wet(0, 2)
+        nc.sync.dma_start(out=dy_w[:], in_=dy_words[0].rearrange("p t d -> p (t d)").bitcast(I32))
+        for q in range(4):
+            nc.gpsimd.dma_start(
+                out=wgt_s[32 * q : 32 * q + 16, :].bitcast(I32), in_=wgt_scales[:, 0, 4 * q : 4 * q + 4, :].bitcast(I32)
+            )
+        nc.sync.dma_start(offs2_sb[:], offs2)
+        load_gate(0)
+        load_wet(1, 1)
+        load_group(0)
+        nc.sync.dma_start(offs_sb[:], offs)
+
+        round_wet(0, 0)
+        round_wet(0, 1, on_vector=True)
+        quantize_wet(0)
+        gather(0, C1)
+        expert_product(0)
+        round_wet(1, 0)
+        round_wet(1, 1)
+        gather(C1, C1)
+        gather(2 * C1, 2 * C1)
+        scatter_z(0, 0, C2)
+        quantize_wet(1)
+        expert_product(1)
+        activations(0)
+        scatter_z(0, C2, C2)
+
+        for f in range(G):
+            if f + 1 < G:
+                load_wet(2 * f + 2, 1)
+                load_wet(2 * f + 3, 1)
+                load_gate(f + 1)
+                load_group(f + 1)
+                for e in (2 * f + 2, 2 * f + 3):
+                    round_wet(e, 0)
+                    round_wet(e, 1)
+            times_sigmoid(f)
+            if f + 1 < G:
+                quantize_wet(2 * f + 2)
+                expert_product(2 * f + 2)
+            finish_da(f)
+            if f + 1 < G:
+                quantize_wet(2 * f + 3)
+                expert_product(2 * f + 3)
+                activations(f + 1)
+            if f > 0:
+                scatter_dx(f - 1, 0)
+            quantize_da(f)
+            group_product(f)
+            if f > 0:
+                for c in range(1, W // P):
+                    scatter_dx(f - 1, c)
+            if f + 1 < G:
+                scatter_z(f + 1, 0, C1)
+        for c in range(W // P):
+            scatter_dx(G - 1, c)

@@ -29,8 +29,6 @@ def tile_moe_hib_silu_kernel(
     with ExitStack() as ctx:
         held = ctx.enter_context(tc.tile_pool(name="held", bufs=1))
         ring2 = ctx.enter_context(tc.tile_pool(name="ring2", bufs=2))
-        ring3 = ctx.enter_context(tc.tile_pool(name="ring3", bufs=3))
-        ring4 = ctx.enter_context(tc.tile_pool(name="ring4", bufs=4))
         psum = ctx.enter_context(tc.psum_pool(name="psum", bufs=2))
 
         offs_sb = held.tile([P, T // LIST], U16, name="offs_sb")
@@ -38,8 +36,8 @@ def tile_moe_hib_silu_kernel(
         dst_sb = held.tile([P, T // LIST], U16, name="dst_sb")
         dy_w = held.tile([P, T], I32, name="dy_w", align_bytes=64)
         dy_s = held.tile([P, T // 4], I32, name="dy_s", align_bytes=64)
-        slot_w = held.tile([P, T], U32, name="slot_w", align_bytes=64)
-        slot_s = held.tile([P, T], U8, name="slot_s", align_bytes=64)
+        zero = held.tile([P, 1], F32, name="zero")
+        no_bias = held.tile([P, 1], F32, name="no_bias")
         wgt_s = held.tile([P, W], U8, name="wgt_s", align_bytes=64)
         wgt_w = [held.tile([P, W], I32, name="wgt_w%d" % f, align_bytes=64) for f in range(G)]
         gate_sb = [held.tile([P, C1], F32, name="gate%d" % f, align_bytes=64) for f in range(G)]
@@ -49,22 +47,28 @@ def tile_moe_hib_silu_kernel(
             [held.tile([P, max(2, f + 1) * C1], F32, name="z_win%d_%d" % (f, t), align_bytes=64) for t in range(PACK)]
             for f in range(G)
         ]
-        out_sb = [held.tile([P, T], F32, name="out_sb%d" % c, align_bytes=64) for c in range(W // P)]
 
         raw, grouped, a_sb, tanh_sb, silu_sb, z_sb, half_sb, da_bf, da_c, da_s, dx_sb = ({} for n in range(11))
+        slot_w, slot_s, out_sb = {}, {}, {}
+
+        def place(shape, dtype, name, after=None):
+            return held.tile(shape, dtype, name=name, tag=after or name, align_bytes=64)
 
         def cols(first, count):
             return slice(first // LIST, (first + count) // LIST)
 
         def load_wet(e, parts):
-            raw[e] = ring4.tile([P, PACK, W], F32, name="raw", align_bytes=64)
+            if e % 2 and e > 1:
+                raw[e] = place([P, PACK, W], F32, "raw%d" % e)
+            else:
+                raw[e] = ring2.tile([P, PACK, W], F32, name="raw", align_bytes=64)
             rows = wet[e].rearrange("(p j) i -> p j i", j=PACK)
             for h in range(parts):
                 part = slice(h * W // parts, (h + 1) * W // parts)
                 nc.sync.dma_start(out=raw[e][:, :, part], in_=rows[:, :, part])
 
         def load_group(f):
-            a_sb[f] = ring3.tile([P, PACK, C1], F32, name="a_sb", align_bytes=64)
+            a_sb[f] = ring2.tile([P, PACK, C1], F32, name="a_sb", align_bytes=64)
             nc.sync.dma_start(out=a_sb[f][:], in_=a.rearrange("(q t) j -> q t j", t=PACK)[:, :, f * C1 : (f + 1) * C1])
             nc.sync.dma_start(out=wgt_w[f][:], in_=wgt_words[f, 0].rearrange("p k d -> p (k d)").bitcast(I32))
 
@@ -73,7 +77,10 @@ def tile_moe_hib_silu_kernel(
 
         def round_wet(e, h, on_vector=False):
             if h == 0:
-                grouped[e] = ring3.tile([P, PACK, P, PACK], BF16, name="grouped", align_bytes=64)
+                if e % 2 and e > 1:
+                    grouped[e] = place([P, PACK, P, PACK], BF16, "grouped%d" % e)
+                else:
+                    grouped[e] = ring2.tile([P, PACK, P, PACK], BF16, name="grouped", align_bytes=64)
             ms = slice(h * P // 2, (h + 1) * P // 2)
             src = raw[e][:].rearrange("p j (m t) -> p m t j", t=PACK)[:, ms]
             to = grouped[e][:].rearrange("p t m j -> p m t j")[:, ms]
@@ -87,24 +94,25 @@ def tile_moe_hib_silu_kernel(
                 out=wet_c[e][:].bitcast(FP8X4), scales=wet_s[e][:], in_=grouped[e][:].rearrange("p t m j -> p (t m j)")
             )
 
-        def gather(first, count):
-            part = slice(first, first + count)
-            nc.vector.tensor_copy(slot_w[:, part], dy_w[:].bitcast(U32).indirect(dst_sb[:, cols(first, count)]))
-            nc.vector.tensor_copy(slot_s[:, part], dy_s[:].bitcast(U8).indirect(dst_sb[:, cols(first, count)]))
+        def gather(f):
+            slot_w[f] = place([P, C1], U32, "slot_w%d" % f, "da_bf0" if f == G - 1 else None)
+            slot_s[f] = place([P, C1], U8, "slot_s%d" % f, "half0" if f == G - 1 else None)
+            nc.vector.tensor_copy(slot_w[f][:], dy_w[:].bitcast(U32).indirect(dst_sb[:, cols(f * C1, C1)]))
+            nc.vector.tensor_copy(slot_s[f][:], dy_s[:].bitcast(U8).indirect(dst_sb[:, cols(f * C1, C1)]))
 
         def expert_product(e):
             f, u = divmod(e, 2)
             if u == 0:
-                z_sb[f] = ring2.tile([P, PACK, C1], F32, name="z_sb", align_bytes=64)
+                z_sb[f] = place([P, PACK, C1], F32, "z_sb%d" % f, "raw%d" % (e + 1) if f else None)
             bank = psum.tile([P, PACK, C2], F32, name="z_bank")
-            slots = slice(e * C2, (e + 1) * C2)
+            slots = slice(u * C2, (u + 1) * C2)
             for t in range(PACK):
                 nc.tensor.matmul_mx(
                     out=bank[:, t, :],
                     lhsT=wet_c[e][:, t * P : (t + 1) * P].bitcast(FP8X4),
                     lhsT_scale=wet_s[e][:, t * P : (t + 1) * P],
-                    rhs=slot_w[:, slots].bitcast(FP8X4),
-                    rhs_scale=slot_s[:, slots],
+                    rhs=slot_w[f][:, slots].bitcast(FP8X4),
+                    rhs_scale=slot_s[f][:, slots],
                     start=True,
                     stop=True,
                 )
@@ -121,20 +129,23 @@ def tile_moe_hib_silu_kernel(
                 )
 
         def activations(f):
-            tanh_sb[f] = ring3.tile([P, PACK, C1], F32, name="tanh_sb", align_bytes=64)
-            silu_sb[f] = ring3.tile([P, C1, PACK], F32, name="silu_sb", align_bytes=64)
-            nc.scalar.activation(out=silu_sb[f][:], in_=a_sb[f][:].rearrange("q t j -> q j t"), func=ACT.Silu, scale=-1.0)
-            nc.scalar.activation(out=tanh_sb[f][:], in_=a_sb[f][:], func=ACT.Tanh, scale=0.5)
+            if f == G - 1:
+                tanh_sb[f] = place([P, PACK, C1], F32, "tanh_last")
+            else:
+                tanh_sb[f] = ring2.tile([P, PACK, C1], F32, name="tanh_sb", align_bytes=64)
+            silu_sb[f] = ring2.tile([P, C1, PACK], F32, name="silu_sb", align_bytes=64)
+            nc.scalar.activation(out=silu_sb[f][:], in_=a_sb[f][:].rearrange("q t j -> q j t"), func=ACT.Silu, scale=-1.0, bias=no_bias[:])
+            nc.scalar.activation(out=tanh_sb[f][:], in_=a_sb[f][:], func=ACT.Tanh, scale=0.5, bias=no_bias[:])
 
         def times_sigmoid(f):
-            half_sb[f] = ring2.tile([P, PACK, C1], F32, name="half_sb", align_bytes=64)
+            half_sb[f] = place([P, PACK, C1], F32, "half%d" % f, {1: "grouped5", 2: "grouped7", 3: "z_sb0"}.get(f))
             for t in range(PACK):
                 nc.vector.scalar_tensor_tensor(
                     half_sb[f][:, t, :], tanh_sb[f][:, t, :], 1.0, z_win[f][t][:, f * C1 : (f + 1) * C1], ALU.add, ALU.mult
                 )
 
         def finish_da(f):
-            da_bf[f] = ring2.tile([P, C1, PACK], BF16, name="da_bf", align_bytes=64)
+            da_bf[f] = place([P, C1, PACK], BF16, "da_bf%d" % f)
             nc.vector.scalar_tensor_tensor(
                 da_bf[f][:], silu_sb[f][:], 1.0, half_sb[f][:].rearrange("q t j -> q j t"), ALU.subtract, ALU.mult
             )
@@ -147,9 +158,12 @@ def tile_moe_hib_silu_kernel(
             )
 
         def group_product(f):
-            dx_sb[f] = ring2.tile([P, W // P, C1], F32, name="dx_sb", align_bytes=64)
+            if f == G - 2:
+                dx_sb[f] = place([P, W // P, C1], F32, "dx_sb%d" % f, "tanh_last")
+            else:
+                dx_sb[f] = ring2.tile([P, W // P, C1], F32, name="dx_sb", align_bytes=64)
             for b in range(2):
-                bank = psum.tile([P, 2, C1], F32, name="dx_bank")
+                bank = psum.tile([P, 2, C1], F32, name="dx_bank", bufs=4)
                 for s in range(2):
                     ks = slice((2 * b + s) * P, (2 * b + s + 1) * P)
                     nc.tensor.matmul_mx(
@@ -164,6 +178,8 @@ def tile_moe_hib_silu_kernel(
                 nc.scalar.copy(out=dx_sb[f][:, 2 * b : 2 * b + 2, :], in_=bank[:])
 
         def scatter_dx(f, c):
+            if f == 0:
+                out_sb[c] = place([P, T], F32, "out_sb%d" % c, "grouped3" if c == W // P - 1 else None)
             nc.vector.tensor_copy(out_sb[c][:].indirect(offs_sb[:, cols(f * C1, C1)]), dx_sb[f][:, c, :])
             if f == G - 1:
                 nc.sync.dma_start(out=out[c * P : (c + 1) * P, :], in_=out_sb[c][:])
@@ -185,47 +201,60 @@ def tile_moe_hib_silu_kernel(
         load_group(0)
         nc.sync.dma_start(offs_sb[:], offs)
 
+        nc.vector.memset(zero[:], 0.0)
+        nc.scalar.activation(out=no_bias[:], in_=zero[:], func=ACT.Silu)
+
         round_wet(0, 0)
         round_wet(0, 1, on_vector=True)
         quantize_wet(0)
-        gather(0, C1)
+        gather(0)
         expert_product(0)
         round_wet(1, 0)
         round_wet(1, 1)
-        gather(C1, C1)
-        gather(2 * C1, 2 * C1)
-        scatter_z(0, 0, C2)
+        gather(1)
         quantize_wet(1)
+        scatter_z(0, 0, C2)
         expert_product(1)
         activations(0)
+        gather(2)
         scatter_z(0, C2, C2)
 
         for f in range(G):
-            if f + 1 < G:
-                load_wet(2 * f + 2, 1)
-                load_wet(2 * f + 3, 1)
+            pair = (2 * f + 2, 2 * f + 3) if f + 1 < G else ()
+            for e in pair:
+                load_wet(e, 1)
+            if pair:
                 load_gate(f + 1)
                 load_group(f + 1)
-                for e in (2 * f + 2, 2 * f + 3):
-                    round_wet(e, 0)
-                    round_wet(e, 1)
+            for e in pair:
+                round_wet(e, 0)
+                round_wet(e, 1)
+            if f > 0:
+                for e in pair:
+                    quantize_wet(e)
+                    expert_product(e)
             times_sigmoid(f)
-            if f + 1 < G:
-                quantize_wet(2 * f + 2)
-                expert_product(2 * f + 2)
             finish_da(f)
-            if f + 1 < G:
-                quantize_wet(2 * f + 3)
-                expert_product(2 * f + 3)
-                activations(f + 1)
-            if f > 0:
-                scatter_dx(f - 1, 0)
             quantize_da(f)
-            group_product(f)
-            if f > 0:
-                for c in range(1, W // P):
-                    scatter_dx(f - 1, c)
-            if f + 1 < G:
+            if f == 0:
+                gather(G - 1)
+                for e in pair:
+                    quantize_wet(e)
+                    expert_product(e)
+            if pair:
+                activations(f + 1)
+            if f == G - 1:
+                group_product(f - 1)
+            if f != G - 2:
+                group_product(f)
+            if f == 0:
+                for c in range(W // P):
+                    scatter_dx(0, c)
+            if pair:
                 scatter_z(f + 1, 0, C1)
-        for c in range(W // P):
-            scatter_dx(G - 1, c)
+            if f == 1:
+                for c in range(W // P):
+                    scatter_dx(1, c)
+        for f in (G - 2, G - 1):
+            for c in range(W // P):
+                scatter_dx(f, c)

@@ -41,15 +41,11 @@ def tile_moe_hib_silu_kernel(
         wgt_s = held.tile([P, W], U8, name="wgt_s", align_bytes=64)
         wgt_w = [held.tile([P, W], I32, name="wgt_w%d" % f, align_bytes=64) for f in range(G)]
         gate_sb = [held.tile([P, C1], F32, name="gate%d" % f, align_bytes=64) for f in range(G)]
-        wet_c = [held.tile([P, W], U32, name="wet_c%d" % e, align_bytes=64) for e in range(E)]
         wet_s = [held.tile([P, W], U8, name="wet_s%d" % e, align_bytes=64) for e in range(E)]
-        z_win = [
-            [held.tile([P, max(2, f + 1) * C1], F32, name="z_win%d_%d" % (f, t), align_bytes=64) for t in range(PACK)]
-            for f in range(G)
-        ]
 
         raw, grouped, a_sb, tanh_sb, silu_sb, z_sb, half_sb, da_bf, da_c, da_s, dx_sb = ({} for n in range(11))
-        slot_w, slot_s, out_sb = {}, {}, {}
+        slot_w, slot_s, wet_c, z_win, dx_last = {}, {}, {}, {}, {}
+        out_sb = [held.tile([P, T], F32, name="out_sb%d" % c, align_bytes=64) for c in range(W // P)]
 
         def place(shape, dtype, name, after=None):
             return held.tile(shape, dtype, name=name, tag=after or name, align_bytes=64)
@@ -57,15 +53,20 @@ def tile_moe_hib_silu_kernel(
         def cols(first, count):
             return slice(first // LIST, (first + count) // LIST)
 
-        def load_wet(e, parts):
-            if e % 2 and e > 1:
-                raw[e] = place([P, PACK, W], F32, "raw%d" % e)
-            else:
-                raw[e] = ring2.tile([P, PACK, W], F32, name="raw", align_bytes=64)
+        def load_wet(e):
             rows = wet[e].rearrange("(p j) i -> p j i", j=PACK)
-            for h in range(parts):
-                part = slice(h * W // parts, (h + 1) * W // parts)
-                nc.sync.dma_start(out=raw[e][:, :, part], in_=rows[:, :, part])
+            if e < 2:
+                for h in range(2):
+                    raw[e, h] = place([P, PACK, W // 2], F32, "raw%d_%d" % (e, h))
+                    nc.sync.dma_start(out=raw[e, h][:], in_=rows[:, :, h * W // 2 : (h + 1) * W // 2])
+                return
+            if e % 2:
+                whole = place([P, PACK, W], F32, "raw%d" % e)
+            else:
+                whole = ring2.tile([P, PACK, W], F32, name="raw", align_bytes=64)
+            nc.sync.dma_start(out=whole[:], in_=rows)
+            for h in range(2):
+                raw[e, h] = whole[:, :, h * W // 2 : (h + 1) * W // 2]
 
         def load_group(f):
             a_sb[f] = ring2.tile([P, PACK, C1], F32, name="a_sb", align_bytes=64)
@@ -77,12 +78,9 @@ def tile_moe_hib_silu_kernel(
 
         def round_wet(e, h, on_vector=False):
             if h == 0:
-                if e % 2 and e > 1:
-                    grouped[e] = place([P, PACK, P, PACK], BF16, "grouped%d" % e)
-                else:
-                    grouped[e] = ring2.tile([P, PACK, P, PACK], BF16, name="grouped", align_bytes=64)
+                grouped[e] = place([P, PACK, P, PACK], BF16, "grouped%d" % e)
             ms = slice(h * P // 2, (h + 1) * P // 2)
-            src = raw[e][:].rearrange("p j (m t) -> p m t j", t=PACK)[:, ms]
+            src = raw[e, h][:].rearrange("p j (m t) -> p m t j", t=PACK)
             to = grouped[e][:].rearrange("p t m j -> p m t j")[:, ms]
             if on_vector:
                 nc.vector.tensor_copy(out=to, in_=src)
@@ -90,20 +88,25 @@ def tile_moe_hib_silu_kernel(
                 nc.scalar.copy(out=to, in_=src)
 
         def quantize_wet(e):
+            wet_c[e] = place([P, W], U32, "wet_c%d" % e, "raw%d" % (e + 1) if e % 2 == 0 and e else None)
             nc.vector.quantize_mx(
                 out=wet_c[e][:].bitcast(FP8X4), scales=wet_s[e][:], in_=grouped[e][:].rearrange("p t m j -> p (t m j)")
             )
 
-        def gather(f):
-            slot_w[f] = place([P, C1], U32, "slot_w%d" % f, "da_bf0" if f == G - 1 else None)
-            slot_s[f] = place([P, C1], U8, "slot_s%d" % f, "half0" if f == G - 1 else None)
+        def gather_words(f, after=None):
+            slot_w[f] = place([P, C1], U32, "slot_w%d" % f, after)
             nc.vector.tensor_copy(slot_w[f][:], dy_w[:].bitcast(U32).indirect(dst_sb[:, cols(f * C1, C1)]))
-            nc.vector.tensor_copy(slot_s[f][:], dy_s[:].bitcast(U8).indirect(dst_sb[:, cols(f * C1, C1)]))
+
+        def gather_scales(f, groups, after=None):
+            picked = place([P, groups * C1], U8, "slot_s%d" % f, after)
+            nc.vector.tensor_copy(picked[:], dy_s[:].bitcast(U8).indirect(dst_sb[:, cols(f * C1, groups * C1)]))
+            for n in range(groups):
+                slot_s[f + n] = picked[:, n * C1 : (n + 1) * C1]
 
         def expert_product(e):
             f, u = divmod(e, 2)
             if u == 0:
-                z_sb[f] = place([P, PACK, C1], F32, "z_sb%d" % f, "raw%d" % (e + 1) if f else None)
+                z_sb[f] = place([P, PACK, C1], F32, "z_sb%d" % f, "raw%d" % (e + 1) if f else "raw1_0")
             bank = psum.tile([P, PACK, C2], F32, name="z_bank")
             slots = slice(u * C2, (u + 1) * C2)
             for t in range(PACK):
@@ -120,35 +123,46 @@ def tile_moe_hib_silu_kernel(
 
         def scatter_z(f, first, count):
             part = slice(first, first + count)
+            after = {(0, 2): "raw1_1", (0, 3): "grouped1", (1, 1): "grouped5", (2, 1): "grouped7"}
             for t in range(PACK):
+                if first == 0:
+                    after_tile = "da_bf%d" % (f - 1) if f and t == 0 else after.get((f, t))
+                    z_win[f, t] = place([P, max(2, f + 1) * C1], F32, "z_win%d_%d" % (f, t), after_tile)
                 nc.vector.tensor_tensor(
-                    z_win[f][t][:].indirect(offs2_sb[:, cols(f * C1 + first, count)]),
+                    z_win[f, t][:].indirect(offs2_sb[:, cols(f * C1 + first, count)]),
                     z_sb[f][:, t, part],
                     gate_sb[f][:, part],
                     ALU.mult,
                 )
 
         def activations(f):
-            if f == G - 1:
-                tanh_sb[f] = place([P, PACK, C1], F32, "tanh_last")
-            else:
-                tanh_sb[f] = ring2.tile([P, PACK, C1], F32, name="tanh_sb", align_bytes=64)
-            silu_sb[f] = ring2.tile([P, C1, PACK], F32, name="silu_sb", align_bytes=64)
-            nc.scalar.activation(out=silu_sb[f][:], in_=a_sb[f][:].rearrange("q t j -> q j t"), func=ACT.Silu, scale=-1.0, bias=no_bias[:])
+            tanh_sb[f] = ring2.tile([P, PACK, C1], F32, name="tanh_sb", align_bytes=64, bufs=3)
+            silu_sb[f] = ring2.tile([P, C1, PACK], F32, name="silu_sb", align_bytes=64, bufs=3)
+            nc.scalar.activation(
+                out=silu_sb[f][:], in_=a_sb[f][:].rearrange("q t j -> q j t"), func=ACT.Silu, scale=-1.0, bias=no_bias[:]
+            )
             nc.scalar.activation(out=tanh_sb[f][:], in_=a_sb[f][:], func=ACT.Tanh, scale=0.5, bias=no_bias[:])
 
+        def shift(f):
+            nc.scalar.activation(out=tanh_sb[f][:], in_=tanh_sb[f][:], func=ACT.Copy, bias=1.0)
+            nc.scalar.activation(out=silu_sb[f][:], in_=silu_sb[f][:], func=ACT.Copy, bias=-1.0)
+
         def times_sigmoid(f):
-            half_sb[f] = place([P, PACK, C1], F32, "half%d" % f, {1: "grouped5", 2: "grouped7", 3: "z_sb0"}.get(f))
+            half_sb[f] = place([P, PACK, C1], F32, "half%d" % f, "raw%d" % (2 * f + 1) if f else None)
             for t in range(PACK):
-                nc.vector.scalar_tensor_tensor(
-                    half_sb[f][:, t, :], tanh_sb[f][:, t, :], 1.0, z_win[f][t][:, f * C1 : (f + 1) * C1], ALU.add, ALU.mult
-                )
+                window = z_win[f, t][:, f * C1 : (f + 1) * C1]
+                if f:
+                    nc.gpsimd.tensor_tensor(half_sb[f][:, t, :], tanh_sb[f][:, t, :], window, ALU.mult)
+                else:
+                    nc.vector.scalar_tensor_tensor(half_sb[f][:, t, :], tanh_sb[f][:, t, :], 1.0, window, ALU.add, ALU.mult)
 
         def finish_da(f):
             da_bf[f] = place([P, C1, PACK], BF16, "da_bf%d" % f)
-            nc.vector.scalar_tensor_tensor(
-                da_bf[f][:], silu_sb[f][:], 1.0, half_sb[f][:].rearrange("q t j -> q j t"), ALU.subtract, ALU.mult
-            )
+            turned = half_sb[f][:].rearrange("q t j -> q j t")
+            if f:
+                nc.gpsimd.tensor_tensor(da_bf[f][:], silu_sb[f][:], turned, ALU.mult)
+            else:
+                nc.vector.scalar_tensor_tensor(da_bf[f][:], silu_sb[f][:], 1.0, turned, ALU.subtract, ALU.mult)
 
         def quantize_da(f):
             da_c[f] = ring2.tile([P, C1], U32, name="da_c", align_bytes=64)
@@ -158,10 +172,7 @@ def tile_moe_hib_silu_kernel(
             )
 
         def group_product(f):
-            if f == G - 2:
-                dx_sb[f] = place([P, W // P, C1], F32, "dx_sb%d" % f, "tanh_last")
-            else:
-                dx_sb[f] = ring2.tile([P, W // P, C1], F32, name="dx_sb", align_bytes=64)
+            dx_sb[f] = place([P, W // P, C1], F32, "dx_sb%d" % f, "grouped%d" % (2 * f + 4) if f < G - 2 else None)
             for b in range(2):
                 bank = psum.tile([P, 2, C1], F32, name="dx_bank", bufs=4)
                 for s in range(2):
@@ -175,12 +186,19 @@ def tile_moe_hib_silu_kernel(
                         start=True,
                         stop=True,
                     )
-                nc.scalar.copy(out=dx_sb[f][:, 2 * b : 2 * b + 2, :], in_=bank[:])
+                if f == G - 2 and b == 1:
+                    nc.scalar.copy(out=dx_sb[f][:, 2, :], in_=bank[:, 0, :])
+                    dx_last[f] = bank
+                else:
+                    nc.scalar.copy(out=dx_sb[f][:, 2 * b : 2 * b + 2, :], in_=bank[:])
 
         def scatter_dx(f, c):
-            if f == 0:
-                out_sb[c] = place([P, T], F32, "out_sb%d" % c, "grouped3" if c == W // P - 1 else None)
-            nc.vector.tensor_copy(out_sb[c][:].indirect(offs_sb[:, cols(f * C1, C1)]), dx_sb[f][:, c, :])
+            values = dx_sb[f][:, c, :]
+            if f == G - 2 and c == 3:
+                held_back = place([P, C1], F32, "held_back", "da_bf%d" % (G - 1))
+                nc.scalar.copy(out=held_back[:], in_=dx_last[f][:, 1, :])
+                values = held_back[:]
+            nc.vector.tensor_copy(out_sb[c][:].indirect(offs_sb[:, cols(f * C1, C1)]), values)
             if f == G - 1:
                 nc.sync.dma_start(out=out[c * P : (c + 1) * P, :], in_=out_sb[c][:])
 
@@ -189,7 +207,7 @@ def tile_moe_hib_silu_kernel(
         nc.sync.dma_start(dst_sb[:], dst)
         for q in range(4):
             nc.sync.dma_start(out=dy_s[32 * q : 32 * q + 4, :], in_=dy_scales[0, 4 * q : 4 * q + 4, :].bitcast(I32))
-        load_wet(0, 2)
+        load_wet(0)
         nc.sync.dma_start(out=dy_w[:], in_=dy_words[0].rearrange("p t d -> p (t d)").bitcast(I32))
         for q in range(4):
             nc.gpsimd.dma_start(
@@ -197,7 +215,7 @@ def tile_moe_hib_silu_kernel(
             )
         nc.sync.dma_start(offs2_sb[:], offs2)
         load_gate(0)
-        load_wet(1, 1)
+        load_wet(1)
         load_group(0)
         nc.sync.dma_start(offs_sb[:], offs)
 
@@ -207,54 +225,60 @@ def tile_moe_hib_silu_kernel(
         round_wet(0, 0)
         round_wet(0, 1, on_vector=True)
         quantize_wet(0)
-        gather(0)
-        expert_product(0)
+        gather_words(0)
+        gather_scales(0, 1)
         round_wet(1, 0)
+        expert_product(0)
         round_wet(1, 1)
-        gather(1)
         quantize_wet(1)
         scatter_z(0, 0, C2)
         expert_product(1)
-        activations(0)
-        gather(2)
+        gather_words(1)
+        gather_scales(1, 1)
+        gather_words(2)
         scatter_z(0, C2, C2)
+        activations(0)
 
-        for f in range(G):
-            pair = (2 * f + 2, 2 * f + 3) if f + 1 < G else ()
-            for e in pair:
-                load_wet(e, 1)
-            if pair:
-                load_gate(f + 1)
-                load_group(f + 1)
-            for e in pair:
+        def loads(f):
+            load_wet(2 * f)
+            load_wet(2 * f + 1)
+            load_gate(f)
+            load_group(f)
+            for e in (2 * f, 2 * f + 1):
                 round_wet(e, 0)
                 round_wet(e, 1)
-            if f > 0:
-                for e in pair:
-                    quantize_wet(e)
-                    expert_product(e)
+
+        loads(1)
+        times_sigmoid(0)
+        finish_da(0)
+        quantize_da(0)
+        quantize_wet(2)
+        quantize_wet(3)
+        expert_product(2)
+        expert_product(3)
+        gather_scales(2, 2, "grouped2")
+        gather_words(3, "grouped3")
+        for f in range(1, G):
+            if f + 1 < G:
+                loads(f + 1)
+                quantize_wet(2 * f + 2)
+                quantize_wet(2 * f + 3)
+            activations(f)
+            if f > 1:
+                shift(f)
+            group_product(f - 1)
+            if f == 1:
+                shift(f)
+            if f + 1 < G:
+                expert_product(2 * f + 2)
+                expert_product(2 * f + 3)
+            scatter_z(f, 0, C1)
             times_sigmoid(f)
             finish_da(f)
+            for c in range(W // P - (f == G - 1)):
+                scatter_dx(f - 1, c)
             quantize_da(f)
-            if f == 0:
-                gather(G - 1)
-                for e in pair:
-                    quantize_wet(e)
-                    expert_product(e)
-            if pair:
-                activations(f + 1)
-            if f == G - 1:
-                group_product(f - 1)
-            if f != G - 2:
-                group_product(f)
-            if f == 0:
-                for c in range(W // P):
-                    scatter_dx(0, c)
-            if pair:
-                scatter_z(f + 1, 0, C1)
-            if f == 1:
-                for c in range(W // P):
-                    scatter_dx(1, c)
-        for f in (G - 2, G - 1):
-            for c in range(W // P):
-                scatter_dx(f, c)
+        scatter_dx(G - 2, W // P - 1)
+        group_product(G - 1)
+        for c in range(W // P):
+            scatter_dx(G - 1, c)

@@ -44,7 +44,7 @@ def tile_moe_hib_silu_kernel(
         wet_s = [held.tile([P, W], U8, name="wet_s%d" % e, align_bytes=64) for e in range(E)]
 
         raw, grouped, a_sb, tanh_sb, silu_sb, z_sb, half_sb, da_bf, da_c, da_s, dx_sb = ({} for n in range(11))
-        slot_w, slot_s, wet_c, z_win, dx_last = {}, {}, {}, {}, {}
+        slot_w, slot_s, wet_c, z_win, planes, dx_bank = {}, {}, {}, {}, {}, {}
         out_sb = [held.tile([P, T], F32, name="out_sb%d" % c, align_bytes=64) for c in range(W // P)]
 
         def place(shape, dtype, name, after=None):
@@ -55,15 +55,15 @@ def tile_moe_hib_silu_kernel(
 
         def load_wet(e):
             rows = wet[e].rearrange("(p j) i -> p j i", j=PACK)
-            if e < 2:
+            if e in (0, 1, 3, 5):
                 for h in range(2):
                     raw[e, h] = place([P, PACK, W // 2], F32, "raw%d_%d" % (e, h))
                     nc.sync.dma_start(out=raw[e, h][:], in_=rows[:, :, h * W // 2 : (h + 1) * W // 2])
                 return
-            if e % 2:
+            if e % 2 or e == 2:
                 whole = place([P, PACK, W], F32, "raw%d" % e)
             else:
-                whole = ring2.tile([P, PACK, W], F32, name="raw", align_bytes=64)
+                whole = place([P, PACK, W], F32, "raw%d" % e, "raw4")
             nc.sync.dma_start(out=whole[:], in_=rows)
             for h in range(2):
                 raw[e, h] = whole[:, :, h * W // 2 : (h + 1) * W // 2]
@@ -71,6 +71,8 @@ def tile_moe_hib_silu_kernel(
         def load_group(f):
             a_sb[f] = ring2.tile([P, PACK, C1], F32, name="a_sb", align_bytes=64)
             nc.sync.dma_start(out=a_sb[f][:], in_=a.rearrange("(q t) j -> q t j", t=PACK)[:, :, f * C1 : (f + 1) * C1])
+
+        def load_wgt(f):
             nc.sync.dma_start(out=wgt_w[f][:], in_=wgt_words[f, 0].rearrange("p k d -> p (k d)").bitcast(I32))
 
         def load_gate(f):
@@ -88,7 +90,7 @@ def tile_moe_hib_silu_kernel(
                 nc.scalar.copy(out=to, in_=src)
 
         def quantize_wet(e):
-            wet_c[e] = place([P, W], U32, "wet_c%d" % e, "raw%d" % (e + 1) if e % 2 == 0 and e else None)
+            wet_c[e] = place([P, W], U32, "wet_c%d" % e, {4: "raw5_0", 6: "raw7"}.get(e))
             nc.vector.quantize_mx(
                 out=wet_c[e][:].bitcast(FP8X4), scales=wet_s[e][:], in_=grouped[e][:].rearrange("p t m j -> p (t m j)")
             )
@@ -106,7 +108,7 @@ def tile_moe_hib_silu_kernel(
         def expert_product(e):
             f, u = divmod(e, 2)
             if u == 0:
-                z_sb[f] = place([P, PACK, C1], F32, "z_sb%d" % f, "raw%d" % (e + 1) if f else "raw1_0")
+                z_sb[f] = place([P, PACK, C1], F32, "z_sb%d" % f, ("raw1_0", "raw3_0", "raw5_0", "raw7")[f])
             bank = psum.tile([P, PACK, C2], F32, name="z_bank")
             slots = slice(u * C2, (u + 1) * C2)
             for t in range(PACK):
@@ -123,11 +125,10 @@ def tile_moe_hib_silu_kernel(
 
         def scatter_z(f, first, count):
             part = slice(first, first + count)
-            after = {(0, 2): "raw1_1", (0, 3): "grouped1", (1, 1): "grouped5", (2, 1): "grouped7"}
+            after = {(0, 2): "raw1_1", (0, 3): "grouped1", (1, 2): "raw3_1", (1, 3): "grouped3"}
             for t in range(PACK):
                 if first == 0:
-                    after_tile = "da_bf%d" % (f - 1) if f and t == 0 else after.get((f, t))
-                    z_win[f, t] = place([P, max(2, f + 1) * C1], F32, "z_win%d_%d" % (f, t), after_tile)
+                    z_win[f, t] = place([P, max(2, f + 1) * C1], F32, "z_win%d_%d" % (f, t), after.get((f, t)))
                 nc.vector.tensor_tensor(
                     z_win[f, t][:].indirect(offs2_sb[:, cols(f * C1 + first, count)]),
                     z_sb[f][:, t, part],
@@ -136,33 +137,27 @@ def tile_moe_hib_silu_kernel(
                 )
 
         def activations(f):
-            tanh_sb[f] = ring2.tile([P, PACK, C1], F32, name="tanh_sb", align_bytes=64, bufs=3)
-            silu_sb[f] = ring2.tile([P, C1, PACK], F32, name="silu_sb", align_bytes=64, bufs=3)
-            nc.scalar.activation(
-                out=silu_sb[f][:], in_=a_sb[f][:].rearrange("q t j -> q j t"), func=ACT.Silu, scale=-1.0, bias=no_bias[:]
-            )
+            tanh_sb[f] = place([P, PACK, C1], F32, "tanh%d" % f)
+            silu_sb[f] = ring2.tile([P, PACK, C1], F32, name="silu_sb", align_bytes=64)
             nc.scalar.activation(out=tanh_sb[f][:], in_=a_sb[f][:], func=ACT.Tanh, scale=0.5, bias=no_bias[:])
-
-        def shift(f):
-            nc.scalar.activation(out=tanh_sb[f][:], in_=tanh_sb[f][:], func=ACT.Copy, bias=1.0)
-            nc.scalar.activation(out=silu_sb[f][:], in_=silu_sb[f][:], func=ACT.Copy, bias=-1.0)
+            nc.scalar.activation(out=silu_sb[f][:], in_=a_sb[f][:], func=ACT.Silu, scale=-1.0, bias=no_bias[:])
 
         def times_sigmoid(f):
-            half_sb[f] = place([P, PACK, C1], F32, "half%d" % f, "raw%d" % (2 * f + 1) if f else None)
+            half_sb[f] = place([P, PACK, C1], F32, "half%d" % f, ("raw2", "grouped0", "grouped6", "grouped2")[f])
             for t in range(PACK):
                 window = z_win[f, t][:, f * C1 : (f + 1) * C1]
-                if f:
-                    nc.gpsimd.tensor_tensor(half_sb[f][:, t, :], tanh_sb[f][:, t, :], window, ALU.mult)
-                else:
-                    nc.vector.scalar_tensor_tensor(half_sb[f][:, t, :], tanh_sb[f][:, t, :], 1.0, window, ALU.add, ALU.mult)
+                nc.vector.scalar_tensor_tensor(half_sb[f][:, t, :], tanh_sb[f][:, t, :], 1.0, window, ALU.add, ALU.mult)
 
         def finish_da(f):
-            da_bf[f] = place([P, C1, PACK], BF16, "da_bf%d" % f)
-            turned = half_sb[f][:].rearrange("q t j -> q j t")
-            if f:
-                nc.gpsimd.tensor_tensor(da_bf[f][:], silu_sb[f][:], turned, ALU.mult)
-            else:
-                nc.vector.scalar_tensor_tensor(da_bf[f][:], silu_sb[f][:], 1.0, turned, ALU.subtract, ALU.mult)
+            planes[f] = place([P, PACK, C1], BF16, "planes%d" % f)
+            for ts in (slice(0, 2), slice(2, 4)):
+                nc.vector.scalar_tensor_tensor(
+                    planes[f][:, ts, :], silu_sb[f][:, ts, :], 1.0, half_sb[f][:, ts, :], ALU.subtract, ALU.mult
+                )
+
+        def interleave_da(f):
+            da_bf[f] = place([P, C1, PACK], BF16, "da_bf%d" % f, (None, "raw5_1", "grouped1", "grouped3")[f])
+            nc.scalar.copy(out=da_bf[f][:], in_=planes[f][:].rearrange("q t j -> q j t"))
 
         def quantize_da(f):
             da_c[f] = ring2.tile([P, C1], U32, name="da_c", align_bytes=64)
@@ -172,7 +167,6 @@ def tile_moe_hib_silu_kernel(
             )
 
         def group_product(f):
-            dx_sb[f] = place([P, W // P, C1], F32, "dx_sb%d" % f, "grouped%d" % (2 * f + 4) if f < G - 2 else None)
             for b in range(2):
                 bank = psum.tile([P, 2, C1], F32, name="dx_bank", bufs=4)
                 for s in range(2):
@@ -186,41 +180,42 @@ def tile_moe_hib_silu_kernel(
                         start=True,
                         stop=True,
                     )
-                if f == G - 2 and b == 1:
-                    nc.scalar.copy(out=dx_sb[f][:, 2, :], in_=bank[:, 0, :])
-                    dx_last[f] = bank
-                else:
-                    nc.scalar.copy(out=dx_sb[f][:, 2 * b : 2 * b + 2, :], in_=bank[:])
+                dx_bank[f, b] = bank
+
+        def fetch_dx(f, first, count, after=None):
+            rows = place([P, count, C1], F32, "dx%d_%d" % (f, first), after)
+            for b in range(2):
+                low, high = max(first, 2 * b), min(first + count, 2 * b + 2)
+                if low < high:
+                    nc.scalar.copy(out=rows[:, low - first : high - first, :], in_=dx_bank[f, b][:, low - 2 * b : high - 2 * b, :])
+            for c in range(first, first + count):
+                dx_sb[f, c] = rows[:, c - first, :]
 
         def scatter_dx(f, c):
-            values = dx_sb[f][:, c, :]
-            if f == G - 2 and c == 3:
-                held_back = place([P, C1], F32, "held_back", "da_bf%d" % (G - 1))
-                nc.scalar.copy(out=held_back[:], in_=dx_last[f][:, 1, :])
-                values = held_back[:]
-            nc.vector.tensor_copy(out_sb[c][:].indirect(offs_sb[:, cols(f * C1, C1)]), values)
+            nc.vector.tensor_copy(out_sb[c][:].indirect(offs_sb[:, cols(f * C1, C1)]), dx_sb[f, c])
             if f == G - 1:
                 nc.sync.dma_start(out=out[c * P : (c + 1) * P, :], in_=out_sb[c][:])
 
-        nc.vector.memset(dy_s[:], 0)
         nc.gpsimd.memset(wgt_s[:].bitcast(I32), 0)
         nc.sync.dma_start(dst_sb[:], dst)
         for q in range(4):
-            nc.sync.dma_start(out=dy_s[32 * q : 32 * q + 4, :], in_=dy_scales[0, 4 * q : 4 * q + 4, :].bitcast(I32))
+            rows = dy_scales[0, 4 * q : 4 * q + 4, :].bitcast(I32)
+            nc.sync.dma_start(out=dy_s[32 * q : 32 * q + 32, :], in_=rows.partition_broadcast(8))
         load_wet(0)
         nc.sync.dma_start(out=dy_w[:], in_=dy_words[0].rearrange("p t d -> p (t d)").bitcast(I32))
-        for q in range(4):
-            nc.gpsimd.dma_start(
-                out=wgt_s[32 * q : 32 * q + 16, :].bitcast(I32), in_=wgt_scales[:, 0, 4 * q : 4 * q + 4, :].bitcast(I32)
-            )
         nc.sync.dma_start(offs2_sb[:], offs2)
-        load_gate(0)
         load_wet(1)
+        load_gate(0)
         load_group(0)
-        nc.sync.dma_start(offs_sb[:], offs)
 
         nc.vector.memset(zero[:], 0.0)
         nc.scalar.activation(out=no_bias[:], in_=zero[:], func=ACT.Silu)
+
+        def loads(f):
+            load_wet(2 * f)
+            load_wet(2 * f + 1)
+            load_gate(f)
+            load_group(f)
 
         round_wet(0, 0)
         round_wet(0, 1, on_vector=True)
@@ -236,49 +231,59 @@ def tile_moe_hib_silu_kernel(
         gather_words(1)
         gather_scales(1, 1)
         gather_words(2)
+        gather_scales(2, 1)
+        gather_words(3)
+        gather_scales(3, 1)
         scatter_z(0, C2, C2)
         activations(0)
-
-        def loads(f):
-            load_wet(2 * f)
-            load_wet(2 * f + 1)
-            load_gate(f)
-            load_group(f)
-            for e in (2 * f, 2 * f + 1):
-                round_wet(e, 0)
-                round_wet(e, 1)
-
         loads(1)
+        for q in range(4):
+            nc.sync.dma_start(
+                out=wgt_s[32 * q : 32 * q + 16, :].bitcast(I32), in_=wgt_scales[:, 0, 4 * q : 4 * q + 4, :].bitcast(I32)
+            )
+        load_wgt(0)
+        nc.sync.dma_start(offs_sb[:], offs)
+        round_wet(2, 0)
+        round_wet(2, 1)
+        quantize_wet(2)
+        expert_product(2)
         times_sigmoid(0)
         finish_da(0)
+        interleave_da(0)
         quantize_da(0)
-        quantize_wet(2)
+        round_wet(3, 0)
+        round_wet(3, 1)
         quantize_wet(3)
-        expert_product(2)
+        scatter_z(1, 0, C2)
         expert_product(3)
-        gather_scales(2, 2, "grouped2")
-        gather_words(3, "grouped3")
+        scatter_z(1, C2, C2)
         for f in range(1, G):
-            if f + 1 < G:
-                loads(f + 1)
-                quantize_wet(2 * f + 2)
-                quantize_wet(2 * f + 3)
+            pair = (2 * f + 2, 2 * f + 3) if f + 1 < G else ()
             activations(f)
-            if f > 1:
-                shift(f)
-            group_product(f - 1)
-            if f == 1:
-                shift(f)
-            if f + 1 < G:
-                expert_product(2 * f + 2)
-                expert_product(2 * f + 3)
-            scatter_z(f, 0, C1)
+            if pair:
+                loads(f + 1)
+            load_wgt(f)
+            for e in pair:
+                round_wet(e, 0)
+                round_wet(e, 1)
+            for e in pair:
+                quantize_wet(e)
             times_sigmoid(f)
             finish_da(f)
-            for c in range(W // P - (f == G - 1)):
-                scatter_dx(f - 1, c)
+            group_product(f - 1)
+            early = 2 if pair else 1
+            fetch_dx(f - 1, 0, early, "tanh%d" % f)
+            interleave_da(f)
             quantize_da(f)
-        scatter_dx(G - 2, W // P - 1)
+            fetch_dx(f - 1, early, W // P - early, "grouped4" if f == 1 else "planes%d" % f)
+            for e in pair:
+                expert_product(e)
+            for c in range(W // P):
+                scatter_dx(f - 1, c)
+            if pair:
+                scatter_z(f + 1, 0, C1)
         group_product(G - 1)
+        fetch_dx(G - 1, 0, 2)
+        fetch_dx(G - 1, 2, 2)
         for c in range(W // P):
             scatter_dx(G - 1, c)

@@ -18,8 +18,40 @@ T = 1024
 G, C1 = 4, 256
 E, C2 = 8, 128
 W = 512
+ROW_TILES = W // P
 LIST = 16
+QUADRANTS, QUADRANT = 4, 32
+SCALE_ROWS = 4
+MIN_WINDOW = 2 * C1
+HALVED = (0, 1, 3, 5)
 FLOPS = 2 * 2 * W * W * T
+
+TAKES_PLACE_OF = {
+    "z_sb0": "raw1_0",
+    "z_sb1": "raw3_0",
+    "z_sb2": "raw5_0",
+    "z_sb3": "raw7",
+    "wet_c4": "raw5_0",
+    "wet_c6": "raw7",
+    "z_win0_2": "raw1_1",
+    "z_win0_3": "grouped1",
+    "z_win1_2": "raw3_1",
+    "z_win1_3": "grouped3",
+    "half0": "raw2",
+    "half2": "grouped6",
+    "da_bf1": "raw5_1",
+    "dx0_0": "tanh1",
+    "dx1_0": "tanh2",
+    "dx2_0": "tanh3",
+    "dx0_2": "grouped4",
+    "dx1_2": "planes2",
+    "dx2_1": "planes3",
+    "raw6": "raw4",
+    "half1": "grouped0",
+    "half3": "grouped2",
+    "da_bf2": "grouped1",
+    "da_bf3": "grouped3",
+}
 
 
 def tile_moe_hib_silu_kernel(
@@ -42,73 +74,72 @@ def tile_moe_hib_silu_kernel(
         wgt_w = [held.tile([P, W], I32, name="wgt_w%d" % f, align_bytes=64) for f in range(G)]
         gate_sb = [held.tile([P, C1], F32, name="gate%d" % f, align_bytes=64) for f in range(G)]
         wet_s = [held.tile([P, W], U8, name="wet_s%d" % e, align_bytes=64) for e in range(E)]
+        out_sb = [held.tile([P, T], F32, name="out_sb%d" % c, align_bytes=64) for c in range(ROW_TILES)]
 
-        raw, grouped, a_sb, tanh_sb, silu_sb, z_sb, half_sb, da_bf, da_c, da_s, dx_sb = ({} for n in range(11))
-        slot_w, slot_s, wet_c, z_win, planes, dx_bank = {}, {}, {}, {}, {}, {}
-        out_sb = [held.tile([P, T], F32, name="out_sb%d" % c, align_bytes=64) for c in range(W // P)]
+        raw, grouped, wet_c, slot_w, slot_s, z_sb, z_win = {}, {}, {}, {}, {}, {}, {}
+        a_sb, tanh_sb, silu_sb, half_sb, planes, da_bf, da_c, da_s = {}, {}, {}, {}, {}, {}, {}, {}
+        dx_bank, dx_sb = {}, {}
 
-        def place(shape, dtype, name, after=None):
-            return held.tile(shape, dtype, name=name, tag=after or name, align_bytes=64)
+        def place(shape, dtype, name):
+            return held.tile(shape, dtype, name=name, tag=TAKES_PLACE_OF.get(name, name), align_bytes=64)
 
-        def cols(first, count):
+        def entries(first, count):
             return slice(first // LIST, (first + count) // LIST)
 
         def load_wet(e):
             rows = wet[e].rearrange("(p j) i -> p j i", j=PACK)
-            if e in (0, 1, 3, 5):
+            halves = [slice(h * W // 2, (h + 1) * W // 2) for h in range(2)]
+            if e in HALVED:
                 for h in range(2):
                     raw[e, h] = place([P, PACK, W // 2], F32, "raw%d_%d" % (e, h))
-                    nc.sync.dma_start(out=raw[e, h][:], in_=rows[:, :, h * W // 2 : (h + 1) * W // 2])
-                return
-            if e % 2 or e == 2:
-                whole = place([P, PACK, W], F32, "raw%d" % e)
+                    nc.sync.dma_start(out=raw[e, h][:], in_=rows[:, :, halves[h]])
             else:
-                whole = place([P, PACK, W], F32, "raw%d" % e, "raw4")
-            nc.sync.dma_start(out=whole[:], in_=rows)
-            for h in range(2):
-                raw[e, h] = whole[:, :, h * W // 2 : (h + 1) * W // 2]
+                whole = place([P, PACK, W], F32, "raw%d" % e)
+                nc.sync.dma_start(out=whole[:], in_=rows)
+                for h in range(2):
+                    raw[e, h] = whole[:, :, halves[h]]
+
+        def load_gate_and_a(f):
+            slots = slice(f * C1, (f + 1) * C1)
+            nc.sync.dma_start(out=gate_sb[f][:], in_=gate[:, slots])
+            a_sb[f] = ring2.tile([P, PACK, C1], F32, name="a_sb", align_bytes=64)
+            nc.sync.dma_start(out=a_sb[f][:], in_=a.rearrange("(q t) j -> q t j", t=PACK)[:, :, slots])
 
         def load_group(f):
-            a_sb[f] = ring2.tile([P, PACK, C1], F32, name="a_sb", align_bytes=64)
-            nc.sync.dma_start(out=a_sb[f][:], in_=a.rearrange("(q t) j -> q t j", t=PACK)[:, :, f * C1 : (f + 1) * C1])
+            load_wet(2 * f)
+            load_wet(2 * f + 1)
+            load_gate_and_a(f)
 
-        def load_wgt(f):
+        def load_wgt_words(f):
             nc.sync.dma_start(out=wgt_w[f][:], in_=wgt_words[f, 0].rearrange("p k d -> p (k d)").bitcast(I32))
-
-        def load_gate(f):
-            nc.sync.dma_start(out=gate_sb[f][:], in_=gate[:, f * C1 : (f + 1) * C1])
 
         def round_wet(e, h, on_vector=False):
             if h == 0:
                 grouped[e] = place([P, PACK, P, PACK], BF16, "grouped%d" % e)
-            ms = slice(h * P // 2, (h + 1) * P // 2)
-            src = raw[e, h][:].rearrange("p j (m t) -> p m t j", t=PACK)
-            to = grouped[e][:].rearrange("p t m j -> p m t j")[:, ms]
+            src = raw[e, h][:].rearrange("p j (m t) -> p m j t", t=PACK)
+            to = grouped[e][:].rearrange("p t m j -> p m j t")[:, h * P // 2 : (h + 1) * P // 2]
             if on_vector:
                 nc.vector.tensor_copy(out=to, in_=src)
             else:
                 nc.scalar.copy(out=to, in_=src)
 
         def quantize_wet(e):
-            wet_c[e] = place([P, W], U32, "wet_c%d" % e, {4: "raw5_0", 6: "raw7"}.get(e))
+            wet_c[e] = place([P, W], U32, "wet_c%d" % e)
             nc.vector.quantize_mx(
                 out=wet_c[e][:].bitcast(FP8X4), scales=wet_s[e][:], in_=grouped[e][:].rearrange("p t m j -> p (t m j)")
             )
 
-        def gather_words(f, after=None):
-            slot_w[f] = place([P, C1], U32, "slot_w%d" % f, after)
-            nc.vector.tensor_copy(slot_w[f][:], dy_w[:].bitcast(U32).indirect(dst_sb[:, cols(f * C1, C1)]))
-
-        def gather_scales(f, groups, after=None):
-            picked = place([P, groups * C1], U8, "slot_s%d" % f, after)
-            nc.vector.tensor_copy(picked[:], dy_s[:].bitcast(U8).indirect(dst_sb[:, cols(f * C1, groups * C1)]))
-            for n in range(groups):
-                slot_s[f + n] = picked[:, n * C1 : (n + 1) * C1]
+        def gather_dy(f):
+            picks = dst_sb[:, entries(f * C1, C1)]
+            slot_w[f] = place([P, C1], U32, "slot_w%d" % f)
+            nc.vector.tensor_copy(slot_w[f][:], dy_w[:].bitcast(U32).indirect(picks))
+            slot_s[f] = place([P, C1], U8, "slot_s%d" % f)
+            nc.vector.tensor_copy(slot_s[f][:], dy_s[:].bitcast(U8).indirect(picks))
 
         def expert_product(e):
             f, u = divmod(e, 2)
             if u == 0:
-                z_sb[f] = place([P, PACK, C1], F32, "z_sb%d" % f, ("raw1_0", "raw3_0", "raw5_0", "raw7")[f])
+                z_sb[f] = place([P, PACK, C1], F32, "z_sb%d" % f)
             bank = psum.tile([P, PACK, C2], F32, name="z_bank")
             slots = slice(u * C2, (u + 1) * C2)
             for t in range(PACK):
@@ -121,18 +152,17 @@ def tile_moe_hib_silu_kernel(
                     start=True,
                     stop=True,
                 )
-            nc.scalar.activation(out=z_sb[f][:, :, u * C2 : (u + 1) * C2], in_=bank[:], func=ACT.Copy, scale=-0.5)
+            nc.scalar.activation(out=z_sb[f][:, :, slots], in_=bank[:], func=ACT.Copy, scale=-0.5)
 
         def scatter_z(f, first, count):
-            part = slice(first, first + count)
-            after = {(0, 2): "raw1_1", (0, 3): "grouped1", (1, 2): "raw3_1", (1, 3): "grouped3"}
+            slots = slice(first, first + count)
             for t in range(PACK):
                 if first == 0:
-                    z_win[f, t] = place([P, max(2, f + 1) * C1], F32, "z_win%d_%d" % (f, t), after.get((f, t)))
+                    z_win[f, t] = place([P, max(MIN_WINDOW, (f + 1) * C1)], F32, "z_win%d_%d" % (f, t))
                 nc.vector.tensor_tensor(
-                    z_win[f, t][:].indirect(offs2_sb[:, cols(f * C1 + first, count)]),
-                    z_sb[f][:, t, part],
-                    gate_sb[f][:, part],
+                    z_win[f, t][:].indirect(offs2_sb[:, entries(f * C1 + first, count)]),
+                    z_sb[f][:, t, slots],
+                    gate_sb[f][:, slots],
                     ALU.mult,
                 )
 
@@ -142,24 +172,20 @@ def tile_moe_hib_silu_kernel(
             nc.scalar.activation(out=tanh_sb[f][:], in_=a_sb[f][:], func=ACT.Tanh, scale=0.5, bias=no_bias[:])
             nc.scalar.activation(out=silu_sb[f][:], in_=a_sb[f][:], func=ACT.Silu, scale=-1.0, bias=no_bias[:])
 
-        def times_sigmoid(f):
-            half_sb[f] = place([P, PACK, C1], F32, "half%d" % f, ("raw2", "grouped0", "grouped6", "grouped2")[f])
+        def derivative_products(f):
+            half_sb[f] = place([P, PACK, C1], F32, "half%d" % f)
             for t in range(PACK):
-                window = z_win[f, t][:, f * C1 : (f + 1) * C1]
-                nc.vector.scalar_tensor_tensor(half_sb[f][:, t, :], tanh_sb[f][:, t, :], 1.0, window, ALU.add, ALU.mult)
-
-        def finish_da(f):
+                scattered = z_win[f, t][:, f * C1 : (f + 1) * C1]
+                nc.vector.scalar_tensor_tensor(half_sb[f][:, t, :], tanh_sb[f][:, t, :], 1.0, scattered, ALU.add, ALU.mult)
             planes[f] = place([P, PACK, C1], BF16, "planes%d" % f)
-            for ts in (slice(0, 2), slice(2, 4)):
+            for two in (slice(0, 2), slice(2, 4)):
                 nc.vector.scalar_tensor_tensor(
-                    planes[f][:, ts, :], silu_sb[f][:, ts, :], 1.0, half_sb[f][:, ts, :], ALU.subtract, ALU.mult
+                    planes[f][:, two, :], silu_sb[f][:, two, :], 1.0, half_sb[f][:, two, :], ALU.subtract, ALU.mult
                 )
 
-        def interleave_da(f):
-            da_bf[f] = place([P, C1, PACK], BF16, "da_bf%d" % f, (None, "raw5_1", "grouped1", "grouped3")[f])
-            nc.scalar.copy(out=da_bf[f][:], in_=planes[f][:].rearrange("q t j -> q j t"))
-
         def quantize_da(f):
+            da_bf[f] = place([P, C1, PACK], BF16, "da_bf%d" % f)
+            nc.scalar.copy(out=da_bf[f][:], in_=planes[f][:].rearrange("q t j -> q j t"))
             da_c[f] = ring2.tile([P, C1], U32, name="da_c", align_bytes=64)
             da_s[f] = ring2.tile([P, C1], U8, name="da_s", align_bytes=64)
             nc.vector.quantize_mx(
@@ -168,88 +194,82 @@ def tile_moe_hib_silu_kernel(
 
         def group_product(f):
             for b in range(2):
-                bank = psum.tile([P, 2, C1], F32, name="dx_bank", bufs=4)
+                dx_bank[f, b] = psum.tile([P, 2, C1], F32, name="dx_bank", bufs=4)
                 for s in range(2):
                     ks = slice((2 * b + s) * P, (2 * b + s + 1) * P)
                     nc.tensor.matmul_mx(
-                        out=bank[:, s, :],
+                        out=dx_bank[f, b][:, s, :],
                         lhsT=wgt_w[f][:, ks].bitcast(FP8X4),
-                        lhsT_scale=wgt_s[PACK * f : P, ks],
+                        lhsT_scale=wgt_s[SCALE_ROWS * f : P, ks],
                         rhs=da_c[f][:].bitcast(FP8X4),
                         rhs_scale=da_s[f][:],
                         start=True,
                         stop=True,
                     )
-                dx_bank[f, b] = bank
 
-        def fetch_dx(f, first, count, after=None):
-            rows = place([P, count, C1], F32, "dx%d_%d" % (f, first), after)
+        def fetch_dx(f, first, count):
+            rows = place([P, count, C1], F32, "dx%d_%d" % (f, first))
             for b in range(2):
                 low, high = max(first, 2 * b), min(first + count, 2 * b + 2)
                 if low < high:
-                    nc.scalar.copy(out=rows[:, low - first : high - first, :], in_=dx_bank[f, b][:, low - 2 * b : high - 2 * b, :])
+                    nc.scalar.copy(
+                        out=rows[:, low - first : high - first, :], in_=dx_bank[f, b][:, low - 2 * b : high - 2 * b, :]
+                    )
             for c in range(first, first + count):
                 dx_sb[f, c] = rows[:, c - first, :]
 
-        def scatter_dx(f, c):
-            nc.vector.tensor_copy(out_sb[c][:].indirect(offs_sb[:, cols(f * C1, C1)]), dx_sb[f, c])
-            if f == G - 1:
-                nc.sync.dma_start(out=out[c * P : (c + 1) * P, :], in_=out_sb[c][:])
+        def scatter_dx(f):
+            for c in range(ROW_TILES):
+                nc.vector.tensor_copy(out_sb[c][:].indirect(offs_sb[:, entries(f * C1, C1)]), dx_sb[f, c])
+                if f == G - 1:
+                    nc.sync.dma_start(out=out[c * P : (c + 1) * P, :], in_=out_sb[c][:])
 
         nc.gpsimd.memset(wgt_s[:].bitcast(I32), 0)
+
         nc.sync.dma_start(dst_sb[:], dst)
-        for q in range(4):
-            rows = dy_scales[0, 4 * q : 4 * q + 4, :].bitcast(I32)
-            nc.sync.dma_start(out=dy_s[32 * q : 32 * q + 32, :], in_=rows.partition_broadcast(8))
+        for q in range(QUADRANTS):
+            rows_q = dy_scales[0, SCALE_ROWS * q : SCALE_ROWS * (q + 1), :].bitcast(I32)
+            nc.sync.dma_start(
+                out=dy_s[QUADRANT * q : QUADRANT * (q + 1), :], in_=rows_q.partition_broadcast(QUADRANT // SCALE_ROWS)
+            )
         load_wet(0)
         nc.sync.dma_start(out=dy_w[:], in_=dy_words[0].rearrange("p t d -> p (t d)").bitcast(I32))
         nc.sync.dma_start(offs2_sb[:], offs2)
         load_wet(1)
-        load_gate(0)
-        load_group(0)
+        load_gate_and_a(0)
 
         nc.vector.memset(zero[:], 0.0)
         nc.scalar.activation(out=no_bias[:], in_=zero[:], func=ACT.Silu)
 
-        def loads(f):
-            load_wet(2 * f)
-            load_wet(2 * f + 1)
-            load_gate(f)
-            load_group(f)
-
         round_wet(0, 0)
         round_wet(0, 1, on_vector=True)
         quantize_wet(0)
-        gather_words(0)
-        gather_scales(0, 1)
+        gather_dy(0)
         round_wet(1, 0)
         expert_product(0)
         round_wet(1, 1)
         quantize_wet(1)
         scatter_z(0, 0, C2)
         expert_product(1)
-        gather_words(1)
-        gather_scales(1, 1)
-        gather_words(2)
-        gather_scales(2, 1)
-        gather_words(3)
-        gather_scales(3, 1)
+        for f in range(1, G):
+            gather_dy(f)
         scatter_z(0, C2, C2)
         activations(0)
-        loads(1)
-        for q in range(4):
+
+        load_group(1)
+        for q in range(QUADRANTS):
             nc.sync.dma_start(
-                out=wgt_s[32 * q : 32 * q + 16, :].bitcast(I32), in_=wgt_scales[:, 0, 4 * q : 4 * q + 4, :].bitcast(I32)
+                out=wgt_s[QUADRANT * q : QUADRANT * q + G * SCALE_ROWS, :].bitcast(I32),
+                in_=wgt_scales[:, 0, SCALE_ROWS * q : SCALE_ROWS * (q + 1), :].bitcast(I32),
             )
-        load_wgt(0)
+        load_wgt_words(0)
         nc.sync.dma_start(offs_sb[:], offs)
+
         round_wet(2, 0)
         round_wet(2, 1)
         quantize_wet(2)
         expert_product(2)
-        times_sigmoid(0)
-        finish_da(0)
-        interleave_da(0)
+        derivative_products(0)
         quantize_da(0)
         round_wet(3, 0)
         round_wet(3, 1)
@@ -257,33 +277,30 @@ def tile_moe_hib_silu_kernel(
         scatter_z(1, 0, C2)
         expert_product(3)
         scatter_z(1, C2, C2)
+
         for f in range(1, G):
-            pair = (2 * f + 2, 2 * f + 3) if f + 1 < G else ()
+            next_experts = range(2 * f + 2, min(2 * f + 4, E))
             activations(f)
-            if pair:
-                loads(f + 1)
-            load_wgt(f)
-            for e in pair:
+            if next_experts:
+                load_group(f + 1)
+            load_wgt_words(f)
+            for e in next_experts:
                 round_wet(e, 0)
                 round_wet(e, 1)
-            for e in pair:
+            for e in next_experts:
                 quantize_wet(e)
-            times_sigmoid(f)
-            finish_da(f)
+            derivative_products(f)
             group_product(f - 1)
-            early = 2 if pair else 1
-            fetch_dx(f - 1, 0, early, "tanh%d" % f)
-            interleave_da(f)
+            early = 2 if next_experts else 1
+            fetch_dx(f - 1, 0, early)
             quantize_da(f)
-            fetch_dx(f - 1, early, W // P - early, "grouped4" if f == 1 else "planes%d" % f)
-            for e in pair:
+            fetch_dx(f - 1, early, ROW_TILES - early)
+            for e in next_experts:
                 expert_product(e)
-            for c in range(W // P):
-                scatter_dx(f - 1, c)
-            if pair:
+            scatter_dx(f - 1)
+            if next_experts:
                 scatter_z(f + 1, 0, C1)
         group_product(G - 1)
         fetch_dx(G - 1, 0, 2)
         fetch_dx(G - 1, 2, 2)
-        for c in range(W // P):
-            scatter_dx(G - 1, c)
+        scatter_dx(G - 1)

@@ -22,35 +22,33 @@ ROW_TILES = W // P
 LIST = 16
 QUADRANTS, QUADRANT = 4, 32
 SCALE_ROWS = 4
-MIN_WINDOW = 2 * C1
-HALVED = (0, 1, 3, 5)
+PAIRS, CP = 2, 2 * C1
+UNITS = 2 * E
 FLOPS = 2 * 2 * W * W * T
 
 TAKES_PLACE_OF = {
-    "z_sb0": "raw1_0",
-    "z_sb1": "raw3_0",
-    "z_sb2": "raw5_0",
-    "z_sb3": "raw7",
-    "wet_c4": "raw5_0",
-    "wet_c6": "raw7",
-    "z_win0_2": "raw1_1",
-    "z_win0_3": "grouped1",
-    "z_win1_2": "raw3_1",
-    "z_win1_3": "grouped3",
-    "half0": "raw2",
-    "half2": "grouped6",
-    "da_bf1": "raw5_1",
-    "dx0_0": "tanh1",
-    "dx1_0": "tanh2",
-    "dx2_0": "tanh3",
-    "dx0_2": "grouped4",
-    "dx1_2": "planes2",
-    "dx2_1": "planes3",
-    "raw6": "raw4",
-    "half1": "grouped0",
-    "half3": "grouped2",
-    "da_bf2": "grouped1",
-    "da_bf3": "grouped3",
+    "slot_w1": "raw0",
+    "z_win0_2": "grouped2",
+    "z_win0_3": "z_win0_3",
+    "tanh0_0": "wet_s7",
+    "tanh0_1": "wet_s9",
+    "silu0": "wet_s11",
+    "tanh1_0": "da_bf0",
+    "tanh1_1": "planes1",
+    "z_sb15": "planes0",
+    "silu1": "da_c1",
+    "half0": "raw1",
+    "half1": "raw2",
+    "out_sb1": "a1",
+    "out_sb2": "planes3",
+    "out_sb3": "planes2",
+    "out_sb0": "raw3",
+    "dx0_0": "raw4",
+    "dx0_1": "raw5",
+    "dx0_2": "raw6",
+    "dx0_3": "raw7",
+    **{"wet_c%d" % u: "unit%d" % (u % 4) for u in range(UNITS)},
+    **{"grouped%d" % u: "unit%d" % ((u - 2) % 4) for u in range(3, UNITS)},
 }
 
 
@@ -60,8 +58,11 @@ def tile_moe_hib_silu_kernel(
     nc = tc.nc
     with ExitStack() as ctx:
         held = ctx.enter_context(tc.tile_pool(name="held", bufs=1))
-        ring2 = ctx.enter_context(tc.tile_pool(name="ring2", bufs=2))
-        psum = ctx.enter_context(tc.psum_pool(name="psum", bufs=2))
+        ring = ctx.enter_context(tc.tile_pool(name="ring", bufs=3))
+        psum = ctx.enter_context(tc.psum_pool(name="psum", bufs=8))
+
+        def place(shape, dtype, name):
+            return held.tile(shape, dtype, name=name, tag=TAKES_PLACE_OF.get(name, name), align_bytes=64)
 
         offs_sb = held.tile([P, T // LIST], U16, name="offs_sb")
         offs2_sb = held.tile([P, T // LIST], U16, name="offs2_sb")
@@ -71,158 +72,163 @@ def tile_moe_hib_silu_kernel(
         zero = held.tile([P, 1], F32, name="zero")
         no_bias = held.tile([P, 1], F32, name="no_bias")
         wgt_s = held.tile([P, W], U8, name="wgt_s", align_bytes=64)
-        wgt_w = [held.tile([P, W], I32, name="wgt_w%d" % f, align_bytes=64) for f in range(G)]
-        gate_sb = [held.tile([P, C1], F32, name="gate%d" % f, align_bytes=64) for f in range(G)]
-        wet_s = [held.tile([P, W], U8, name="wet_s%d" % e, align_bytes=64) for e in range(E)]
-        out_sb = [held.tile([P, T], F32, name="out_sb%d" % c, align_bytes=64) for c in range(ROW_TILES)]
+        wgt_w = held.tile([P, G, W], I32, name="wgt_w", align_bytes=64)
+        shares = (slice(0, C1), slice(C1, T))
+        gate_sb = [held.tile([P, s.stop - s.start], F32, name="gate%d" % x, align_bytes=64) for x, s in enumerate(shares)]
 
-        raw, grouped, wet_c, slot_w, slot_s, z_sb, z_win = {}, {}, {}, {}, {}, {}, {}
+        raw, grouped, wet_c, wet_s, slot_w, slot_s, z_sb, z_win = {}, {}, {}, {}, {}, {}, {}, {}
         a_sb, tanh_sb, silu_sb, half_sb, planes, da_bf, da_c, da_s = {}, {}, {}, {}, {}, {}, {}, {}
-        dx_bank, dx_sb = {}, {}
-
-        def place(shape, dtype, name):
-            return held.tile(shape, dtype, name=name, tag=TAKES_PLACE_OF.get(name, name), align_bytes=64)
+        dx_sb, out_sb, z_bank = {}, {}, {}
 
         def entries(first, count):
             return slice(first // LIST, (first + count) // LIST)
 
+        def in_share(tiles, e):
+            x = 0 if e * C2 < C1 else 1
+            first = e * C2 - shares[x].start
+            return tiles[x][:, first : first + C2]
+
         def load_wet(e):
-            rows = wet[e].rearrange("(p j) i -> p j i", j=PACK)
-            halves = [slice(h * W // 2, (h + 1) * W // 2) for h in range(2)]
-            if e in HALVED:
-                for h in range(2):
-                    raw[e, h] = place([P, PACK, W // 2], F32, "raw%d_%d" % (e, h))
-                    nc.sync.dma_start(out=raw[e, h][:], in_=rows[:, :, halves[h]])
-            else:
-                whole = place([P, PACK, W], F32, "raw%d" % e)
-                nc.sync.dma_start(out=whole[:], in_=rows)
-                for h in range(2):
-                    raw[e, h] = whole[:, :, halves[h]]
+            raw[e] = place([P, PACK, W], F32, "raw%d" % e)
+            nc.sync.dma_start(out=raw[e][:], in_=wet[e].rearrange("(p j) i -> p j i", j=PACK))
 
-        def load_gate_and_a(f):
-            slots = slice(f * C1, (f + 1) * C1)
-            nc.sync.dma_start(out=gate_sb[f][:], in_=gate[:, slots])
-            a_sb[f] = ring2.tile([P, PACK, C1], F32, name="a_sb", align_bytes=64)
-            nc.sync.dma_start(out=a_sb[f][:], in_=a.rearrange("(q t) j -> q t j", t=PACK)[:, :, slots])
+        def load_gate(x):
+            nc.sync.dma_start(out=gate_sb[x][:], in_=gate[:, shares[x]])
 
-        def load_group(f):
-            load_wet(2 * f)
-            load_wet(2 * f + 1)
-            load_gate_and_a(f)
+        def load_a(h, ts):
+            if ts.start == 0:
+                a_sb[h] = place([P, PACK, CP], F32, "a%d" % h)
+            nc.sync.dma_start(
+                out=a_sb[h][:, ts, :], in_=a.rearrange("(q t) j -> q t j", t=PACK)[:, ts, h * CP : (h + 1) * CP]
+            )
 
-        def load_wgt_words(f):
-            nc.sync.dma_start(out=wgt_w[f][:], in_=wgt_words[f, 0].rearrange("p k d -> p (k d)").bitcast(I32))
-
-        def round_wet(e, h, on_vector=False):
-            if h == 0:
-                grouped[e] = place([P, PACK, P, PACK], BF16, "grouped%d" % e)
-            src = raw[e, h][:].rearrange("p j (m t) -> p m j t", t=PACK)
-            to = grouped[e][:].rearrange("p t m j -> p m j t")[:, h * P // 2 : (h + 1) * P // 2]
+        def round_wet(u, on_vector=False):
+            e, x = divmod(u, 2)
+            grouped[u] = place([P, 2, P, PACK], BF16, "grouped%d" % u)
+            src = raw[e][:].rearrange("p j (m t) -> p m j t", t=PACK)[:, :, :, 2 * x : 2 * x + 2]
+            to = grouped[u][:].rearrange("p s m j -> p m j s")
             if on_vector:
                 nc.vector.tensor_copy(out=to, in_=src)
             else:
                 nc.scalar.copy(out=to, in_=src)
 
-        def quantize_wet(e):
-            wet_c[e] = place([P, W], U32, "wet_c%d" % e)
+        def quantize_wet(u):
+            wet_c[u] = place([P, 2 * P], U32, "wet_c%d" % u)
+            wet_s[u] = place([P, 2 * P], U8, "wet_s%d" % u)
             nc.vector.quantize_mx(
-                out=wet_c[e][:].bitcast(FP8X4), scales=wet_s[e][:], in_=grouped[e][:].rearrange("p t m j -> p (t m j)")
+                out=wet_c[u][:].bitcast(FP8X4), scales=wet_s[u][:], in_=grouped[u][:].rearrange("p s m j -> p (s m j)")
             )
 
-        def gather_dy(f):
-            picks = dst_sb[:, entries(f * C1, C1)]
-            slot_w[f] = place([P, C1], U32, "slot_w%d" % f)
-            nc.vector.tensor_copy(slot_w[f][:], dy_w[:].bitcast(U32).indirect(picks))
-            slot_s[f] = place([P, C1], U8, "slot_s%d" % f)
-            nc.vector.tensor_copy(slot_s[f][:], dy_s[:].bitcast(U8).indirect(picks))
+        def gather_scales(h):
+            slot_s[h] = place([P, CP], U8, "slot_s%d" % h)
+            nc.vector.tensor_copy(slot_s[h][:], dy_s[:].bitcast(U8).indirect(dst_sb[:, entries(h * CP, CP)]))
 
-        def expert_product(e):
-            f, u = divmod(e, 2)
-            if u == 0:
-                z_sb[f] = place([P, PACK, C1], F32, "z_sb%d" % f)
-            bank = psum.tile([P, PACK, C2], F32, name="z_bank")
-            slots = slice(u * C2, (u + 1) * C2)
-            for t in range(PACK):
+        def gather_words(x):
+            count = shares[x].stop - shares[x].start
+            slot_w[x] = place([P, count], U32, "slot_w%d" % x)
+            nc.vector.tensor_copy(slot_w[x][:], dy_w[:].bitcast(U32).indirect(dst_sb[:, entries(shares[x].start, count)]))
+
+        def expert_product(u):
+            e = u // 2
+            bank = psum.tile([P, 2, C2], F32, name="bank")
+            h, first = divmod(e * C2, CP)
+            for s in range(2):
                 nc.tensor.matmul_mx(
-                    out=bank[:, t, :],
-                    lhsT=wet_c[e][:, t * P : (t + 1) * P].bitcast(FP8X4),
-                    lhsT_scale=wet_s[e][:, t * P : (t + 1) * P],
-                    rhs=slot_w[f][:, slots].bitcast(FP8X4),
-                    rhs_scale=slot_s[f][:, slots],
+                    out=bank[:, s, :],
+                    lhsT=wet_c[u][:, s * P : (s + 1) * P].bitcast(FP8X4),
+                    lhsT_scale=wet_s[u][:, s * P : (s + 1) * P],
+                    rhs=in_share(slot_w, e).bitcast(FP8X4),
+                    rhs_scale=slot_s[h][:, first : first + C2],
                     start=True,
                     stop=True,
                 )
-            nc.scalar.activation(out=z_sb[f][:, :, slots], in_=bank[:], func=ACT.Copy, scale=-0.5)
+            z_bank[u] = bank
 
-        def scatter_z(f, first, count):
-            slots = slice(first, first + count)
-            for t in range(PACK):
-                if first == 0:
-                    z_win[f, t] = place([P, max(MIN_WINDOW, (f + 1) * C1)], F32, "z_win%d_%d" % (f, t))
+        def fetch_z(u):
+            z_sb[u] = place([P, 2, C2], F32, "z_sb%d" % u)
+            nc.scalar.activation(out=z_sb[u][:], in_=z_bank[u][:], func=ACT.Copy, scale=-0.5)
+
+        def scatter_z(u):
+            e, x = divmod(u, 2)
+            h = e * C2 // CP
+            for s in range(2):
+                t = 2 * x + s
+                if (h, t) not in z_win:
+                    z_win[h, t] = place([P, (h + 1) * CP], F32, "z_win%d_%d" % (h, t))
                 nc.vector.tensor_tensor(
-                    z_win[f, t][:].indirect(offs2_sb[:, entries(f * C1 + first, count)]),
-                    z_sb[f][:, t, slots],
-                    gate_sb[f][:, slots],
-                    ALU.mult,
+                    z_win[h, t][:].indirect(offs2_sb[:, entries(e * C2, C2)]), z_sb[u][:, s, :], in_share(gate_sb, e), ALU.mult
                 )
 
-        def activations(f):
-            tanh_sb[f] = place([P, PACK, C1], F32, "tanh%d" % f)
-            silu_sb[f] = ring2.tile([P, PACK, C1], F32, name="silu_sb", align_bytes=64)
-            nc.scalar.activation(out=tanh_sb[f][:], in_=a_sb[f][:], func=ACT.Tanh, scale=0.5, bias=no_bias[:])
-            nc.scalar.activation(out=silu_sb[f][:], in_=a_sb[f][:], func=ACT.Silu, scale=-1.0, bias=no_bias[:])
+        def tanh_of(h, t):
+            x, s = divmod(t, 2)
+            if s == 0:
+                tanh_sb[h, x] = place([P, 2, CP], F32, "tanh%d_%d" % (h, x))
+            nc.scalar.activation(out=tanh_sb[h, x][:, s, :], in_=a_sb[h][:, t, :], func=ACT.Tanh, scale=0.5, bias=no_bias[:])
 
-        def derivative_products(f):
-            half_sb[f] = place([P, PACK, C1], F32, "half%d" % f)
-            for t in range(PACK):
-                scattered = z_win[f, t][:, f * C1 : (f + 1) * C1]
-                nc.vector.scalar_tensor_tensor(half_sb[f][:, t, :], tanh_sb[f][:, t, :], 1.0, scattered, ALU.add, ALU.mult)
+        def silu_of(f):
+            h, u = divmod(f, 2)
+            slots = slice(u * C1, (u + 1) * C1)
+            if u == 0:
+                silu_sb[h] = place([P, PACK, CP], F32, "silu%d" % h)
+            nc.scalar.activation(
+                out=silu_sb[h][:, :, slots], in_=a_sb[h][:, :, slots], func=ACT.Silu, scale=-1.0, bias=no_bias[:]
+            )
+
+        def first_product(h, t, slots):
+            if h not in half_sb:
+                half_sb[h] = place([P, PACK, CP], F32, "half%d" % h)
+            scattered = z_win[h, t][:, h * CP : (h + 1) * CP]
+            nc.vector.scalar_tensor_tensor(
+                half_sb[h][:, t, slots], tanh_sb[h, t // 2][:, t % 2, slots], 1.0, scattered[:, slots], ALU.add, ALU.mult
+            )
+
+        def second_product(f):
+            h, u = divmod(f, 2)
+            slots = slice(u * C1, (u + 1) * C1)
             planes[f] = place([P, PACK, C1], BF16, "planes%d" % f)
-            for two in (slice(0, 2), slice(2, 4)):
-                nc.vector.scalar_tensor_tensor(
-                    planes[f][:, two, :], silu_sb[f][:, two, :], 1.0, half_sb[f][:, two, :], ALU.subtract, ALU.mult
-                )
+            nc.vector.scalar_tensor_tensor(
+                planes[f][:], silu_sb[h][:, :, slots], 1.0, half_sb[h][:, :, slots], ALU.subtract, ALU.mult
+            )
+
+        def interleave_da(f):
+            da_bf[f] = place([P, C1, PACK], BF16, "da_bf%d" % f)
+            nc.scalar.copy(
+                out=da_bf[f][:].rearrange("q (c i) t -> q c t i", i=PACK),
+                in_=planes[f][:].rearrange("q t (c i) -> q c t i", i=PACK),
+            )
 
         def quantize_da(f):
-            da_bf[f] = place([P, C1, PACK], BF16, "da_bf%d" % f)
-            nc.scalar.copy(out=da_bf[f][:], in_=planes[f][:].rearrange("q t j -> q j t"))
-            da_c[f] = ring2.tile([P, C1], U32, name="da_c", align_bytes=64)
-            da_s[f] = ring2.tile([P, C1], U8, name="da_s", align_bytes=64)
+            da_c[f] = place([P, C1], U32, "da_c%d" % f)
+            da_s[f] = place([P, C1], U8, "da_s%d" % f)
             nc.vector.quantize_mx(
                 out=da_c[f][:].bitcast(FP8X4), scales=da_s[f][:], in_=da_bf[f][:].rearrange("q j t -> q (j t)")
             )
 
-        def group_product(f):
-            for b in range(2):
-                dx_bank[f, b] = psum.tile([P, 2, C1], F32, name="dx_bank", bufs=4)
-                for s in range(2):
-                    ks = slice((2 * b + s) * P, (2 * b + s + 1) * P)
+        def group_products(h):
+            for c in range(ROW_TILES):
+                bank = psum.tile([P, 2, C1], F32, name="bank")
+                ks = slice(c * P, (c + 1) * P)
+                for u in range(2):
+                    f = 2 * h + u
                     nc.tensor.matmul_mx(
-                        out=dx_bank[f, b][:, s, :],
-                        lhsT=wgt_w[f][:, ks].bitcast(FP8X4),
+                        out=bank[:, u, :],
+                        lhsT=wgt_w[:, f, ks].bitcast(FP8X4),
                         lhsT_scale=wgt_s[SCALE_ROWS * f : P, ks],
                         rhs=da_c[f][:].bitcast(FP8X4),
                         rhs_scale=da_s[f][:],
                         start=True,
                         stop=True,
                     )
+                dx_sb[h, c] = place([P, CP], F32, "dx%d_%d" % (h, c))
+                nc.scalar.copy(out=dx_sb[h, c][:], in_=bank[:].rearrange("p u j -> p (u j)"))
 
-        def fetch_dx(f, first, count):
-            rows = place([P, count, C1], F32, "dx%d_%d" % (f, first))
-            for b in range(2):
-                low, high = max(first, 2 * b), min(first + count, 2 * b + 2)
-                if low < high:
-                    nc.scalar.copy(
-                        out=rows[:, low - first : high - first, :], in_=dx_bank[f, b][:, low - 2 * b : high - 2 * b, :]
-                    )
-            for c in range(first, first + count):
-                dx_sb[f, c] = rows[:, c - first, :]
+        def scatter_dx(h, c):
+            if h == 0:
+                out_sb[c] = place([P, T], F32, "out_sb%d" % c)
+            nc.vector.tensor_copy(out_sb[c][:].indirect(offs_sb[:, entries(h * CP, CP)]), dx_sb[h, c][:])
+            if h == PAIRS - 1:
+                nc.sync.dma_start(out=out[c * P : (c + 1) * P, :], in_=out_sb[c][:])
 
-        def scatter_dx(f):
-            for c in range(ROW_TILES):
-                nc.vector.tensor_copy(out_sb[c][:].indirect(offs_sb[:, entries(f * C1, C1)]), dx_sb[f, c])
-                if f == G - 1:
-                    nc.sync.dma_start(out=out[c * P : (c + 1) * P, :], in_=out_sb[c][:])
 
         nc.gpsimd.memset(wgt_s[:].bitcast(I32), 0)
 
@@ -235,72 +241,79 @@ def tile_moe_hib_silu_kernel(
         load_wet(0)
         nc.sync.dma_start(out=dy_w[:], in_=dy_words[0].rearrange("p t d -> p (t d)").bitcast(I32))
         nc.sync.dma_start(offs2_sb[:], offs2)
+        load_gate(0)
         load_wet(1)
-        load_gate_and_a(0)
-
-        nc.vector.memset(zero[:], 0.0)
-        nc.scalar.activation(out=no_bias[:], in_=zero[:], func=ACT.Silu)
-
-        round_wet(0, 0)
-        round_wet(0, 1, on_vector=True)
-        quantize_wet(0)
-        gather_dy(0)
-        round_wet(1, 0)
-        expert_product(0)
-        round_wet(1, 1)
-        quantize_wet(1)
-        scatter_z(0, 0, C2)
-        expert_product(1)
-        for f in range(1, G):
-            gather_dy(f)
-        scatter_z(0, C2, C2)
-        activations(0)
-
-        load_group(1)
+        load_wet(2)
+        load_wet(3)
+        load_gate(1)
+        load_wet(4)
+        load_wet(5)
+        load_a(0, slice(0, 2))
+        load_wet(6)
+        load_a(0, slice(2, PACK))
+        load_wet(7)
+        load_a(1, slice(0, PACK))
         for q in range(QUADRANTS):
             nc.sync.dma_start(
                 out=wgt_s[QUADRANT * q : QUADRANT * q + G * SCALE_ROWS, :].bitcast(I32),
                 in_=wgt_scales[:, 0, SCALE_ROWS * q : SCALE_ROWS * (q + 1), :].bitcast(I32),
             )
-        load_wgt_words(0)
+        nc.sync.dma_start(out=wgt_w[:], in_=wgt_words[:, 0].rearrange("f p k d -> p f (k d)").bitcast(I32))
         nc.sync.dma_start(offs_sb[:], offs)
 
-        round_wet(2, 0)
-        round_wet(2, 1)
-        quantize_wet(2)
-        expert_product(2)
-        derivative_products(0)
-        quantize_da(0)
-        round_wet(3, 0)
-        round_wet(3, 1)
-        quantize_wet(3)
-        scatter_z(1, 0, C2)
-        expert_product(3)
-        scatter_z(1, C2, C2)
+        nc.vector.memset(zero[:], 0.0)
+        nc.scalar.activation(out=no_bias[:], in_=zero[:], func=ACT.Silu)
 
-        for f in range(1, G):
-            next_experts = range(2 * f + 2, min(2 * f + 4, E))
-            activations(f)
-            if next_experts:
-                load_group(f + 1)
-            load_wgt_words(f)
-            for e in next_experts:
-                round_wet(e, 0)
-                round_wet(e, 1)
-            for e in next_experts:
-                quantize_wet(e)
-            derivative_products(f)
-            group_product(f - 1)
-            early = 2 if next_experts else 1
-            fetch_dx(f - 1, 0, early)
-            quantize_da(f)
-            fetch_dx(f - 1, early, ROW_TILES - early)
-            for e in next_experts:
-                expert_product(e)
-            scatter_dx(f - 1)
-            if next_experts:
-                scatter_z(f + 1, 0, C1)
-        group_product(G - 1)
-        fetch_dx(G - 1, 0, 2)
-        fetch_dx(G - 1, 2, 2)
-        scatter_dx(G - 1)
+        for h in range(PAIRS):
+            gather_scales(h)
+        round_wet(0, on_vector=True)
+        round_wet(1)
+        gather_words(0)
+        quantize_wet(0)
+        quantize_wet(1)
+        gather_words(1)
+
+        whole = slice(0, CP)
+        for u in range(UNITS - 1):
+            expert_product(u)
+            fetch_z(u)
+            if u + 2 < UNITS:
+                round_wet(u + 2)
+            if 7 <= u < 11:
+                tanh_of(0, u - 7)
+            if 11 <= u < 13:
+                silu_of(u - 11)
+            if 13 <= u:
+                interleave_da(u - 13)
+            scatter_z(u)
+            if u + 2 < UNITS:
+                quantize_wet(u + 2)
+            if 7 <= u < 11:
+                first_product(0, u - 7, whole)
+            if 11 <= u < 13:
+                second_product(u - 11)
+        expert_product(UNITS - 1)
+        quantize_da(0)
+        quantize_da(1)
+        fetch_z(UNITS - 1)
+        for t in range(PACK):
+            tanh_of(1, t)
+        scatter_z(UNITS - 1)
+        for t in range(PACK):
+            first_product(1, t, whole)
+        group_products(0)
+        silu_of(2)
+        silu_of(3)
+        scatter_dx(0, 0)
+        second_product(2)
+        second_product(3)
+        interleave_da(2)
+        interleave_da(3)
+        scatter_dx(0, 1)
+        quantize_da(2)
+        quantize_da(3)
+        scatter_dx(0, 3)
+        scatter_dx(0, 2)
+        group_products(1)
+        for c in range(ROW_TILES):
+            scatter_dx(1, c)

@@ -33,20 +33,21 @@ TAKES_PLACE_OF = {
     "tanh0_0": "wet_s7",
     "tanh0_1": "wet_s9",
     "silu0": "wet_s11",
-    "tanh1_0": "da_bf0",
-    "tanh1_1": "planes1",
     "z_sb15": "planes0",
-    "silu1": "da_c1",
+    "tanh_g2": "planes1",
+    "tanh_g3": "raw6",
+    "plus_g2": "planes0",
+    "silu_g2": "raw2",
+    "silu_g3": "raw2",
+    "slope2": "raw4",
+    "slope3": "raw4",
     "half0": "raw1",
-    "half1": "raw2",
-    "out_sb1": "a1",
-    "out_sb2": "planes3",
-    "out_sb3": "planes2",
+    "dx1_0_0": "planes3",
+    "out_sb2": "minus_g2",
+    "out_sb3": "plus_g3",
     "out_sb0": "raw3",
-    "dx0_0": "raw4",
-    "dx0_1": "raw5",
-    "dx0_2": "raw6",
-    "dx0_3": "raw7",
+        "dx0_1_0": "raw5",
+    "dx0_3_0": "raw7",
     **{"wet_c%d" % u: "unit%d" % (u % 4) for u in range(UNITS)},
     **{"grouped%d" % u: "unit%d" % ((u - 2) % 4) for u in range(3, UNITS)},
 }
@@ -78,7 +79,9 @@ def tile_moe_hib_silu_kernel(
 
         raw, grouped, wet_c, wet_s, slot_w, slot_s, z_sb, z_win = {}, {}, {}, {}, {}, {}, {}, {}
         a_sb, tanh_sb, silu_sb, half_sb, planes, da_bf, da_c, da_s = {}, {}, {}, {}, {}, {}, {}, {}
-        dx_sb, out_sb, z_bank = {}, {}, {}
+        dx_sb, out_sb, z_bank, plus, minus, slope, dx_bank = {}, {}, {}, {}, {}, {}, {}
+        minus_one = held.tile([P, 1], F32, name="minus_one")
+        nc.vector.memset(minus_one[:], -1.0)
 
         def entries(first, count):
             return slice(first // LIST, (first + count) // LIST)
@@ -190,6 +193,29 @@ def tile_moe_hib_silu_kernel(
                 planes[f][:], silu_sb[h][:, :, slots], 1.0, half_sb[h][:, :, slots], ALU.subtract, ALU.mult
             )
 
+        def plus_factor(f):
+            slots = slice((f % 2) * C1, (f % 2 + 1) * C1)
+            th = place([P, PACK, C1], F32, "tanh_g%d" % f)
+            plus[f] = place([P, PACK, C1], F32, "plus_g%d" % f)
+            nc.scalar.activation(out=th[:], in_=a_sb[1][:, :, slots], func=ACT.Tanh, scale=0.5, bias=no_bias[:])
+            nc.gpsimd.tensor_scalar(plus[f][:], th[:], 1.0, 1.0, ALU.mult, ALU.add)
+
+        def minus_factor(f):
+            slots = slice((f % 2) * C1, (f % 2 + 1) * C1)
+            sl = place([P, PACK, C1], F32, "silu_g%d" % f)
+            minus[f] = place([P, PACK, C1], F32, "minus_g%d" % f)
+            nc.scalar.activation(out=sl[:], in_=a_sb[1][:, :, slots], func=ACT.Silu, scale=-1.0, bias=no_bias[:])
+            nc.scalar.activation(out=minus[f][:], in_=sl[:], func=ACT.Identity, bias=minus_one[:])
+
+        def slope_on_gpsimd(f):
+            slope[f] = place([P, PACK, C1], F32, "slope%d" % f)
+            nc.gpsimd.tensor_tensor(slope[f][:], plus[f][:], minus[f][:], ALU.mult)
+
+        def only_product(f):
+            planes[f] = place([P, PACK, C1], BF16, "planes%d" % f)
+            for t in range(PACK):
+                nc.vector.tensor_tensor(planes[f][:, t, :], slope[f][:, t, :], z_win[1, t][:, f * C1 : (f + 1) * C1], ALU.mult)
+
         def interleave_da(f):
             da_bf[f] = place([P, C1, PACK], BF16, "da_bf%d" % f)
             nc.scalar.copy(
@@ -204,31 +230,31 @@ def tile_moe_hib_silu_kernel(
                 out=da_c[f][:].bitcast(FP8X4), scales=da_s[f][:], in_=da_bf[f][:].rearrange("q j t -> q (j t)")
             )
 
-        def group_products(h):
-            for c in range(ROW_TILES):
-                bank = psum.tile([P, 2, C1], F32, name="bank")
-                ks = slice(c * P, (c + 1) * P)
-                for u in range(2):
-                    f = 2 * h + u
-                    nc.tensor.matmul_mx(
-                        out=bank[:, u, :],
-                        lhsT=wgt_w[:, f, ks].bitcast(FP8X4),
-                        lhsT_scale=wgt_s[SCALE_ROWS * f : P, ks],
-                        rhs=da_c[f][:].bitcast(FP8X4),
-                        rhs_scale=da_s[f][:],
-                        start=True,
-                        stop=True,
-                    )
-                dx_sb[h, c] = place([P, CP], F32, "dx%d_%d" % (h, c))
-                nc.scalar.copy(out=dx_sb[h, c][:], in_=bank[:].rearrange("p u j -> p (u j)"))
+        def dx_product(f, c):
+            h, u = divmod(f, 2)
+            if u == 0:
+                dx_bank[h, c] = psum.tile([P, CP], F32, name="bank")
+            ks = slice(c * P, (c + 1) * P)
+            nc.tensor.matmul_mx(
+                out=dx_bank[h, c][:, u * C1 : (u + 1) * C1],
+                lhsT=wgt_w[:, f, ks].bitcast(FP8X4),
+                lhsT_scale=wgt_s[SCALE_ROWS * f : P, ks],
+                rhs=da_c[f][:].bitcast(FP8X4),
+                rhs_scale=da_s[f][:],
+                start=True,
+                stop=True,
+            )
 
-        def scatter_dx(h, c):
+        def fetch_dx(h, c, first=0, count=CP):
+            dx_sb[h, c, first] = place([P, count], F32, "dx%d_%d_%d" % (h, c, first))
+            nc.scalar.copy(out=dx_sb[h, c, first][:], in_=dx_bank[h, c][:, first : first + count])
+
+        def scatter_dx(h, c, first=0, count=CP):
             if h == 0:
                 out_sb[c] = place([P, T], F32, "out_sb%d" % c)
-            nc.vector.tensor_copy(out_sb[c][:].indirect(offs_sb[:, entries(h * CP, CP)]), dx_sb[h, c][:])
-            if h == PAIRS - 1:
+            nc.vector.tensor_copy(out_sb[c][:].indirect(offs_sb[:, entries(h * CP + first, count)]), dx_sb[h, c, first][:])
+            if h * CP + first + count == T:
                 nc.sync.dma_start(out=out[c * P : (c + 1) * P, :], in_=out_sb[c][:])
-
 
         nc.gpsimd.memset(wgt_s[:].bitcast(I32), 0)
 
@@ -296,24 +322,41 @@ def tile_moe_hib_silu_kernel(
         quantize_da(0)
         quantize_da(1)
         fetch_z(UNITS - 1)
-        for t in range(PACK):
-            tanh_of(1, t)
         scatter_z(UNITS - 1)
-        for t in range(PACK):
-            first_product(1, t, whole)
-        group_products(0)
-        silu_of(2)
-        silu_of(3)
-        scatter_dx(0, 0)
-        second_product(2)
-        second_product(3)
-        interleave_da(2)
-        interleave_da(3)
-        scatter_dx(0, 1)
-        quantize_da(2)
-        quantize_da(3)
-        scatter_dx(0, 3)
-        scatter_dx(0, 2)
-        group_products(1)
+        plus_factor(2)
         for c in range(ROW_TILES):
-            scatter_dx(1, c)
+            dx_product(0, c)
+            dx_product(1, c)
+        fetch_dx(0, 0)
+        minus_factor(2)
+        fetch_dx(0, 1)
+        slope_on_gpsimd(2)
+        scatter_dx(0, 0)
+        scatter_dx(0, 1)
+        plus_factor(3)
+        minus_factor(3)
+        fetch_dx(0, 2)
+        only_product(2)
+        interleave_da(2)
+        fetch_dx(0, 3)
+        slope_on_gpsimd(3)
+        scatter_dx(0, 2)
+        only_product(3)
+        interleave_da(3)
+        quantize_da(2)
+        scatter_dx(0, 3)
+        for c in range(ROW_TILES):
+            dx_product(2, c)
+        quantize_da(3)
+        fetch_dx(1, 0, 0, C1)
+        scatter_dx(1, 0, 0, C1)
+        for c in (1, 0, 2, 3):
+            dx_product(3, c)
+        fetch_dx(1, 1)
+        fetch_dx(1, 0, C1, C1)
+        fetch_dx(1, 2)
+        fetch_dx(1, 3)
+        scatter_dx(1, 1)
+        scatter_dx(1, 0, C1, C1)
+        scatter_dx(1, 2)
+        scatter_dx(1, 3)

@@ -33,18 +33,18 @@ TAKES_PLACE_OF = {
     "tanh0_0": "wet_s7",
     "tanh0_1": "wet_s9",
     "silu0": "wet_s11",
-    "z_sb15": "planes0",
-    "tanh_g2": "planes1",
+    "z_sb15": "planes1",
+    "plus_g2": "planes1",
+    "tanh_g2": "planes0",
     "tanh_g3": "raw6",
-    "plus_g2": "planes0",
-    "silu_g2": "raw2",
+    "silu_g2": "da_bf0",
     "silu_g3": "raw2",
     "slope2": "raw4",
     "slope3": "raw4",
+    "planes3": "da_bf2",
     "half0": "raw1",
-    "dx1_0_0": "planes3",
-    "out_sb2": "minus_g2",
-    "out_sb3": "plus_g3",
+    "dx1_1_0": "da_bf2",
+    "out_sb3": "planes2",
     "out_sb0": "raw3",
         "dx0_1_0": "raw5",
     "dx0_3_0": "raw7",
@@ -80,6 +80,8 @@ def tile_moe_hib_silu_kernel(
         raw, grouped, wet_c, wet_s, slot_w, slot_s, z_sb, z_win = {}, {}, {}, {}, {}, {}, {}, {}
         a_sb, tanh_sb, silu_sb, half_sb, planes, da_bf, da_c, da_s = {}, {}, {}, {}, {}, {}, {}, {}
         dx_sb, out_sb, z_bank, plus, minus, slope, dx_bank = {}, {}, {}, {}, {}, {}, {}
+        one = held.tile([P, 1], F32, name="one")
+        nc.vector.memset(one[:], 1.0)
         minus_one = held.tile([P, 1], F32, name="minus_one")
         nc.vector.memset(minus_one[:], -1.0)
 
@@ -193,18 +195,27 @@ def tile_moe_hib_silu_kernel(
                 planes[f][:], silu_sb[h][:, :, slots], 1.0, half_sb[h][:, :, slots], ALU.subtract, ALU.mult
             )
 
-        def plus_factor(f):
+        def group_tanh(f):
             slots = slice((f % 2) * C1, (f % 2 + 1) * C1)
-            th = place([P, PACK, C1], F32, "tanh_g%d" % f)
+            tanh_sb[f] = place([P, PACK, C1], F32, "tanh_g%d" % f)
+            nc.scalar.activation(out=tanh_sb[f][:], in_=a_sb[1][:, :, slots], func=ACT.Tanh, scale=0.5, bias=no_bias[:])
+
+        def plus_factor(f, on_gpsimd):
+            th = tanh_sb[f]
             plus[f] = place([P, PACK, C1], F32, "plus_g%d" % f)
-            nc.scalar.activation(out=th[:], in_=a_sb[1][:, :, slots], func=ACT.Tanh, scale=0.5, bias=no_bias[:])
-            nc.gpsimd.tensor_scalar(plus[f][:], th[:], 1.0, 1.0, ALU.mult, ALU.add)
+            if on_gpsimd:
+                nc.gpsimd.tensor_scalar(plus[f][:], th[:], 1.0, 1.0, ALU.mult, ALU.add)
+            else:
+                nc.scalar.activation(out=plus[f][:], in_=th[:], func=ACT.Identity, bias=one[:])
+
+        def group_silu(f):
+            slots = slice((f % 2) * C1, (f % 2 + 1) * C1)
+            silu_sb[f] = place([P, PACK, C1], F32, "silu_g%d" % f)
+            nc.scalar.activation(out=silu_sb[f][:], in_=a_sb[1][:, :, slots], func=ACT.Silu, scale=-1.0, bias=no_bias[:])
 
         def minus_factor(f):
-            slots = slice((f % 2) * C1, (f % 2 + 1) * C1)
-            sl = place([P, PACK, C1], F32, "silu_g%d" % f)
+            sl = silu_sb[f]
             minus[f] = place([P, PACK, C1], F32, "minus_g%d" % f)
-            nc.scalar.activation(out=sl[:], in_=a_sb[1][:, :, slots], func=ACT.Silu, scale=-1.0, bias=no_bias[:])
             nc.scalar.activation(out=minus[f][:], in_=sl[:], func=ACT.Identity, bias=minus_one[:])
 
         def slope_on_gpsimd(f):
@@ -214,7 +225,7 @@ def tile_moe_hib_silu_kernel(
         def only_product(f):
             planes[f] = place([P, PACK, C1], BF16, "planes%d" % f)
             for t in range(PACK):
-                nc.vector.tensor_tensor(planes[f][:, t, :], slope[f][:, t, :], z_win[1, t][:, f * C1 : (f + 1) * C1], ALU.mult)
+                nc.gpsimd.tensor_tensor(planes[f][:, t, :], slope[f][:, t, :], z_win[1, t][:, f * C1 : (f + 1) * C1], ALU.mult)
 
         def interleave_da(f):
             da_bf[f] = place([P, C1, PACK], BF16, "da_bf%d" % f)
@@ -321,42 +332,48 @@ def tile_moe_hib_silu_kernel(
         expert_product(UNITS - 1)
         quantize_da(0)
         quantize_da(1)
+        group_tanh(2)
         fetch_z(UNITS - 1)
+        group_silu(2)
         scatter_z(UNITS - 1)
-        plus_factor(2)
+        plus_factor(2, on_gpsimd=True)
         for c in range(ROW_TILES):
             dx_product(0, c)
             dx_product(1, c)
         fetch_dx(0, 0)
         minus_factor(2)
-        fetch_dx(0, 1)
         slope_on_gpsimd(2)
-        scatter_dx(0, 0)
-        scatter_dx(0, 1)
-        plus_factor(3)
+        only_product(2)
+        fetch_dx(0, 1)
+        group_tanh(3)
+        group_silu(3)
+        plus_factor(3, on_gpsimd=False)
         minus_factor(3)
         fetch_dx(0, 2)
-        only_product(2)
+        slope_on_gpsimd(3)
         interleave_da(2)
         fetch_dx(0, 3)
-        slope_on_gpsimd(3)
+        scatter_dx(0, 0)
+        scatter_dx(0, 1)
         scatter_dx(0, 2)
-        only_product(3)
-        interleave_da(3)
         quantize_da(2)
+        only_product(3)
         scatter_dx(0, 3)
         for c in range(ROW_TILES):
             dx_product(2, c)
-        quantize_da(3)
         fetch_dx(1, 0, 0, C1)
+        interleave_da(3)
         scatter_dx(1, 0, 0, C1)
-        for c in (1, 0, 2, 3):
+        quantize_da(3)
+        fetch_dx(1, 1, 0, C1)
+        scatter_dx(1, 1, 0, C1)
+        for c in (0, 2, 3, 1):
             dx_product(3, c)
-        fetch_dx(1, 1)
         fetch_dx(1, 0, C1, C1)
+        fetch_dx(1, 1, C1, C1)
         fetch_dx(1, 2)
         fetch_dx(1, 3)
-        scatter_dx(1, 1)
         scatter_dx(1, 0, C1, C1)
+        scatter_dx(1, 1, C1, C1)
         scatter_dx(1, 2)
         scatter_dx(1, 3)

@@ -22,34 +22,39 @@ ROW_TILES = W // P
 LIST = 16
 QUADRANTS, QUADRANT = 4, 32
 SCALE_ROWS = 4
-PAIRS, CP = 2, 2 * C1
 UNITS = 2 * E
 FLOPS = 2 * 2 * W * W * T
 
+FIRST_COPY_UNIT = 14
 TAKES_PLACE_OF = {
     "slot_w1": "raw0",
     "z_win0_2": "grouped2",
-    "z_win0_3": "z_win0_3",
-    "tanh0_0": "wet_s7",
-    "tanh0_1": "wet_s9",
-    "silu0": "wet_s11",
-    "z_sb15": "planes1",
-    "plus_g2": "planes1",
-    "tanh_g2": "planes0",
-    "tanh_g3": "raw6",
-    "silu_g2": "da_bf0",
-    "silu_g3": "raw2",
-    "slope2": "raw4",
-    "slope3": "raw4",
-    "planes3": "da_bf2",
+    "tanh0": "wet_s4",
     "half0": "raw1",
-    "dx1_1_0": "da_bf2",
-    "out_sb3": "planes2",
-    "out_sb0": "raw3",
-        "dx0_1_0": "raw5",
-    "dx0_3_0": "raw7",
+    "tanh1": "wet_s8",
+    "silu1": "silu0",
+    "plus3": "da_c1",
+    "z_sb14": "raw7",
+    **{"minus%d" % f: "a%d" % f for f in range(1, G)},
+    **{"z_sb%d" % u: "z_sb%d" % (u % 4) for u in range(FIRST_COPY_UNIT)},
+    **{"dx%d_%d" % (f, c): "dx%d_%d" % (f % 2, c) for f in range(G) for c in range(ROW_TILES - 1)},
+    "half1": "grouped15",
+    "slope2": "grouped15",
+    "slope3": "grouped15",
+    "tanh2": "wet_s4",
+    "tanh3": "plus1",
+    "silu2": "raw6",
+    "silu3": "raw6",
+    "planes2": "da_bf1",
+    "planes3": "da_bf2",
+    "dx1_3": "da_bf1",
+    "dx2_3": "da_bf2",
+    "out_sb0": "wet_s15",
+    "out_sb1": "raw3",
+    "out_sb2": "raw4",
+    "out_sb3": "planes1",
     **{"wet_c%d" % u: "unit%d" % (u % 4) for u in range(UNITS)},
-    **{"grouped%d" % u: "unit%d" % ((u - 2) % 4) for u in range(3, UNITS)},
+    **{"grouped%d" % u: "unit%d" % ((u - 2) % 4) for u in range(3, UNITS - 2)},
 }
 
 
@@ -100,12 +105,9 @@ def tile_moe_hib_silu_kernel(
         def load_gate(x):
             nc.sync.dma_start(out=gate_sb[x][:], in_=gate[:, shares[x]])
 
-        def load_a(h, ts):
-            if ts.start == 0:
-                a_sb[h] = place([P, PACK, CP], F32, "a%d" % h)
-            nc.sync.dma_start(
-                out=a_sb[h][:, ts, :], in_=a.rearrange("(q t) j -> q t j", t=PACK)[:, ts, h * CP : (h + 1) * CP]
-            )
+        def load_a(f):
+            a_sb[f] = place([P, PACK, C1], F32, "a%d" % f)
+            nc.sync.dma_start(out=a_sb[f][:], in_=a.rearrange("(q t) j -> q t j", t=PACK)[:, :, f * C1 : (f + 1) * C1])
 
         def round_wet(u, on_vector=False):
             e, x = divmod(u, 2)
@@ -125,8 +127,8 @@ def tile_moe_hib_silu_kernel(
             )
 
         def gather_scales(h):
-            slot_s[h] = place([P, CP], U8, "slot_s%d" % h)
-            nc.vector.tensor_copy(slot_s[h][:], dy_s[:].bitcast(U8).indirect(dst_sb[:, entries(h * CP, CP)]))
+            slot_s[h] = place([P, T // 2], U8, "slot_s%d" % h)
+            nc.vector.tensor_copy(slot_s[h][:], dy_s[:].bitcast(U8).indirect(dst_sb[:, entries(h * T // 2, T // 2)]))
 
         def gather_words(x):
             count = shares[x].stop - shares[x].start
@@ -136,7 +138,7 @@ def tile_moe_hib_silu_kernel(
         def expert_product(u):
             e = u // 2
             bank = psum.tile([P, 2, C2], F32, name="bank")
-            h, first = divmod(e * C2, CP)
+            h, first = divmod(e * C2, T // 2)
             for s in range(2):
                 nc.tensor.matmul_mx(
                     out=bank[:, s, :],
@@ -151,81 +153,70 @@ def tile_moe_hib_silu_kernel(
 
         def fetch_z(u):
             z_sb[u] = place([P, 2, C2], F32, "z_sb%d" % u)
-            nc.scalar.activation(out=z_sb[u][:], in_=z_bank[u][:], func=ACT.Copy, scale=-0.5)
+            if u < FIRST_COPY_UNIT:
+                nc.scalar.activation(out=z_sb[u][:], in_=z_bank[u][:], func=ACT.Copy, scale=-0.5)
+            else:
+                both = in_share(gate_sb, u // 2).unsqueeze(1).to_broadcast([P, 2, C2])
+                nc.vector.scalar_tensor_tensor(z_sb[u][:], z_bank[u][:], -0.5, both, ALU.mult, ALU.mult)
 
         def scatter_z(u):
             e, x = divmod(u, 2)
-            h = e * C2 // CP
+            f = e // 2
             for s in range(2):
                 t = 2 * x + s
-                if (h, t) not in z_win:
-                    z_win[h, t] = place([P, (h + 1) * CP], F32, "z_win%d_%d" % (h, t))
-                nc.vector.tensor_tensor(
-                    z_win[h, t][:].indirect(offs2_sb[:, entries(e * C2, C2)]), z_sb[u][:, s, :], in_share(gate_sb, e), ALU.mult
-                )
+                if (f, t) not in z_win:
+                    z_win[f, t] = place([P, max(2, f + 1) * C1], F32, "z_win%d_%d" % (f, t))
+                to = z_win[f, t][:].indirect(offs2_sb[:, entries(e * C2, C2)])
+                if u < FIRST_COPY_UNIT:
+                    nc.vector.tensor_tensor(to, z_sb[u][:, s, :], in_share(gate_sb, e), ALU.mult)
+                else:
+                    nc.vector.tensor_copy(to, z_sb[u][:, s, :])
 
-        def tanh_of(h, t):
-            x, s = divmod(t, 2)
-            if s == 0:
-                tanh_sb[h, x] = place([P, 2, CP], F32, "tanh%d_%d" % (h, x))
-            nc.scalar.activation(out=tanh_sb[h, x][:, s, :], in_=a_sb[h][:, t, :], func=ACT.Tanh, scale=0.5, bias=no_bias[:])
+        def tanh_of(f, ts):
+            if ts.start == 0:
+                tanh_sb[f] = place([P, PACK, C1], F32, "tanh%d" % f)
+            nc.scalar.activation(out=tanh_sb[f][:, ts, :], in_=a_sb[f][:, ts, :], func=ACT.Tanh, scale=0.5, bias=no_bias[:])
 
-        def silu_of(f):
-            h, u = divmod(f, 2)
-            slots = slice(u * C1, (u + 1) * C1)
-            if u == 0:
-                silu_sb[h] = place([P, PACK, CP], F32, "silu%d" % h)
-            nc.scalar.activation(
-                out=silu_sb[h][:, :, slots], in_=a_sb[h][:, :, slots], func=ACT.Silu, scale=-1.0, bias=no_bias[:]
-            )
+        def silu_of(f, ts):
+            if ts.start == 0:
+                silu_sb[f] = place([P, PACK, C1], F32, "silu%d" % f)
+            nc.scalar.activation(out=silu_sb[f][:, ts, :], in_=a_sb[f][:, ts, :], func=ACT.Silu, scale=-1.0, bias=no_bias[:])
 
-        def first_product(h, t, slots):
-            if h not in half_sb:
-                half_sb[h] = place([P, PACK, CP], F32, "half%d" % h)
-            scattered = z_win[h, t][:, h * CP : (h + 1) * CP]
-            nc.vector.scalar_tensor_tensor(
-                half_sb[h][:, t, slots], tanh_sb[h, t // 2][:, t % 2, slots], 1.0, scattered[:, slots], ALU.add, ALU.mult
-            )
+        def scattered(f, t):
+            return z_win[f, t][:, f * C1 : (f + 1) * C1]
+
+        def first_product(f):
+            half_sb[f] = place([P, PACK, C1], F32, "half%d" % f)
+            for t in range(PACK):
+                nc.vector.scalar_tensor_tensor(half_sb[f][:, t, :], tanh_sb[f][:, t, :], 1.0, scattered(f, t), ALU.add, ALU.mult)
 
         def second_product(f):
-            h, u = divmod(f, 2)
-            slots = slice(u * C1, (u + 1) * C1)
             planes[f] = place([P, PACK, C1], BF16, "planes%d" % f)
-            nc.vector.scalar_tensor_tensor(
-                planes[f][:], silu_sb[h][:, :, slots], 1.0, half_sb[h][:, :, slots], ALU.subtract, ALU.mult
-            )
+            nc.vector.scalar_tensor_tensor(planes[f][:], silu_sb[f][:], 1.0, half_sb[f][:], ALU.subtract, ALU.mult)
 
-        def group_tanh(f):
-            slots = slice((f % 2) * C1, (f % 2 + 1) * C1)
-            tanh_sb[f] = place([P, PACK, C1], F32, "tanh_g%d" % f)
-            nc.scalar.activation(out=tanh_sb[f][:], in_=a_sb[1][:, :, slots], func=ACT.Tanh, scale=0.5, bias=no_bias[:])
-
-        def plus_factor(f, on_gpsimd):
-            th = tanh_sb[f]
-            plus[f] = place([P, PACK, C1], F32, "plus_g%d" % f)
-            if on_gpsimd:
-                nc.gpsimd.tensor_scalar(plus[f][:], th[:], 1.0, 1.0, ALU.mult, ALU.add)
-            else:
-                nc.scalar.activation(out=plus[f][:], in_=th[:], func=ACT.Identity, bias=one[:])
-
-        def group_silu(f):
-            slots = slice((f % 2) * C1, (f % 2 + 1) * C1)
-            silu_sb[f] = place([P, PACK, C1], F32, "silu_g%d" % f)
-            nc.scalar.activation(out=silu_sb[f][:], in_=a_sb[1][:, :, slots], func=ACT.Silu, scale=-1.0, bias=no_bias[:])
+        def plus_factor(f):
+            plus[f] = place([P, PACK, C1], F32, "plus%d" % f)
+            nc.scalar.activation(out=plus[f][:], in_=tanh_sb[f][:], func=ACT.Identity, bias=one[:])
 
         def minus_factor(f):
-            sl = silu_sb[f]
-            minus[f] = place([P, PACK, C1], F32, "minus_g%d" % f)
-            nc.scalar.activation(out=minus[f][:], in_=sl[:], func=ACT.Identity, bias=minus_one[:])
+            minus[f] = place([P, PACK, C1], F32, "minus%d" % f)
+            nc.scalar.activation(out=minus[f][:], in_=silu_sb[f][:], func=ACT.Identity, bias=minus_one[:])
 
-        def slope_on_gpsimd(f):
+        def slope_of(f):
             slope[f] = place([P, PACK, C1], F32, "slope%d" % f)
             nc.gpsimd.tensor_tensor(slope[f][:], plus[f][:], minus[f][:], ALU.mult)
 
         def only_product(f):
             planes[f] = place([P, PACK, C1], BF16, "planes%d" % f)
             for t in range(PACK):
-                nc.gpsimd.tensor_tensor(planes[f][:, t, :], slope[f][:, t, :], z_win[1, t][:, f * C1 : (f + 1) * C1], ALU.mult)
+                nc.gpsimd.tensor_tensor(planes[f][:, t, :], slope[f][:, t, :], scattered(f, t), ALU.mult)
+
+        def both_products(f):
+            half_sb[f] = place([P, PACK, C1], F32, "half%d" % f)
+            for t in range(PACK):
+                nc.gpsimd.tensor_tensor(half_sb[f][:, t, :], plus[f][:, t, :], scattered(f, t), ALU.mult)
+            planes[f] = place([P, PACK, C1], BF16, "planes%d" % f)
+            nc.gpsimd.tensor_tensor(planes[f][:], minus[f][:], half_sb[f][:], ALU.mult)
 
         def interleave_da(f):
             da_bf[f] = place([P, C1, PACK], BF16, "da_bf%d" % f)
@@ -241,31 +232,32 @@ def tile_moe_hib_silu_kernel(
                 out=da_c[f][:].bitcast(FP8X4), scales=da_s[f][:], in_=da_bf[f][:].rearrange("q j t -> q (j t)")
             )
 
-        def dx_product(f, c):
-            h, u = divmod(f, 2)
-            if u == 0:
-                dx_bank[h, c] = psum.tile([P, CP], F32, name="bank")
-            ks = slice(c * P, (c + 1) * P)
-            nc.tensor.matmul_mx(
-                out=dx_bank[h, c][:, u * C1 : (u + 1) * C1],
-                lhsT=wgt_w[:, f, ks].bitcast(FP8X4),
-                lhsT_scale=wgt_s[SCALE_ROWS * f : P, ks],
-                rhs=da_c[f][:].bitcast(FP8X4),
-                rhs_scale=da_s[f][:],
-                start=True,
-                stop=True,
-            )
+        def group_product(f):
+            for b in range(2):
+                dx_bank[f, b] = psum.tile([P, 2, C1], F32, name="bank")
+                for s in range(2):
+                    ks = slice((2 * b + s) * P, (2 * b + s + 1) * P)
+                    nc.tensor.matmul_mx(
+                        out=dx_bank[f, b][:, s, :],
+                        lhsT=wgt_w[:, f, ks].bitcast(FP8X4),
+                        lhsT_scale=wgt_s[SCALE_ROWS * f : P, ks],
+                        rhs=da_c[f][:].bitcast(FP8X4),
+                        rhs_scale=da_s[f][:],
+                        start=True,
+                        stop=True,
+                    )
 
-        def fetch_dx(h, c, first=0, count=CP):
-            dx_sb[h, c, first] = place([P, count], F32, "dx%d_%d_%d" % (h, c, first))
-            nc.scalar.copy(out=dx_sb[h, c, first][:], in_=dx_bank[h, c][:, first : first + count])
+        def fetch_dx(f, c):
+            dx_sb[f, c] = place([P, C1], F32, "dx%d_%d" % (f, c))
+            nc.scalar.copy(out=dx_sb[f, c][:], in_=dx_bank[f, c // 2][:, c % 2, :])
 
-        def scatter_dx(h, c, first=0, count=CP):
-            if h == 0:
+        def scatter_dx(f, c):
+            if f == 0:
                 out_sb[c] = place([P, T], F32, "out_sb%d" % c)
-            nc.vector.tensor_copy(out_sb[c][:].indirect(offs_sb[:, entries(h * CP + first, count)]), dx_sb[h, c, first][:])
-            if h * CP + first + count == T:
+            nc.vector.tensor_copy(out_sb[c][:].indirect(offs_sb[:, entries(f * C1, C1)]), dx_sb[f, c][:])
+            if f == G - 1:
                 nc.sync.dma_start(out=out[c * P : (c + 1) * P, :], in_=out_sb[c][:])
+
 
         nc.gpsimd.memset(wgt_s[:].bitcast(I32), 0)
 
@@ -282,14 +274,13 @@ def tile_moe_hib_silu_kernel(
         load_wet(1)
         load_wet(2)
         load_wet(3)
+        load_a(0)
         load_gate(1)
         load_wet(4)
         load_wet(5)
-        load_a(0, slice(0, 2))
+        load_a(1)
         load_wet(6)
-        load_a(0, slice(2, PACK))
         load_wet(7)
-        load_a(1, slice(0, PACK))
         for q in range(QUADRANTS):
             nc.sync.dma_start(
                 out=wgt_s[QUADRANT * q : QUADRANT * q + G * SCALE_ROWS, :].bitcast(I32),
@@ -297,11 +288,13 @@ def tile_moe_hib_silu_kernel(
             )
         nc.sync.dma_start(out=wgt_w[:], in_=wgt_words[:, 0].rearrange("f p k d -> p f (k d)").bitcast(I32))
         nc.sync.dma_start(offs_sb[:], offs)
+        load_a(2)
+        load_a(3)
 
         nc.vector.memset(zero[:], 0.0)
         nc.scalar.activation(out=no_bias[:], in_=zero[:], func=ACT.Silu)
 
-        for h in range(PAIRS):
+        for h in range(2):
             gather_scales(h)
         round_wet(0, on_vector=True)
         round_wet(1)
@@ -310,70 +303,74 @@ def tile_moe_hib_silu_kernel(
         quantize_wet(1)
         gather_words(1)
 
-        whole = slice(0, CP)
-        for u in range(UNITS - 1):
-            expert_product(u)
-            fetch_z(u)
+        low, high, all_planes = slice(0, 2), slice(2, PACK), slice(0, PACK)
+        for u in range(UNITS):
+            if u < FIRST_COPY_UNIT:
+                expert_product(u)
+                fetch_z(u)
             if u + 2 < UNITS:
                 round_wet(u + 2)
-            if 7 <= u < 11:
-                tanh_of(0, u - 7)
-            if 11 <= u < 13:
-                silu_of(u - 11)
-            if 13 <= u:
-                interleave_da(u - 13)
+            if u == 4:
+                tanh_of(0, all_planes)
+            if u == 5:
+                silu_of(0, all_planes)
+            if u == 6:
+                interleave_da(0)
+            if u in (8, 9):
+                tanh_of(1, low if u == 8 else high)
+            if u in (10, 11):
+                silu_of(1, low if u == 10 else high)
+            if u == 13:
+                plus_factor(1)
+                group_product(0)
+                fetch_dx(0, 0)
+                minus_factor(1)
+            if u == UNITS - 1:
+                scatter_dx(0, 0)
             scatter_z(u)
+            if FIRST_COPY_UNIT <= u + 1 < UNITS:
+                expert_product(u + 1)
+                fetch_z(u + 1)
             if u + 2 < UNITS:
                 quantize_wet(u + 2)
-            if 7 <= u < 11:
-                first_product(0, u - 7, whole)
-            if 11 <= u < 13:
-                second_product(u - 11)
-        expert_product(UNITS - 1)
-        quantize_da(0)
-        quantize_da(1)
-        group_tanh(2)
-        fetch_z(UNITS - 1)
-        group_silu(2)
-        scatter_z(UNITS - 1)
-        plus_factor(2, on_gpsimd=True)
-        for c in range(ROW_TILES):
-            dx_product(0, c)
-            dx_product(1, c)
-        fetch_dx(0, 0)
-        minus_factor(2)
-        slope_on_gpsimd(2)
-        only_product(2)
+            if u == 4:
+                first_product(0)
+            if u == 5:
+                second_product(0)
+            if u == 7:
+                quantize_da(0)
+            if u == 13:
+                both_products(1)
+        tanh_of(2, all_planes)
+        silu_of(2, all_planes)
         fetch_dx(0, 1)
-        group_tanh(3)
-        group_silu(3)
-        plus_factor(3, on_gpsimd=False)
-        minus_factor(3)
+        plus_factor(2)
+        minus_factor(2)
+        slope_of(2)
         fetch_dx(0, 2)
-        slope_on_gpsimd(3)
-        interleave_da(2)
-        fetch_dx(0, 3)
-        scatter_dx(0, 0)
-        scatter_dx(0, 1)
-        scatter_dx(0, 2)
-        quantize_da(2)
-        only_product(3)
-        scatter_dx(0, 3)
+        for f in range(1, G):
+            last = ROW_TILES - 1
+            interleave_da(f)
+            fetch_dx(f - 1, last)
+            for c in range(1 if f == 1 else 0, last):
+                scatter_dx(f - 1, c)
+            quantize_da(f)
+            if f + 1 < G:
+                only_product(f + 1)
+            scatter_dx(f - 1, last)
+            if f == 1:
+                tanh_of(3, all_planes)
+                silu_of(3, all_planes)
+            group_product(f)
+            if f == 1:
+                fetch_dx(f, 0)
+                plus_factor(3)
+                fetch_dx(f, 1)
+                minus_factor(3)
+                slope_of(3)
+                fetch_dx(f, 2)
+            else:
+                for c in range(last if f + 1 < G else ROW_TILES):
+                    fetch_dx(f, c)
         for c in range(ROW_TILES):
-            dx_product(2, c)
-        fetch_dx(1, 0, 0, C1)
-        interleave_da(3)
-        scatter_dx(1, 0, 0, C1)
-        quantize_da(3)
-        fetch_dx(1, 1, 0, C1)
-        scatter_dx(1, 1, 0, C1)
-        for c in (0, 2, 3, 1):
-            dx_product(3, c)
-        fetch_dx(1, 0, C1, C1)
-        fetch_dx(1, 1, C1, C1)
-        fetch_dx(1, 2)
-        fetch_dx(1, 3)
-        scatter_dx(1, 0, C1, C1)
-        scatter_dx(1, 1, C1, C1)
-        scatter_dx(1, 2)
-        scatter_dx(1, 3)
+            scatter_dx(G - 1, c)

@@ -31,24 +31,25 @@ TAKES_PLACE_OF = {
     "z_win0_2": "grouped2",
     "tanh0": "wet_s4",
     "half0": "raw1",
-    "tanh1": "wet_s8",
-    "silu1": "silu0",
-    "plus3": "da_c1",
+    "tanh1": "wet_s9",
     "z_sb14": "raw7",
     **{"minus%d" % f: "a%d" % f for f in range(1, G)},
     **{"z_sb%d" % u: "z_sb%d" % (u % 4) for u in range(FIRST_COPY_UNIT)},
     **{"dx%d_%d" % (f, c): "dx%d_%d" % (f % 2, c) for f in range(G) for c in range(ROW_TILES - 1)},
-    "half1": "grouped15",
-    "slope2": "grouped15",
-    "slope3": "grouped15",
+    "half1_0": "grouped15",
+    "half2_0": "raw1",
+    "half3_0": "raw1",
+    "half2_1": "da_bf1",
+    "half3_1": "da_bf2",
     "tanh2": "wet_s4",
-    "tanh3": "plus1",
+    "tanh3": "raw5",
     "silu2": "raw6",
-    "silu3": "raw6",
-    "planes2": "da_bf1",
-    "planes3": "da_bf2",
+    "silu3": "da_c1",
+    "plus2": "plus1",
+    "plus3": "da_s1",
     "dx1_3": "da_bf1",
     "dx2_3": "da_bf2",
+    "planes3": "planes2",
     "out_sb0": "wet_s15",
     "out_sb1": "raw3",
     "out_sb2": "raw4",
@@ -202,21 +203,17 @@ def tile_moe_hib_silu_kernel(
             minus[f] = place([P, PACK, C1], F32, "minus%d" % f)
             nc.scalar.activation(out=minus[f][:], in_=silu_sb[f][:], func=ACT.Identity, bias=minus_one[:])
 
-        def slope_of(f):
-            slope[f] = place([P, PACK, C1], F32, "slope%d" % f)
-            nc.gpsimd.tensor_tensor(slope[f][:], plus[f][:], minus[f][:], ALU.mult)
+        def half_product(f, x):
+            half_sb[f, x] = place([P, 2, C1], F32, "half%d_%d" % (f, x))
+            for s in range(2):
+                t = 2 * x + s
+                nc.gpsimd.tensor_tensor(half_sb[f, x][:, s, :], plus[f][:, t, :], scattered(f, t), ALU.mult)
 
-        def only_product(f):
+        def last_product(f):
             planes[f] = place([P, PACK, C1], BF16, "planes%d" % f)
-            for t in range(PACK):
-                nc.gpsimd.tensor_tensor(planes[f][:, t, :], slope[f][:, t, :], scattered(f, t), ALU.mult)
-
-        def both_products(f):
-            half_sb[f] = place([P, PACK, C1], F32, "half%d" % f)
-            for t in range(PACK):
-                nc.gpsimd.tensor_tensor(half_sb[f][:, t, :], plus[f][:, t, :], scattered(f, t), ALU.mult)
-            planes[f] = place([P, PACK, C1], BF16, "planes%d" % f)
-            nc.gpsimd.tensor_tensor(planes[f][:], minus[f][:], half_sb[f][:], ALU.mult)
+            for x in range(2):
+                ts = slice(2 * x, 2 * x + 2)
+                nc.gpsimd.tensor_tensor(planes[f][:, ts, :], minus[f][:, ts, :], half_sb[f, x][:], ALU.mult)
 
         def interleave_da(f):
             da_bf[f] = place([P, C1, PACK], BF16, "da_bf%d" % f)
@@ -316,14 +313,15 @@ def tile_moe_hib_silu_kernel(
                 silu_of(0, all_planes)
             if u == 6:
                 interleave_da(0)
-            if u in (8, 9):
-                tanh_of(1, low if u == 8 else high)
-            if u in (10, 11):
-                silu_of(1, low if u == 10 else high)
+            if u in (9, 11):
+                tanh_of(1, low if u == 9 else high)
             if u == 13:
                 plus_factor(1)
                 group_product(0)
                 fetch_dx(0, 0)
+                silu_of(1, all_planes)
+                fetch_dx(0, 1)
+                fetch_dx(0, 2)
                 minus_factor(1)
             if u == UNITS - 1:
                 scatter_dx(0, 0)
@@ -340,37 +338,36 @@ def tile_moe_hib_silu_kernel(
             if u == 7:
                 quantize_da(0)
             if u == 13:
-                both_products(1)
-        tanh_of(2, all_planes)
-        silu_of(2, all_planes)
-        fetch_dx(0, 1)
-        plus_factor(2)
-        minus_factor(2)
-        slope_of(2)
-        fetch_dx(0, 2)
+                half_product(1, 0)
+                half_product(1, 1)
+                last_product(1)
+        last = ROW_TILES - 1
         for f in range(1, G):
-            last = ROW_TILES - 1
+            following = f + 1 < G
+            if f == 1:
+                tanh_of(2, all_planes)
+            else:
+                for c in range(last):
+                    fetch_dx(f - 1, c)
+            if following:
+                plus_factor(f + 1)
+                silu_of(f + 1, all_planes)
+                half_product(f + 1, 0)
             interleave_da(f)
             fetch_dx(f - 1, last)
+            if following:
+                minus_factor(f + 1)
+            if f == 1:
+                tanh_of(3, all_planes)
             for c in range(1 if f == 1 else 0, last):
                 scatter_dx(f - 1, c)
             quantize_da(f)
-            if f + 1 < G:
-                only_product(f + 1)
+            if following:
+                half_product(f + 1, 1)
+                last_product(f + 1)
             scatter_dx(f - 1, last)
-            if f == 1:
-                tanh_of(3, all_planes)
-                silu_of(3, all_planes)
             group_product(f)
-            if f == 1:
-                fetch_dx(f, 0)
-                plus_factor(3)
-                fetch_dx(f, 1)
-                minus_factor(3)
-                slope_of(3)
-                fetch_dx(f, 2)
-            else:
-                for c in range(last if f + 1 < G else ROW_TILES):
-                    fetch_dx(f, c)
+        for c in range(ROW_TILES):
+            fetch_dx(G - 1, c)
         for c in range(ROW_TILES):
             scatter_dx(G - 1, c)

@@ -23,39 +23,41 @@ LIST = 16
 QUADRANTS, QUADRANT = 4, 32
 SCALE_ROWS = 4
 UNITS = 2 * E
+BANKS = 8
 FLOPS = 2 * 2 * W * W * T
 
-FIRST_COPY_UNIT = 14
+AHEAD = 2
+RING = 2 * AHEAD
+FIRST_COPY_UNIT = UNITS - 2
+FIRST_PRODUCT_STEP, SECOND_PRODUCT_STEP, INTERLEAVE_STEP, QUANTISE_STEP = 4, 5, 6, 7
+TANH_HALF_STEPS = [9, 11]
+
 TAKES_PLACE_OF = {
+    **{"wet_c%d" % u: "unit%d" % (u % RING) for u in range(UNITS)},
+    **{"grouped%d" % u: "unit%d" % ((u - AHEAD) % RING) for u in range(5, FIRST_COPY_UNIT)},
+    **{"z_sb%d" % u: "z_sb%d" % (u % RING) for u in range(FIRST_COPY_UNIT)},
     "slot_w1": "raw0",
-    "z_win0_2": "grouped2",
-    "tanh0": "wet_s4",
-    "half0": "raw1",
-    "tanh1": "wet_s9",
-    "z_sb14": "raw7",
-    **{"minus%d" % f: "a%d" % f for f in range(1, G)},
-    **{"z_sb%d" % u: "z_sb%d" % (u % 4) for u in range(FIRST_COPY_UNIT)},
-    **{"dx%d_%d" % (f, c): "dx%d_%d" % (f % 2, c) for f in range(G) for c in range(ROW_TILES - 1)},
-    "half1_0": "grouped15",
-    "half2_0": "raw1",
-    "half3_0": "raw1",
-    "half2_1": "da_bf1",
-    "half3_1": "da_bf2",
-    "tanh2": "wet_s4",
-    "tanh3": "raw5",
-    "silu2": "raw6",
-    "silu3": "da_c1",
+    "z_win0_3": "raw1",
+    "z_sb%d" % FIRST_COPY_UNIT: "raw%d" % (E - 1),
+    "tanh0": "wet_s%d" % FIRST_PRODUCT_STEP,
+    "tanh1": "wet_s%d" % TANH_HALF_STEPS[0],
+    "out_sb0": "wet_s%d" % (UNITS - 1),
+    "half1": "grouped%d" % (UNITS - 1),
+    **{"half%d_1" % f: "da_bf%d" % (f - 1) for f in range(2, G)},
+    **{"dx%d_%d" % (f, ROW_TILES - 1): "da_bf%d" % f for f in range(1, G - 1)},
+    "out_sb%d" % (ROW_TILES - 1): "planes1",
+    "tanh2": "wet_s%d" % FIRST_PRODUCT_STEP,
     "plus2": "plus1",
     "plus3": "da_s1",
-    "dx1_3": "da_bf1",
-    "dx2_3": "da_bf2",
-    "planes3": "planes2",
-    "out_sb0": "wet_s15",
+    "silu3": "da_c1",
+    **{"minus%d" % f: "a%d" % f for f in range(1, G)},
+    **{"dx%d_%d" % (f, c): "dx%d_%d" % (f % 2, c) for f in range(G) for c in range(ROW_TILES - 1)},
+    **{name: "raw2" for name in ("half0", "half2_0", "half3_0")},
     "out_sb1": "raw3",
     "out_sb2": "raw4",
-    "out_sb3": "planes1",
-    **{"wet_c%d" % u: "unit%d" % (u % 4) for u in range(UNITS)},
-    **{"grouped%d" % u: "unit%d" % ((u - 2) % 4) for u in range(3, UNITS - 2)},
+    "tanh3": "raw5",
+    "silu2": "raw6",
+    "planes3": "planes2",
 }
 
 
@@ -65,8 +67,7 @@ def tile_moe_hib_silu_kernel(
     nc = tc.nc
     with ExitStack() as ctx:
         held = ctx.enter_context(tc.tile_pool(name="held", bufs=1))
-        ring = ctx.enter_context(tc.tile_pool(name="ring", bufs=3))
-        psum = ctx.enter_context(tc.psum_pool(name="psum", bufs=8))
+        psum = ctx.enter_context(tc.psum_pool(name="psum", bufs=BANKS))
 
         def place(shape, dtype, name):
             return held.tile(shape, dtype, name=name, tag=TAKES_PLACE_OF.get(name, name), align_bytes=64)
@@ -85,7 +86,7 @@ def tile_moe_hib_silu_kernel(
 
         raw, grouped, wet_c, wet_s, slot_w, slot_s, z_sb, z_win = {}, {}, {}, {}, {}, {}, {}, {}
         a_sb, tanh_sb, silu_sb, half_sb, planes, da_bf, da_c, da_s = {}, {}, {}, {}, {}, {}, {}, {}
-        dx_sb, out_sb, z_bank, plus, minus, slope, dx_bank = {}, {}, {}, {}, {}, {}, {}
+        dx_sb, out_sb, z_bank, plus, minus, dx_bank = {}, {}, {}, {}, {}, {}
         one = held.tile([P, 1], F32, name="one")
         nc.vector.memset(one[:], 1.0)
         minus_one = held.tile([P, 1], F32, name="minus_one")
@@ -110,11 +111,12 @@ def tile_moe_hib_silu_kernel(
             a_sb[f] = place([P, PACK, C1], F32, "a%d" % f)
             nc.sync.dma_start(out=a_sb[f][:], in_=a.rearrange("(q t) j -> q t j", t=PACK)[:, :, f * C1 : (f + 1) * C1])
 
-        def round_wet(u, on_vector=False):
+        def round_wet(u, on_vector=False, ms=slice(0, P)):
             e, x = divmod(u, 2)
-            grouped[u] = place([P, 2, P, PACK], BF16, "grouped%d" % u)
-            src = raw[e][:].rearrange("p j (m t) -> p m j t", t=PACK)[:, :, :, 2 * x : 2 * x + 2]
-            to = grouped[u][:].rearrange("p s m j -> p m j s")
+            if ms.start == 0:
+                grouped[u] = place([P, 2, P, PACK], BF16, "grouped%d" % u)
+            src = raw[e][:].rearrange("p j (m t) -> p m j t", t=PACK)[:, ms, :, 2 * x : 2 * x + 2]
+            to = grouped[u][:].rearrange("p s m j -> p m j s")[:, ms]
             if on_vector:
                 nc.vector.tensor_copy(out=to, in_=src)
             else:
@@ -160,10 +162,10 @@ def tile_moe_hib_silu_kernel(
                 both = in_share(gate_sb, u // 2).unsqueeze(1).to_broadcast([P, 2, C2])
                 nc.vector.scalar_tensor_tensor(z_sb[u][:], z_bank[u][:], -0.5, both, ALU.mult, ALU.mult)
 
-        def scatter_z(u):
+        def scatter_z(u, which=range(2)):
             e, x = divmod(u, 2)
             f = e // 2
-            for s in range(2):
+            for s in which:
                 t = 2 * x + s
                 if (f, t) not in z_win:
                     z_win[f, t] = place([P, max(2, f + 1) * C1], F32, "z_win%d_%d" % (f, t))
@@ -215,6 +217,13 @@ def tile_moe_hib_silu_kernel(
                 ts = slice(2 * x, 2 * x + 2)
                 nc.gpsimd.tensor_tensor(planes[f][:, ts, :], minus[f][:, ts, :], half_sb[f, x][:], ALU.mult)
 
+        def whole_products(f):
+            half_sb[f] = place([P, PACK, C1], F32, "half%d" % f)
+            for t in range(PACK):
+                nc.gpsimd.tensor_tensor(half_sb[f][:, t, :], plus[f][:, t, :], scattered(f, t), ALU.mult)
+            planes[f] = place([P, PACK, C1], BF16, "planes%d" % f)
+            nc.gpsimd.tensor_tensor(planes[f][:], minus[f][:], half_sb[f][:], ALU.mult)
+
         def interleave_da(f):
             da_bf[f] = place([P, C1, PACK], BF16, "da_bf%d" % f)
             nc.scalar.copy(
@@ -255,13 +264,12 @@ def tile_moe_hib_silu_kernel(
             if f == G - 1:
                 nc.sync.dma_start(out=out[c * P : (c + 1) * P, :], in_=out_sb[c][:])
 
-
         nc.gpsimd.memset(wgt_s[:].bitcast(I32), 0)
 
         nc.sync.dma_start(dst_sb[:], dst)
         for q in range(QUADRANTS):
             rows_q = dy_scales[0, SCALE_ROWS * q : SCALE_ROWS * (q + 1), :].bitcast(I32)
-            nc.sync.dma_start(
+            (nc.sync, nc.scalar)[q // 2].dma_start(
                 out=dy_s[QUADRANT * q : QUADRANT * (q + 1), :], in_=rows_q.partition_broadcast(QUADRANT // SCALE_ROWS)
             )
         load_wet(0)
@@ -301,21 +309,35 @@ def tile_moe_hib_silu_kernel(
         gather_words(1)
 
         low, high, all_planes = slice(0, 2), slice(2, PACK), slice(0, PACK)
-        for u in range(UNITS):
+        for u in range(2):
+            expert_product(u)
+            fetch_z(u)
+        round_wet(2)
+        round_wet(3)
+        scatter_z(0)
+        scatter_z(1, [0])
+        quantize_wet(2)
+        scatter_z(1, [1])
+        quantize_wet(3)
+
+        for u in range(AHEAD, UNITS):
+            done = P // 2 if u == AHEAD else 0
             if u < FIRST_COPY_UNIT:
                 expert_product(u)
+                if done:
+                    round_wet(u + AHEAD, ms=slice(0, done))
                 fetch_z(u)
-            if u + 2 < UNITS:
-                round_wet(u + 2)
-            if u == 4:
+            if u + AHEAD < UNITS:
+                round_wet(u + AHEAD, ms=slice(done, P))
+            if u == FIRST_PRODUCT_STEP:
                 tanh_of(0, all_planes)
-            if u == 5:
+            if u == SECOND_PRODUCT_STEP:
                 silu_of(0, all_planes)
-            if u == 6:
+            if u == INTERLEAVE_STEP:
                 interleave_da(0)
-            if u in (9, 11):
-                tanh_of(1, low if u == 9 else high)
-            if u == 13:
+            if u in TANH_HALF_STEPS:
+                tanh_of(1, (low, high)[TANH_HALF_STEPS.index(u)])
+            if u == FIRST_COPY_UNIT - 1:
                 plus_factor(1)
                 group_product(0)
                 fetch_dx(0, 0)
@@ -329,18 +351,17 @@ def tile_moe_hib_silu_kernel(
             if FIRST_COPY_UNIT <= u + 1 < UNITS:
                 expert_product(u + 1)
                 fetch_z(u + 1)
-            if u + 2 < UNITS:
-                quantize_wet(u + 2)
-            if u == 4:
+            if u + AHEAD < UNITS:
+                quantize_wet(u + AHEAD)
+            if u == FIRST_PRODUCT_STEP:
                 first_product(0)
-            if u == 5:
+            if u == SECOND_PRODUCT_STEP:
                 second_product(0)
-            if u == 7:
+            if u == QUANTISE_STEP:
                 quantize_da(0)
-            if u == 13:
-                half_product(1, 0)
-                half_product(1, 1)
-                last_product(1)
+            if u == FIRST_COPY_UNIT - 1:
+                whole_products(1)
+
         last = ROW_TILES - 1
         for f in range(1, G):
             following = f + 1 < G

@@ -29,35 +29,39 @@ FLOPS = 2 * 2 * W * W * T
 AHEAD = 2
 RING = 2 * AHEAD
 FIRST_COPY_UNIT = UNITS - 2
-FIRST_PRODUCT_STEP, SECOND_PRODUCT_STEP, INTERLEAVE_STEP, QUANTISE_STEP = 4, 5, 6, 7
-TANH_HALF_STEPS = [9, 11]
+PRODUCT_STEPS, INTERLEAVE_STEP, QUANTISE_STEP = [4, 7], 9, 10
+FIRST_JOINT = 8
+TANH_HALF_STEPS = [11, 13]
 
 TAKES_PLACE_OF = {
     **{"wet_c%d" % u: "unit%d" % (u % RING) for u in range(UNITS)},
-    **{"grouped%d" % u: "unit%d" % ((u - AHEAD) % RING) for u in range(5, FIRST_COPY_UNIT)},
+    **{"grouped%d" % u: "unit%d" % ((u - AHEAD) % RING) for u in range(5, UNITS) if u % 2 or u <= FIRST_JOINT + 2},
+    "grouped%d" % (FIRST_JOINT + 1): "wet_s%d" % (FIRST_JOINT - AHEAD),
+    **{"grouped%d" % u: "grouped%d" % (u % RING) for u in range(FIRST_JOINT + 4, UNITS, 2)},
     **{"z_sb%d" % u: "z_sb%d" % (u % RING) for u in range(FIRST_COPY_UNIT)},
     "slot_w1": "raw0",
     "z_win0_3": "raw1",
-    "z_sb%d" % FIRST_COPY_UNIT: "raw%d" % (E - 1),
-    "tanh0": "wet_s%d" % FIRST_PRODUCT_STEP,
+    **{"tanh0_%d" % x: "wet_s%d" % PRODUCT_STEPS[0] for x in range(2)},
+    **{"silu0_%d" % x: "wet_s%d" % (PRODUCT_STEPS[0] - 1) for x in range(2)},
     "tanh1": "wet_s%d" % TANH_HALF_STEPS[0],
     "out_sb0": "wet_s%d" % (UNITS - 1),
-    "half1": "grouped%d" % (UNITS - 1),
+    "half1": "z_sb%d" % ((FIRST_COPY_UNIT - 1) % RING),
     **{"half%d_1" % f: "da_bf%d" % (f - 1) for f in range(2, G)},
     **{"dx%d_%d" % (f, ROW_TILES - 1): "da_bf%d" % f for f in range(1, G - 1)},
     "out_sb%d" % (ROW_TILES - 1): "planes1",
-    "tanh2": "wet_s%d" % FIRST_PRODUCT_STEP,
+    "tanh2": "wet_s%d" % PRODUCT_STEPS[0],
     "plus2": "plus1",
     "plus3": "da_s1",
     "silu3": "da_c1",
     **{"minus%d" % f: "a%d" % f for f in range(1, G)},
     **{"dx%d_%d" % (f, c): "dx%d_%d" % (f % 2, c) for f in range(G) for c in range(ROW_TILES - 1)},
-    **{name: "raw2" for name in ("half0", "half2_0", "half3_0")},
+    **{name: "raw2" for name in ("half0_0", "half0_2", "half2_0", "half3_0")},
     "out_sb1": "raw3",
     "out_sb2": "raw4",
     "tanh3": "raw5",
     "silu2": "raw6",
     "planes3": "planes2",
+    "half0_3": "half0_1",
 }
 
 
@@ -82,7 +86,10 @@ def tile_moe_hib_silu_kernel(
         wgt_s = held.tile([P, W], U8, name="wgt_s", align_bytes=64)
         wgt_w = held.tile([P, G, W], I32, name="wgt_w", align_bytes=64)
         shares = (slice(0, C1), slice(C1, T))
-        gate_sb = [held.tile([P, s.stop - s.start], F32, name="gate%d" % x, align_bytes=64) for x, s in enumerate(shares)]
+        gate_shares = [slice(f * C1, (f + 1) * C1) for f in range(G)]
+        gate_sb = [
+            held.tile([P, s.stop - s.start], F32, name="gate%d" % x, align_bytes=64) for x, s in enumerate(gate_shares)
+        ]
 
         raw, grouped, wet_c, wet_s, slot_w, slot_s, z_sb, z_win = {}, {}, {}, {}, {}, {}, {}, {}
         a_sb, tanh_sb, silu_sb, half_sb, planes, da_bf, da_c, da_s = {}, {}, {}, {}, {}, {}, {}, {}
@@ -100,19 +107,33 @@ def tile_moe_hib_silu_kernel(
             first = e * C2 - shares[x].start
             return tiles[x][:, first : first + C2]
 
+        def gate_of(first, count):
+            x = first // C1
+            first -= gate_shares[x].start
+            return gate_sb[x][:, first : first + count]
+
+        def expert_and_pair(u):
+            if u < FIRST_JOINT:
+                return divmod(u, 2)
+            return 2 * (u // PACK) + (0, 1, 1, 0)[u % PACK], u % PACK // 2
+
         def load_wet(e):
             raw[e] = place([P, PACK, W], F32, "raw%d" % e)
             nc.sync.dma_start(out=raw[e][:], in_=wet[e].rearrange("(p j) i -> p j i", j=PACK))
 
         def load_gate(x):
-            nc.sync.dma_start(out=gate_sb[x][:], in_=gate[:, shares[x]])
+            nc.sync.dma_start(out=gate_sb[x][:], in_=gate[:, gate_shares[x]])
 
         def load_a(f):
             a_sb[f] = place([P, PACK, C1], F32, "a%d" % f)
             nc.sync.dma_start(out=a_sb[f][:], in_=a.rearrange("(q t) j -> q t j", t=PACK)[:, :, f * C1 : (f + 1) * C1])
 
+        def load_first_a(x):
+            a_sb[0, x] = place([P, 2, C1], F32, "a0_%d" % x)
+            nc.sync.dma_start(out=a_sb[0, x][:], in_=a.rearrange("(q t) j -> q t j", t=PACK)[:, 2 * x : 2 * x + 2, 0:C1])
+
         def round_wet(u, on_vector=False, ms=slice(0, P)):
-            e, x = divmod(u, 2)
+            e, x = expert_and_pair(u)
             if ms.start == 0:
                 grouped[u] = place([P, 2, P, PACK], BF16, "grouped%d" % u)
             src = raw[e][:].rearrange("p j (m t) -> p m j t", t=PACK)[:, ms, :, 2 * x : 2 * x + 2]
@@ -139,12 +160,17 @@ def tile_moe_hib_silu_kernel(
             nc.vector.tensor_copy(slot_w[x][:], dy_w[:].bitcast(U32).indirect(dst_sb[:, entries(shares[x].start, count)]))
 
         def expert_product(u):
-            e = u // 2
-            bank = psum.tile([P, 2, C2], F32, name="bank")
+            e = expert_and_pair(u)[0]
+            if u < FIRST_JOINT:
+                bank = psum.tile([P, 2, C2], F32, name="bank")
+                columns = slice(0, C2)
+            else:
+                bank = z_bank[u - 1] if u % 2 else psum.tile([P, 2, C1], F32, name="bank")
+                columns = slice(e % 2 * C2, (e % 2 + 1) * C2)
             h, first = divmod(e * C2, T // 2)
             for s in range(2):
                 nc.tensor.matmul_mx(
-                    out=bank[:, s, :],
+                    out=bank[:, s, columns],
                     lhsT=wet_c[u][:, s * P : (s + 1) * P].bitcast(FP8X4),
                     lhsT_scale=wet_s[u][:, s * P : (s + 1) * P],
                     rhs=in_share(slot_w, e).bitcast(FP8X4),
@@ -155,14 +181,27 @@ def tile_moe_hib_silu_kernel(
             z_bank[u] = bank
 
         def fetch_z(u):
-            z_sb[u] = place([P, 2, C2], F32, "z_sb%d" % u)
-            if u < FIRST_COPY_UNIT:
+            if u < FIRST_JOINT:
+                z_sb[u] = place([P, 2, C2], F32, "z_sb%d" % u)
                 nc.scalar.activation(out=z_sb[u][:], in_=z_bank[u][:], func=ACT.Copy, scale=-0.5)
+                return
+            z_sb[u] = place([P, C1], F32, "z_sb%d" % u)
+            plane = z_bank[u][:, u % 2, :]
+            if u < FIRST_COPY_UNIT:
+                nc.scalar.activation(out=z_sb[u][:], in_=plane, func=ACT.Copy, scale=-0.5)
             else:
-                both = in_share(gate_sb, u // 2).unsqueeze(1).to_broadcast([P, 2, C2])
-                nc.vector.scalar_tensor_tensor(z_sb[u][:], z_bank[u][:], -0.5, both, ALU.mult, ALU.mult)
+                nc.vector.scalar_tensor_tensor(z_sb[u][:], plane, -0.5, gate_of(u // PACK * C1, C1), ALU.mult, ALU.mult)
 
         def scatter_z(u, which=range(2)):
+            if u >= FIRST_JOINT:
+                f, t = divmod(u, PACK)
+                z_win[f, t] = place([P, (f + 1) * C1], F32, "z_win%d_%d" % (f, t))
+                to = z_win[f, t][:].indirect(offs2_sb[:, entries(f * C1, C1)])
+                if u < FIRST_COPY_UNIT:
+                    nc.vector.tensor_tensor(to, z_sb[u][:], gate_of(f * C1, C1), ALU.mult)
+                else:
+                    nc.vector.tensor_copy(to, z_sb[u][:])
+                return
             e, x = divmod(u, 2)
             f = e // 2
             for s in which:
@@ -170,10 +209,7 @@ def tile_moe_hib_silu_kernel(
                 if (f, t) not in z_win:
                     z_win[f, t] = place([P, max(2, f + 1) * C1], F32, "z_win%d_%d" % (f, t))
                 to = z_win[f, t][:].indirect(offs2_sb[:, entries(e * C2, C2)])
-                if u < FIRST_COPY_UNIT:
-                    nc.vector.tensor_tensor(to, z_sb[u][:, s, :], in_share(gate_sb, e), ALU.mult)
-                else:
-                    nc.vector.tensor_copy(to, z_sb[u][:, s, :])
+                nc.vector.tensor_tensor(to, z_sb[u][:, s, :], gate_of(e * C2, C2), ALU.mult)
 
         def tanh_of(f, ts):
             if ts.start == 0:
@@ -188,14 +224,22 @@ def tile_moe_hib_silu_kernel(
         def scattered(f, t):
             return z_win[f, t][:, f * C1 : (f + 1) * C1]
 
-        def first_product(f):
-            half_sb[f] = place([P, PACK, C1], F32, "half%d" % f)
-            for t in range(PACK):
-                nc.vector.scalar_tensor_tensor(half_sb[f][:, t, :], tanh_sb[f][:, t, :], 1.0, scattered(f, t), ALU.add, ALU.mult)
+        def first_factors(x):
+            tanh_sb[0, x] = place([P, 2, C1], F32, "tanh0_%d" % x)
+            nc.scalar.activation(out=tanh_sb[0, x][:], in_=a_sb[0, x][:], func=ACT.Tanh, scale=0.5, bias=no_bias[:])
+            silu_sb[0, x] = place([P, 2, C1], F32, "silu0_%d" % x)
+            nc.scalar.activation(out=silu_sb[0, x][:], in_=a_sb[0, x][:], func=ACT.Silu, scale=-1.0, bias=no_bias[:])
 
-        def second_product(f):
-            planes[f] = place([P, PACK, C1], BF16, "planes%d" % f)
-            nc.vector.scalar_tensor_tensor(planes[f][:], silu_sb[f][:], 1.0, half_sb[f][:], ALU.subtract, ALU.mult)
+        def first_products(x):
+            if x == 0:
+                planes[0] = place([P, PACK, C1], BF16, "planes0")
+            half = [place([P, C1], F32, "half0_%d" % (2 * x + s)) for s in range(2)]
+            for s in range(2):
+                nc.vector.scalar_tensor_tensor(half[s][:], tanh_sb[0, x][:, s, :], 1.0, scattered(0, 2 * x + s), ALU.add, ALU.mult)
+            for s in range(2):
+                nc.vector.scalar_tensor_tensor(
+                    planes[0][:, 2 * x + s, :], silu_sb[0, x][:, s, :], 1.0, half[s][:], ALU.subtract, ALU.mult
+                )
 
         def plus_factor(f):
             plus[f] = place([P, PACK, C1], F32, "plus%d" % f)
@@ -279,13 +323,16 @@ def tile_moe_hib_silu_kernel(
         load_wet(1)
         load_wet(2)
         load_wet(3)
-        load_a(0)
+        load_first_a(0)
         load_gate(1)
         load_wet(4)
         load_wet(5)
-        load_a(1)
+        load_first_a(1)
+        load_gate(2)
         load_wet(6)
         load_wet(7)
+        load_gate(3)
+        load_a(1)
         for q in range(QUADRANTS):
             nc.sync.dma_start(
                 out=wgt_s[QUADRANT * q : QUADRANT * q + G * SCALE_ROWS, :].bitcast(I32),
@@ -320,47 +367,60 @@ def tile_moe_hib_silu_kernel(
         scatter_z(1, [1])
         quantize_wet(3)
 
-        for u in range(AHEAD, UNITS):
+        for u in range(AHEAD, FIRST_COPY_UNIT):
             done = P // 2 if u == AHEAD else 0
-            if u < FIRST_COPY_UNIT:
+            if u < FIRST_JOINT - 1:
+                coming, extra = [u + AHEAD], []
+            elif u == FIRST_JOINT - 1:
+                coming, extra = [u + AHEAD], [u + AHEAD + 1]
+            else:
+                coming, extra = [v for v in [u + AHEAD + 1] if v < UNITS], []
+            if u < FIRST_JOINT:
                 expert_product(u)
-                if done:
-                    round_wet(u + AHEAD, ms=slice(0, done))
+            elif u % 2 == 0:
+                expert_product(u)
+                expert_product(u + 1)
+            if done:
+                round_wet(u + AHEAD, ms=slice(0, done))
+            if not extra:
                 fetch_z(u)
-            if u + AHEAD < UNITS:
-                round_wet(u + AHEAD, ms=slice(done, P))
-            if u == FIRST_PRODUCT_STEP:
-                tanh_of(0, all_planes)
-            if u == SECOND_PRODUCT_STEP:
-                silu_of(0, all_planes)
+            for v in coming:
+                round_wet(v, ms=slice(done, P))
+            if extra:
+                fetch_z(u)
+            if u in PRODUCT_STEPS:
+                first_factors(PRODUCT_STEPS.index(u))
+            for v in extra:
+                round_wet(v)
             if u == INTERLEAVE_STEP:
                 interleave_da(0)
             if u in TANH_HALF_STEPS:
                 tanh_of(1, (low, high)[TANH_HALF_STEPS.index(u)])
-            if u == FIRST_COPY_UNIT - 1:
-                plus_factor(1)
-                group_product(0)
-                fetch_dx(0, 0)
-                silu_of(1, all_planes)
-                fetch_dx(0, 1)
-                fetch_dx(0, 2)
-                minus_factor(1)
-            if u == UNITS - 1:
-                scatter_dx(0, 0)
             scatter_z(u)
-            if FIRST_COPY_UNIT <= u + 1 < UNITS:
-                expert_product(u + 1)
-                fetch_z(u + 1)
-            if u + AHEAD < UNITS:
-                quantize_wet(u + AHEAD)
-            if u == FIRST_PRODUCT_STEP:
-                first_product(0)
-            if u == SECOND_PRODUCT_STEP:
-                second_product(0)
             if u == QUANTISE_STEP:
                 quantize_da(0)
-            if u == FIRST_COPY_UNIT - 1:
-                whole_products(1)
+            for v in coming:
+                quantize_wet(v)
+            if u in PRODUCT_STEPS:
+                first_products(PRODUCT_STEPS.index(u))
+            for v in extra:
+                quantize_wet(v)
+
+        plus_factor(1)
+        group_product(0)
+        fetch_dx(0, 0)
+        silu_of(1, all_planes)
+        fetch_dx(0, 1)
+        fetch_dx(0, 2)
+        minus_factor(1)
+        whole_products(1)
+        for u in range(FIRST_COPY_UNIT, UNITS):
+            expert_product(u)
+        for u in range(FIRST_COPY_UNIT, UNITS):
+            fetch_z(u)
+        for u in range(FIRST_COPY_UNIT, UNITS):
+            scatter_z(u)
+        scatter_dx(0, 0)
 
         last = ROW_TILES - 1
         for f in range(1, G):

@@ -29,8 +29,8 @@ FLOPS = 2 * 2 * W * W * T
 AHEAD = 2
 RING = 2 * AHEAD
 FIRST_COPY_UNIT = UNITS - 2
-PRODUCT_STEPS, INTERLEAVE_STEP, QUANTISE_STEP = [4, 7], 9, 10
-FIRST_JOINT = 8
+PRODUCT_STEPS, INTERLEAVE_STEP, QUANTISE_STEP = [3, 7], 9, 10
+FIRST_JOINT = 4
 TANH_HALF_STEPS = [11, 13]
 
 TAKES_PLACE_OF = {
@@ -42,7 +42,7 @@ TAKES_PLACE_OF = {
     "slot_w1": "raw0",
     "z_win0_3": "raw1",
     **{"tanh0_%d" % x: "wet_s%d" % PRODUCT_STEPS[0] for x in range(2)},
-    **{"silu0_%d" % x: "wet_s%d" % (PRODUCT_STEPS[0] - 1) for x in range(2)},
+    **{"silu0_%d" % x: "wet_s%d" % (PRODUCT_STEPS[0] - 2) for x in range(2)},
     "tanh1": "wet_s%d" % TANH_HALF_STEPS[0],
     "out_sb0": "wet_s%d" % (UNITS - 1),
     "half1": "z_sb%d" % ((FIRST_COPY_UNIT - 1) % RING),
@@ -55,12 +55,13 @@ TAKES_PLACE_OF = {
     "silu3": "da_c1",
     **{"minus%d" % f: "a%d" % f for f in range(1, G)},
     **{"dx%d_%d" % (f, c): "dx%d_%d" % (f % 2, c) for f in range(G) for c in range(ROW_TILES - 1)},
-    **{name: "raw2" for name in ("half0_0", "half0_2", "half2_0", "half3_0")},
+    **{name: "raw2" for name in ("half2_0", "half3_0")},
     "out_sb1": "raw3",
     "out_sb2": "raw4",
     "tanh3": "raw5",
     "silu2": "raw6",
     "planes3": "planes2",
+    "half0_2": "half0_0",
     "half0_3": "half0_1",
 }
 

@@ -26,6 +26,7 @@ UNITS = 2 * E
 BANKS = 8
 FLOPS = 2 * 2 * W * W * T
 
+SCALE_WINDOW = T + 3 * T // 8
 AHEAD = 2
 RING = 2 * AHEAD
 FIRST_COPY_UNIT = UNITS - 2
@@ -60,7 +61,8 @@ TAKES_PLACE_OF = {
     "out_sb2": "raw4",
     "tanh3": "raw5",
     "silu2": "raw6",
-    "planes3": "planes2",
+    "planes2": "wgt_w1",
+    "planes3": "wgt_w2",
     "half0_2": "half0_0",
     "half0_3": "half0_1",
 }
@@ -81,18 +83,19 @@ def tile_moe_hib_silu_kernel(
         offs2_sb = held.tile([P, T // LIST], U16, name="offs2_sb")
         dst_sb = held.tile([P, T // LIST], U16, name="dst_sb")
         dy_w = held.tile([P, T], I32, name="dy_w", align_bytes=64)
-        dy_s = held.tile([P, T // 4], I32, name="dy_s", align_bytes=64)
+        dy_s = held.tile([P, SCALE_WINDOW // 4], I32, name="dy_s", align_bytes=64)
         zero = held.tile([P, 1], F32, name="zero")
         no_bias = held.tile([P, 1], F32, name="no_bias")
         wgt_s = held.tile([P, W], U8, name="wgt_s", align_bytes=64)
-        wgt_w = held.tile([P, G, W], I32, name="wgt_w", align_bytes=64)
+        wgt_w = [held.tile([P, W], I32, name="wgt_w%d" % f, align_bytes=64) for f in range(G)]
         shares = (slice(0, C1), slice(C1, T))
         gate_shares = [slice(f * C1, (f + 1) * C1) for f in range(G)]
         gate_sb = [
             held.tile([P, s.stop - s.start], F32, name="gate%d" % x, align_bytes=64) for x, s in enumerate(gate_shares)
         ]
 
-        raw, grouped, wet_c, wet_s, slot_w, slot_s, z_sb, z_win = {}, {}, {}, {}, {}, {}, {}, {}
+        slot_s = held.tile([P, T], U8, name="slot_s", align_bytes=64)
+        raw, grouped, wet_c, wet_s, slot_w, z_sb, z_win = {}, {}, {}, {}, {}, {}, {}
         a_sb, tanh_sb, silu_sb, half_sb, planes, da_bf, da_c, da_s = {}, {}, {}, {}, {}, {}, {}, {}
         dx_sb, out_sb, z_bank, plus, minus, dx_bank = {}, {}, {}, {}, {}, {}
         one = held.tile([P, 1], F32, name="one")
@@ -125,6 +128,9 @@ def tile_moe_hib_silu_kernel(
         def load_gate(x):
             nc.sync.dma_start(out=gate_sb[x][:], in_=gate[:, gate_shares[x]])
 
+        def load_wgt(f):
+            nc.sync.dma_start(out=wgt_w[f][:], in_=wgt_words[f, 0].rearrange("p k d -> p (k d)").bitcast(I32))
+
         def load_a(f):
             a_sb[f] = place([P, PACK, C1], F32, "a%d" % f)
             nc.sync.dma_start(out=a_sb[f][:], in_=a.rearrange("(q t) j -> q t j", t=PACK)[:, :, f * C1 : (f + 1) * C1])
@@ -151,9 +157,8 @@ def tile_moe_hib_silu_kernel(
                 out=wet_c[u][:].bitcast(FP8X4), scales=wet_s[u][:], in_=grouped[u][:].rearrange("p s m j -> p (s m j)")
             )
 
-        def gather_scales(h):
-            slot_s[h] = place([P, T // 2], U8, "slot_s%d" % h)
-            nc.vector.tensor_copy(slot_s[h][:], dy_s[:].bitcast(U8).indirect(dst_sb[:, entries(h * T // 2, T // 2)]))
+        def gather_scales():
+            nc.vector.tensor_copy(slot_s[:], dy_s[:].bitcast(U8).indirect(dst_sb[:]))
 
         def gather_words(x):
             count = shares[x].stop - shares[x].start
@@ -168,14 +173,13 @@ def tile_moe_hib_silu_kernel(
             else:
                 bank = z_bank[u - 1] if u % 2 else psum.tile([P, 2, C1], F32, name="bank")
                 columns = slice(e % 2 * C2, (e % 2 + 1) * C2)
-            h, first = divmod(e * C2, T // 2)
             for s in range(2):
                 nc.tensor.matmul_mx(
                     out=bank[:, s, columns],
                     lhsT=wet_c[u][:, s * P : (s + 1) * P].bitcast(FP8X4),
                     lhsT_scale=wet_s[u][:, s * P : (s + 1) * P],
                     rhs=in_share(slot_w, e).bitcast(FP8X4),
-                    rhs_scale=slot_s[h][:, first : first + C2],
+                    rhs_scale=slot_s[:, e * C2 : (e + 1) * C2],
                     start=True,
                     stop=True,
                 )
@@ -284,23 +288,27 @@ def tile_moe_hib_silu_kernel(
             )
 
         def group_product(f):
-            for b in range(2):
-                dx_bank[f, b] = psum.tile([P, 2, C1], F32, name="bank")
-                for s in range(2):
-                    ks = slice((2 * b + s) * P, (2 * b + s + 1) * P)
-                    nc.tensor.matmul_mx(
-                        out=dx_bank[f, b][:, s, :],
-                        lhsT=wgt_w[:, f, ks].bitcast(FP8X4),
-                        lhsT_scale=wgt_s[SCALE_ROWS * f : P, ks],
-                        rhs=da_c[f][:].bitcast(FP8X4),
-                        rhs_scale=da_s[f][:],
-                        start=True,
-                        stop=True,
-                    )
+            for c in range(ROW_TILES):
+                if f > 0:
+                    dx_bank[f, c] = psum.tile([P, C1], F32, name="bank")[:]
+                else:
+                    if c % 2 == 0:
+                        both = psum.tile([P, 2, C1], F32, name="bank")
+                    dx_bank[f, c] = both[:, c % 2, :]
+                ks = slice(c * P, (c + 1) * P)
+                nc.tensor.matmul_mx(
+                    out=dx_bank[f, c],
+                    lhsT=wgt_w[f][:, ks].bitcast(FP8X4),
+                    lhsT_scale=wgt_s[SCALE_ROWS * f : P, ks],
+                    rhs=da_c[f][:].bitcast(FP8X4),
+                    rhs_scale=da_s[f][:],
+                    start=True,
+                    stop=True,
+                )
 
         def fetch_dx(f, c):
             dx_sb[f, c] = place([P, C1], F32, "dx%d_%d" % (f, c))
-            nc.scalar.copy(out=dx_sb[f, c][:], in_=dx_bank[f, c // 2][:, c % 2, :])
+            nc.scalar.copy(out=dx_sb[f, c][:], in_=dx_bank[f, c])
 
         def scatter_dx(f, c):
             if f == 0:
@@ -315,7 +323,7 @@ def tile_moe_hib_silu_kernel(
         for q in range(QUADRANTS):
             rows_q = dy_scales[0, SCALE_ROWS * q : SCALE_ROWS * (q + 1), :].bitcast(I32)
             (nc.sync, nc.scalar)[q // 2].dma_start(
-                out=dy_s[QUADRANT * q : QUADRANT * (q + 1), :], in_=rows_q.partition_broadcast(QUADRANT // SCALE_ROWS)
+                out=dy_s[QUADRANT * q : QUADRANT * (q + 1), 0 : T // 4], in_=rows_q.partition_broadcast(QUADRANT // SCALE_ROWS)
             )
         load_wet(0)
         nc.sync.dma_start(out=dy_w[:], in_=dy_words[0].rearrange("p t d -> p (t d)").bitcast(I32))
@@ -339,16 +347,19 @@ def tile_moe_hib_silu_kernel(
                 out=wgt_s[QUADRANT * q : QUADRANT * q + G * SCALE_ROWS, :].bitcast(I32),
                 in_=wgt_scales[:, 0, SCALE_ROWS * q : SCALE_ROWS * (q + 1), :].bitcast(I32),
             )
-        nc.sync.dma_start(out=wgt_w[:], in_=wgt_words[:, 0].rearrange("f p k d -> p f (k d)").bitcast(I32))
+        load_wgt(0)
         nc.sync.dma_start(offs_sb[:], offs)
         load_a(2)
+        load_wgt(1)
         load_a(3)
+        load_wgt(2)
+        load_wgt(3)
 
         nc.vector.memset(zero[:], 0.0)
         nc.scalar.activation(out=no_bias[:], in_=zero[:], func=ACT.Silu)
 
-        for h in range(2):
-            gather_scales(h)
+        nc.vector.memset(dy_s[:, T // 4 :], 0)
+        gather_scales()
         round_wet(0, on_vector=True)
         round_wet(1)
         gather_words(0)
@@ -432,13 +443,18 @@ def tile_moe_hib_silu_kernel(
                 for c in range(last):
                     fetch_dx(f - 1, c)
             if following:
+                if f == 1:
+                    silu_of(2, all_planes)
                 plus_factor(f + 1)
-                silu_of(f + 1, all_planes)
+                if f == 2:
+                    silu_of(3, all_planes)
                 half_product(f + 1, 0)
+            if f == 1:
+                minus_factor(2)
             interleave_da(f)
             fetch_dx(f - 1, last)
-            if following:
-                minus_factor(f + 1)
+            if f == 2:
+                minus_factor(3)
             if f == 1:
                 tanh_of(3, all_planes)
             for c in range(1 if f == 1 else 0, last):

@@ -27,6 +27,7 @@ BANKS = 8
 FLOPS = 2 * 2 * W * W * T
 
 SCALE_WINDOW = T + 3 * T // 8
+HALVED = (1, 2)
 AHEAD = 2
 RING = 2 * AHEAD
 FIRST_COPY_UNIT = UNITS - 2
@@ -36,17 +37,19 @@ TANH_HALF_STEPS = [11, 13]
 
 TAKES_PLACE_OF = {
     **{"wet_c%d" % u: "unit%d" % (u % RING) for u in range(UNITS)},
-    **{"grouped%d" % u: "unit%d" % ((u - AHEAD) % RING) for u in range(5, UNITS) if u % 2 or u <= FIRST_JOINT + 2},
-    "grouped%d" % (FIRST_JOINT + 1): "wet_s%d" % (FIRST_JOINT - AHEAD),
+    **{"grouped%d" % u: "unit%d" % ((u - AHEAD) % RING) for u in range(9, UNITS, 2)},
+    "grouped7": "wet_s4",
     **{"grouped%d" % u: "grouped%d" % (u % RING) for u in range(FIRST_JOINT + 4, UNITS, 2)},
-    **{"z_sb%d" % u: "z_sb%d" % (u % RING) for u in range(FIRST_COPY_UNIT)},
+    **{"z_sb%d" % u: "z_ring%d" % (u % RING) for u in range(FIRST_COPY_UNIT)},
     "slot_w1": "raw0",
-    "z_win0_3": "raw1",
+    "z_win0_3": "raw1_1",
+    "z_sb1": "raw1_0",
+    "z_sb3": "raw2_0",
     **{"tanh0_%d" % x: "wet_s%d" % PRODUCT_STEPS[0] for x in range(2)},
     **{"silu0_%d" % x: "wet_s%d" % (PRODUCT_STEPS[0] - 2) for x in range(2)},
     "tanh1": "wet_s%d" % TANH_HALF_STEPS[0],
     "out_sb0": "wet_s%d" % (UNITS - 1),
-    "half1": "z_sb%d" % ((FIRST_COPY_UNIT - 1) % RING),
+    "half1": "z_ring%d" % ((FIRST_COPY_UNIT - 1) % RING),
     **{"half%d_1" % f: "da_bf%d" % (f - 1) for f in range(2, G)},
     **{"dx%d_%d" % (f, ROW_TILES - 1): "da_bf%d" % f for f in range(1, G - 1)},
     "out_sb%d" % (ROW_TILES - 1): "planes1",
@@ -56,7 +59,7 @@ TAKES_PLACE_OF = {
     "silu3": "da_c1",
     **{"minus%d" % f: "a%d" % f for f in range(1, G)},
     **{"dx%d_%d" % (f, c): "dx%d_%d" % (f % 2, c) for f in range(G) for c in range(ROW_TILES - 1)},
-    **{name: "raw2" for name in ("half2_0", "half3_0")},
+    **{name: "raw2_1" for name in ("half2_0", "half3_0")},
     "out_sb1": "raw3",
     "out_sb2": "raw4",
     "tanh3": "raw5",
@@ -117,13 +120,18 @@ def tile_moe_hib_silu_kernel(
             return gate_sb[x][:, first : first + count]
 
         def expert_and_pair(u):
-            if u < FIRST_JOINT:
+            if u < 2 * FIRST_JOINT:
                 return divmod(u, 2)
             return 2 * (u // PACK) + (0, 1, 1, 0)[u % PACK], u % PACK // 2
 
         def load_wet(e):
             raw[e] = place([P, PACK, W], F32, "raw%d" % e)
             nc.sync.dma_start(out=raw[e][:], in_=wet[e].rearrange("(p j) i -> p j i", j=PACK))
+
+        def load_half_wet(e, h):
+            raw[e, h] = place([P, PACK, W // 2], F32, "raw%d_%d" % (e, h))
+            columns = slice(h * W // 2, (h + 1) * W // 2)
+            nc.sync.dma_start(out=raw[e, h][:], in_=wet[e].rearrange("(p j) i -> p j i", j=PACK)[:, :, columns])
 
         def load_gate(x):
             nc.sync.dma_start(out=gate_sb[x][:], in_=gate[:, gate_shares[x]])
@@ -143,8 +151,14 @@ def tile_moe_hib_silu_kernel(
             e, x = expert_and_pair(u)
             if ms.start == 0:
                 grouped[u] = place([P, 2, P, PACK], BF16, "grouped%d" % u)
-            src = raw[e][:].rearrange("p j (m t) -> p m j t", t=PACK)[:, ms, :, 2 * x : 2 * x + 2]
             to = grouped[u][:].rearrange("p s m j -> p m j s")[:, ms]
+            if e in HALVED:
+                for h in range(ms.start // (P // 2), ms.stop // (P // 2)):
+                    src = raw[e, h][:].rearrange("p j (m t) -> p m j t", t=PACK)[:, :, :, 2 * x : 2 * x + 2]
+                    first = h * P // 2 - ms.start
+                    nc.scalar.copy(out=to[:, first : first + P // 2], in_=src)
+                return
+            src = raw[e][:].rearrange("p j (m t) -> p m j t", t=PACK)[:, ms, :, 2 * x : 2 * x + 2]
             if on_vector:
                 nc.vector.tensor_copy(out=to, in_=src)
             else:
@@ -166,16 +180,19 @@ def tile_moe_hib_silu_kernel(
             nc.vector.tensor_copy(slot_w[x][:], dy_w[:].bitcast(U32).indirect(dst_sb[:, entries(shares[x].start, count)]))
 
         def expert_product(u):
-            e = expert_and_pair(u)[0]
+            e, x = expert_and_pair(u)
             if u < FIRST_JOINT:
-                bank = psum.tile([P, 2, C2], F32, name="bank")
-                columns = slice(0, C2)
+                z_bank[u] = psum.tile([P, 2, C2], F32, name="bank")
+                outs = [z_bank[u][:, s, :] for s in range(2)]
             else:
-                bank = z_bank[u - 1] if u % 2 else psum.tile([P, 2, C1], F32, name="bank")
-                columns = slice(e % 2 * C2, (e % 2 + 1) * C2)
+                steps = [e // 2 * PACK + 2 * x + s for s in range(2)]
+                for step in steps:
+                    if step not in z_bank:
+                        z_bank[step] = psum.tile([P, C1], F32, name="bank")
+                outs = [z_bank[step][:, e % 2 * C2 : (e % 2 + 1) * C2] for step in steps]
             for s in range(2):
                 nc.tensor.matmul_mx(
-                    out=bank[:, s, columns],
+                    out=outs[s],
                     lhsT=wet_c[u][:, s * P : (s + 1) * P].bitcast(FP8X4),
                     lhsT_scale=wet_s[u][:, s * P : (s + 1) * P],
                     rhs=in_share(slot_w, e).bitcast(FP8X4),
@@ -183,7 +200,6 @@ def tile_moe_hib_silu_kernel(
                     start=True,
                     stop=True,
                 )
-            z_bank[u] = bank
 
         def fetch_z(u):
             if u < FIRST_JOINT:
@@ -191,7 +207,7 @@ def tile_moe_hib_silu_kernel(
                 nc.scalar.activation(out=z_sb[u][:], in_=z_bank[u][:], func=ACT.Copy, scale=-0.5)
                 return
             z_sb[u] = place([P, C1], F32, "z_sb%d" % u)
-            plane = z_bank[u][:, u % 2, :]
+            plane = z_bank[u][:]
             if u < FIRST_COPY_UNIT:
                 nc.scalar.activation(out=z_sb[u][:], in_=plane, func=ACT.Copy, scale=-0.5)
             else:
@@ -329,8 +345,10 @@ def tile_moe_hib_silu_kernel(
         nc.sync.dma_start(out=dy_w[:], in_=dy_words[0].rearrange("p t d -> p (t d)").bitcast(I32))
         nc.sync.dma_start(offs2_sb[:], offs2)
         load_gate(0)
-        load_wet(1)
-        load_wet(2)
+        load_half_wet(1, 0)
+        load_half_wet(1, 1)
+        load_half_wet(2, 0)
+        load_half_wet(2, 1)
         load_wet(3)
         load_first_a(0)
         load_gate(1)
@@ -368,42 +386,48 @@ def tile_moe_hib_silu_kernel(
         gather_words(1)
 
         low, high, all_planes = slice(0, 2), slice(2, PACK), slice(0, PACK)
-        for u in range(2):
-            expert_product(u)
-            fetch_z(u)
+        expert_product(0)
+        fetch_z(0)
         round_wet(2)
-        round_wet(3)
+        round_wet(3, ms=slice(0, P // 2))
+        expert_product(1)
+        fetch_z(1)
+        round_wet(3, ms=slice(P // 2, P))
         scatter_z(0)
-        scatter_z(1, [0])
         quantize_wet(2)
+        scatter_z(1, [0])
         scatter_z(1, [1])
         quantize_wet(3)
 
-        for u in range(AHEAD, FIRST_COPY_UNIT):
-            done = P // 2 if u == AHEAD else 0
-            if u < FIRST_JOINT - 1:
-                coming, extra = [u + AHEAD], []
-            elif u == FIRST_JOINT - 1:
-                coming, extra = [u + AHEAD], [u + AHEAD + 1]
-            else:
-                coming, extra = [v for v in [u + AHEAD + 1] if v < UNITS], []
-            if u < FIRST_JOINT:
-                expert_product(u)
-            elif u % 2 == 0:
-                expert_product(u)
-                expert_product(u + 1)
-            if done:
-                round_wet(u + AHEAD, ms=slice(0, done))
-            if not extra:
-                fetch_z(u)
-            for v in coming:
-                round_wet(v, ms=slice(done, P))
-            if extra:
-                fetch_z(u)
-            if u in PRODUCT_STEPS:
-                first_factors(PRODUCT_STEPS.index(u))
-            for v in extra:
-                round_wet(v)
+        early, late = slice(0, P // 2), slice(P // 2, P)
+        expert_product(2)
+        round_wet(4, ms=early)
+        fetch_z(2)
+        round_wet(5, ms=early)
+        round_wet(4, ms=late)
+        scatter_z(2)
+        quantize_wet(4)
+        expert_product(3)
+        fetch_z(3)
+        round_wet(5, ms=late)
+        round_wet(6)
+        first_factors(0)
+        round_wet(7, ms=early)
+        scatter_z(3)
+        quantize_wet(5)
+        quantize_wet(6)
+        first_products(0)
+        for u in range(FIRST_JOINT, FIRST_COPY_UNIT):
+            coming = u + AHEAD + 1
+            if u % 2 == 0:
+                pair = (4 + u // 2 % 2, 6 + u // 2 % 2) if u < 2 * FIRST_JOINT else (u, u + 1)
+                for v in pair:
+                    expert_product(v)
+            fetch_z(u)
+            if coming < UNITS:
+                round_wet(coming, ms=late if u == FIRST_JOINT else slice(0, P))
+            if u == PRODUCT_STEPS[1]:
+                first_factors(1)
             if u == INTERLEAVE_STEP:
                 interleave_da(0)
             if u in TANH_HALF_STEPS:
@@ -411,12 +435,10 @@ def tile_moe_hib_silu_kernel(
             scatter_z(u)
             if u == QUANTISE_STEP:
                 quantize_da(0)
-            for v in coming:
-                quantize_wet(v)
-            if u in PRODUCT_STEPS:
-                first_products(PRODUCT_STEPS.index(u))
-            for v in extra:
-                quantize_wet(v)
+            if coming < UNITS:
+                quantize_wet(coming)
+            if u == PRODUCT_STEPS[1]:
+                first_products(1)
 
         plus_factor(1)
         group_product(0)

@@ -27,7 +27,7 @@ BANKS = 8
 FLOPS = 2 * 2 * W * W * T
 
 SCALE_WINDOW = T + 3 * T // 8
-HALVED = (1, 2)
+HALVED = (0, 1, 2)
 AHEAD = 2
 RING = 2 * AHEAD
 FIRST_COPY_UNIT = UNITS - 2
@@ -38,10 +38,10 @@ TANH_HALF_STEPS = [11, 13]
 TAKES_PLACE_OF = {
     **{"wet_c%d" % u: "unit%d" % (u % RING) for u in range(UNITS)},
     **{"grouped%d" % u: "unit%d" % ((u - AHEAD) % RING) for u in range(9, UNITS, 2)},
-    "grouped7": "wet_s4",
+    "grouped7": "wet_s6",
     **{"grouped%d" % u: "grouped%d" % (u % RING) for u in range(FIRST_JOINT + 4, UNITS, 2)},
     **{"z_sb%d" % u: "z_ring%d" % (u % RING) for u in range(FIRST_COPY_UNIT)},
-    "slot_w1": "raw0",
+    "slot_w1": "raw0_1",
     "z_win0_3": "raw1_1",
     "z_sb1": "raw1_0",
     "z_sb3": "raw2_0",
@@ -91,7 +91,7 @@ def tile_moe_hib_silu_kernel(
         no_bias = held.tile([P, 1], F32, name="no_bias")
         wgt_s = held.tile([P, W], U8, name="wgt_s", align_bytes=64)
         wgt_w = [held.tile([P, W], I32, name="wgt_w%d" % f, align_bytes=64) for f in range(G)]
-        shares = (slice(0, C1), slice(C1, T))
+        shares = (slice(0, T // 2), slice(T // 2, T))
         gate_shares = [slice(f * C1, (f + 1) * C1) for f in range(G)]
         gate_sb = [
             held.tile([P, s.stop - s.start], F32, name="gate%d" % x, align_bytes=64) for x, s in enumerate(gate_shares)
@@ -110,7 +110,7 @@ def tile_moe_hib_silu_kernel(
             return slice(first // LIST, (first + count) // LIST)
 
         def in_share(tiles, e):
-            x = 0 if e * C2 < C1 else 1
+            x = 0 if e * C2 < T // 2 else 1
             first = e * C2 - shares[x].start
             return tiles[x][:, first : first + C2]
 
@@ -156,13 +156,13 @@ def tile_moe_hib_silu_kernel(
                 for h in range(ms.start // (P // 2), ms.stop // (P // 2)):
                     src = raw[e, h][:].rearrange("p j (m t) -> p m j t", t=PACK)[:, :, :, 2 * x : 2 * x + 2]
                     first = h * P // 2 - ms.start
-                    nc.scalar.copy(out=to[:, first : first + P // 2], in_=src)
+                    if on_vector:
+                        nc.vector.tensor_copy(out=to[:, first : first + P // 2], in_=src)
+                    else:
+                        nc.scalar.copy(out=to[:, first : first + P // 2], in_=src)
                 return
             src = raw[e][:].rearrange("p j (m t) -> p m j t", t=PACK)[:, ms, :, 2 * x : 2 * x + 2]
-            if on_vector:
-                nc.vector.tensor_copy(out=to, in_=src)
-            else:
-                nc.scalar.copy(out=to, in_=src)
+            nc.scalar.copy(out=to, in_=src)
 
         def quantize_wet(u):
             wet_c[u] = place([P, 2 * P], U32, "wet_c%d" % u)
@@ -341,8 +341,9 @@ def tile_moe_hib_silu_kernel(
             (nc.sync, nc.scalar)[q // 2].dma_start(
                 out=dy_s[QUADRANT * q : QUADRANT * (q + 1), 0 : T // 4], in_=rows_q.partition_broadcast(QUADRANT // SCALE_ROWS)
             )
-        load_wet(0)
+        load_half_wet(0, 0)
         nc.sync.dma_start(out=dy_w[:], in_=dy_words[0].rearrange("p t d -> p (t d)").bitcast(I32))
+        load_half_wet(0, 1)
         nc.sync.dma_start(offs2_sb[:], offs2)
         load_gate(0)
         load_half_wet(1, 0)
@@ -378,9 +379,10 @@ def tile_moe_hib_silu_kernel(
 
         nc.vector.memset(dy_s[:, T // 4 :], 0)
         gather_scales()
-        round_wet(0, on_vector=True)
+        round_wet(0, ms=slice(0, P // 2))
         round_wet(1)
         gather_words(0)
+        round_wet(0, on_vector=True, ms=slice(P // 2, P))
         quantize_wet(0)
         quantize_wet(1)
         gather_words(1)
@@ -412,7 +414,6 @@ def tile_moe_hib_silu_kernel(
         round_wet(5, ms=late)
         round_wet(6)
         first_factors(0)
-        round_wet(7, ms=early)
         scatter_z(3)
         quantize_wet(5)
         quantize_wet(6)
@@ -425,7 +426,7 @@ def tile_moe_hib_silu_kernel(
                     expert_product(v)
             fetch_z(u)
             if coming < UNITS:
-                round_wet(coming, ms=late if u == FIRST_JOINT else slice(0, P))
+                round_wet(coming)
             if u == PRODUCT_STEPS[1]:
                 first_factors(1)
             if u == INTERLEAVE_STEP:

@@ -22,52 +22,22 @@ ROW_TILES = W // P
 LIST = 16
 QUADRANTS, QUADRANT = 4, 32
 SCALE_ROWS = 4
-UNITS = 2 * E
 BANKS = 8
 FLOPS = 2 * 2 * W * W * T
 
-SCALE_WINDOW = T + 3 * T // 8
-HALVED = (0, 1, 2)
-AHEAD = 2
-RING = 2 * AHEAD
-FIRST_COPY_UNIT = UNITS - 2
-PRODUCT_STEPS, INTERLEAVE_STEP, QUANTISE_STEP = [3, 7], 9, 10
-FIRST_JOINT = 4
-TANH_HALF_STEPS = [11, 13]
+BY_EXPERT = 2
 
 TAKES_PLACE_OF = {
-    **{"wet_c%d" % u: "unit%d" % (u % RING) for u in range(UNITS)},
-    **{"grouped%d" % u: "unit%d" % ((u - AHEAD) % RING) for u in range(9, UNITS, 2)},
-    "grouped7": "wet_s6",
-    **{"grouped%d" % u: "grouped%d" % (u % RING) for u in range(FIRST_JOINT + 4, UNITS, 2)},
-    **{"z_sb%d" % u: "z_ring%d" % (u % RING) for u in range(FIRST_COPY_UNIT)},
-    "slot_w1": "raw0_1",
-    "z_win0_3": "raw1_1",
-    "z_sb1": "raw1_0",
-    "z_sb3": "raw2_0",
-    **{"tanh0_%d" % x: "wet_s%d" % PRODUCT_STEPS[0] for x in range(2)},
-    **{"silu0_%d" % x: "wet_s%d" % (PRODUCT_STEPS[0] - 2) for x in range(2)},
-    "tanh1": "wet_s%d" % TANH_HALF_STEPS[0],
-    "out_sb0": "wet_s%d" % (UNITS - 1),
-    "half1": "z_ring%d" % ((FIRST_COPY_UNIT - 1) % RING),
-    **{"half%d_1" % f: "da_bf%d" % (f - 1) for f in range(2, G)},
-    **{"dx%d_%d" % (f, ROW_TILES - 1): "da_bf%d" % f for f in range(1, G - 1)},
-    "out_sb%d" % (ROW_TILES - 1): "planes1",
-    "tanh2": "wet_s%d" % PRODUCT_STEPS[0],
-    "plus2": "plus1",
-    "plus3": "da_s1",
-    "silu3": "da_c1",
-    **{"minus%d" % f: "a%d" % f for f in range(1, G)},
-    **{"dx%d_%d" % (f, c): "dx%d_%d" % (f % 2, c) for f in range(G) for c in range(ROW_TILES - 1)},
-    **{name: "raw2_1" for name in ("half2_0", "half3_0")},
-    "out_sb1": "raw3",
-    "out_sb2": "raw4",
-    "tanh3": "raw5",
-    "silu2": "raw6",
-    "planes2": "wgt_w1",
-    "planes3": "wgt_w2",
-    "half0_2": "half0_0",
-    "half0_3": "half0_1",
+    **{"grouped%d" % e: "grouped%d" % (e % 2) for e in range(E)},
+    **{"wet_c%d" % e: "wet_c%d" % (e % 2) for e in range(E)},
+    **{"wet_s%d" % e: "wet_s%d" % (e % 2) for e in range(E)},
+    **{"z_win%d_%d" % (f, t): "z_win%d_%d" % (f % 2, t) for f in range(G) for t in range(PACK)},
+    **{"%s%d_%d" % (name, f, x): "%s1_%d" % (name, x) for name in ("tanh", "silu") for f in range(1, G) for x in range(2)},
+    **{"half%d_%d" % (f, x): "half1_%d" % x for f in range(1, G) for x in range(2)},
+    "half0_0": "raw3",
+    **{"planes%d" % f: "planes0" for f in range(G)},
+    **{"da_bf%d" % f: "da_bf0" for f in range(G)},
+    **{"dx%d_%d" % (f, b): "dx%d_%d" % (f % 2, b) for f in range(G) for b in range(2)},
 }
 
 
@@ -86,43 +56,18 @@ def tile_moe_hib_silu_kernel(
         offs2_sb = held.tile([P, T // LIST], U16, name="offs2_sb")
         dst_sb = held.tile([P, T // LIST], U16, name="dst_sb")
         dy_w = held.tile([P, T], I32, name="dy_w", align_bytes=64)
-        dy_s = held.tile([P, SCALE_WINDOW // 4], I32, name="dy_s", align_bytes=64)
+        dy_s = held.tile([P, T // 4], I32, name="dy_s", align_bytes=64)
         zero = held.tile([P, 1], F32, name="zero")
         no_bias = held.tile([P, 1], F32, name="no_bias")
         wgt_s = held.tile([P, W], U8, name="wgt_s", align_bytes=64)
         wgt_w = [held.tile([P, W], I32, name="wgt_w%d" % f, align_bytes=64) for f in range(G)]
-        shares = (slice(0, T // 2), slice(T // 2, T))
-        gate_shares = [slice(f * C1, (f + 1) * C1) for f in range(G)]
-        gate_sb = [
-            held.tile([P, s.stop - s.start], F32, name="gate%d" % x, align_bytes=64) for x, s in enumerate(gate_shares)
-        ]
-
-        slot_s = held.tile([P, T], U8, name="slot_s", align_bytes=64)
-        raw, grouped, wet_c, wet_s, slot_w, z_sb, z_win = {}, {}, {}, {}, {}, {}, {}
+        gate_sb = [held.tile([P, C1], F32, name="gate%d" % f, align_bytes=64) for f in range(G)]
+        raw, grouped, wet_c, wet_s, slot_w, slot_s, z_sb, z_win, z_bank = {}, {}, {}, {}, {}, {}, {}, {}, {}
         a_sb, tanh_sb, silu_sb, half_sb, planes, da_bf, da_c, da_s = {}, {}, {}, {}, {}, {}, {}, {}
-        dx_sb, out_sb, z_bank, plus, minus, dx_bank = {}, {}, {}, {}, {}, {}
-        one = held.tile([P, 1], F32, name="one")
-        nc.vector.memset(one[:], 1.0)
-        minus_one = held.tile([P, 1], F32, name="minus_one")
-        nc.vector.memset(minus_one[:], -1.0)
+        dx_sb, out_sb, dx_bank = {}, {}, {}
 
         def entries(first, count):
             return slice(first // LIST, (first + count) // LIST)
-
-        def in_share(tiles, e):
-            x = 0 if e * C2 < T // 2 else 1
-            first = e * C2 - shares[x].start
-            return tiles[x][:, first : first + C2]
-
-        def gate_of(first, count):
-            x = first // C1
-            first -= gate_shares[x].start
-            return gate_sb[x][:, first : first + count]
-
-        def expert_and_pair(u):
-            if u < 2 * FIRST_JOINT:
-                return divmod(u, 2)
-            return 2 * (u // PACK) + (0, 1, 1, 0)[u % PACK], u % PACK // 2
 
         def load_wet(e):
             raw[e] = place([P, PACK, W], F32, "raw%d" % e)
@@ -133,8 +78,8 @@ def tile_moe_hib_silu_kernel(
             columns = slice(h * W // 2, (h + 1) * W // 2)
             nc.sync.dma_start(out=raw[e, h][:], in_=wet[e].rearrange("(p j) i -> p j i", j=PACK)[:, :, columns])
 
-        def load_gate(x):
-            nc.sync.dma_start(out=gate_sb[x][:], in_=gate[:, gate_shares[x]])
+        def load_gate(f):
+            nc.sync.dma_start(out=gate_sb[f][:], in_=gate[:, f * C1 : (f + 1) * C1])
 
         def load_wgt(f):
             nc.sync.dma_start(out=wgt_w[f][:], in_=wgt_words[f, 0].rearrange("p k d -> p (k d)").bitcast(I32))
@@ -143,155 +88,107 @@ def tile_moe_hib_silu_kernel(
             a_sb[f] = place([P, PACK, C1], F32, "a%d" % f)
             nc.sync.dma_start(out=a_sb[f][:], in_=a.rearrange("(q t) j -> q t j", t=PACK)[:, :, f * C1 : (f + 1) * C1])
 
-        def load_first_a(x):
-            a_sb[0, x] = place([P, 2, C1], F32, "a0_%d" % x)
-            nc.sync.dma_start(out=a_sb[0, x][:], in_=a.rearrange("(q t) j -> q t j", t=PACK)[:, 2 * x : 2 * x + 2, 0:C1])
+        def copy_on(engine, to, src):
+            if engine == "vector":
+                nc.vector.tensor_copy(out=to, in_=src)
+            else:
+                nc.scalar.copy(out=to, in_=src)
 
-        def round_wet(u, on_vector=False, ms=slice(0, P)):
-            e, x = expert_and_pair(u)
-            if ms.start == 0:
-                grouped[u] = place([P, 2, P, PACK], BF16, "grouped%d" % u)
-            to = grouped[u][:].rearrange("p s m j -> p m j s")[:, ms]
-            if e in HALVED:
-                for h in range(ms.start // (P // 2), ms.stop // (P // 2)):
-                    src = raw[e, h][:].rearrange("p j (m t) -> p m j t", t=PACK)[:, :, :, 2 * x : 2 * x + 2]
-                    first = h * P // 2 - ms.start
-                    if on_vector:
-                        nc.vector.tensor_copy(out=to[:, first : first + P // 2], in_=src)
-                    else:
-                        nc.scalar.copy(out=to[:, first : first + P // 2], in_=src)
-                return
-            src = raw[e][:].rearrange("p j (m t) -> p m j t", t=PACK)[:, ms, :, 2 * x : 2 * x + 2]
-            nc.scalar.copy(out=to, in_=src)
+        def scatter_on(engine, to, src):
+            if engine == "vector":
+                nc.vector.tensor_copy(to, src)
+            else:
+                nc.scalar.activation(out=to, in_=src, func=ACT.Copy)
 
-        def quantize_wet(u):
-            wet_c[u] = place([P, 2 * P], U32, "wet_c%d" % u)
-            wet_s[u] = place([P, 2 * P], U8, "wet_s%d" % u)
-            nc.vector.quantize_mx(
-                out=wet_c[u][:].bitcast(FP8X4), scales=wet_s[u][:], in_=grouped[u][:].rearrange("p s m j -> p (s m j)")
+        def round_wet(e):
+            grouped[e] = place([P, PACK, P, PACK], BF16, "grouped%d" % e)
+            nc.vector.tensor_copy(
+                out=grouped[e][:].rearrange("p t m j -> p m j t"),
+                in_=raw[e][:].rearrange("p j (m t) -> p m j t", t=PACK),
             )
 
-        def gather_scales():
-            nc.vector.tensor_copy(slot_s[:], dy_s[:].bitcast(U8).indirect(dst_sb[:]))
+        def round_half_wet(e, h, engine):
+            if h == 0:
+                grouped[e] = place([P, PACK, P, PACK], BF16, "grouped%d" % e)
+            to = grouped[e][:].rearrange("p t m j -> p m j t")[:, h * P // 2 : (h + 1) * P // 2]
+            copy_on(engine, to, raw[e, h][:].rearrange("p j (m t) -> p m j t", t=PACK))
 
-        def gather_words(x):
-            count = shares[x].stop - shares[x].start
-            slot_w[x] = place([P, count], U32, "slot_w%d" % x)
-            nc.vector.tensor_copy(slot_w[x][:], dy_w[:].bitcast(U32).indirect(dst_sb[:, entries(shares[x].start, count)]))
-
-        def expert_product(u):
-            e, x = expert_and_pair(u)
-            if u < FIRST_JOINT:
-                z_bank[u] = psum.tile([P, 2, C2], F32, name="bank")
-                outs = [z_bank[u][:, s, :] for s in range(2)]
-            else:
-                steps = [e // 2 * PACK + 2 * x + s for s in range(2)]
-                for step in steps:
-                    if step not in z_bank:
-                        z_bank[step] = psum.tile([P, C1], F32, name="bank")
-                outs = [z_bank[step][:, e % 2 * C2 : (e % 2 + 1) * C2] for step in steps]
-            for s in range(2):
+        def quantize_wet(e):
+            wet_c[e] = place([P, W], U32, "wet_c%d" % e)
+            wet_s[e] = place([P, W], U8, "wet_s%d" % e)
+            nc.vector.quantize_mx(
+                out=wet_c[e][:].bitcast(FP8X4), scales=wet_s[e][:], in_=grouped[e][:].rearrange("p t m j -> p (t m j)")
+            )
+            z_bank[e] = psum.tile([P, PACK, C2], F32, name="bank")
+            f, x = divmod(e, 2)
+            for t in range(PACK):
                 nc.tensor.matmul_mx(
-                    out=outs[s],
-                    lhsT=wet_c[u][:, s * P : (s + 1) * P].bitcast(FP8X4),
-                    lhsT_scale=wet_s[u][:, s * P : (s + 1) * P],
-                    rhs=in_share(slot_w, e).bitcast(FP8X4),
-                    rhs_scale=slot_s[:, e * C2 : (e + 1) * C2],
+                    out=z_bank[e][:, t, :],
+                    lhsT=wet_c[e][:, t * P : (t + 1) * P].bitcast(FP8X4),
+                    lhsT_scale=wet_s[e][:, t * P : (t + 1) * P],
+                    rhs=slot_w[f][:, x * C2 : (x + 1) * C2].bitcast(FP8X4),
+                    rhs_scale=slot_s[f][:, x * C2 : (x + 1) * C2],
                     start=True,
                     stop=True,
                 )
 
-        def fetch_z(u):
-            if u < FIRST_JOINT:
-                z_sb[u] = place([P, 2, C2], F32, "z_sb%d" % u)
-                nc.scalar.activation(out=z_sb[u][:], in_=z_bank[u][:], func=ACT.Copy, scale=-0.5)
-                return
-            z_sb[u] = place([P, C1], F32, "z_sb%d" % u)
-            plane = z_bank[u][:]
-            if u < FIRST_COPY_UNIT:
-                nc.scalar.activation(out=z_sb[u][:], in_=plane, func=ACT.Copy, scale=-0.5)
+        def gather_scales(f):
+            slot_s[f] = place([P, C1], U8, "slot_s%d" % f)
+            nc.vector.tensor_copy(slot_s[f][:], dy_s[:].bitcast(U8).indirect(dst_sb[:, entries(f * C1, C1)]))
+
+        def gather_words(f):
+            slot_w[f] = place([P, C1], U32, "slot_w%d" % f)
+            nc.vector.tensor_copy(slot_w[f][:], dy_w[:].bitcast(U32).indirect(dst_sb[:, entries(f * C1, C1)]))
+
+        def fetch_z(e):
+            f, x = divmod(e, 2)
+            if f < BY_EXPERT:
+                z_sb[e] = place([P, PACK, C2], F32, "z_sb%d" % e)
+                to = z_sb[e][:]
             else:
-                nc.vector.scalar_tensor_tensor(z_sb[u][:], plane, -0.5, gate_of(u // PACK * C1, C1), ALU.mult, ALU.mult)
+                if x == 0:
+                    z_sb[e] = place([P, PACK, C1], F32, "z_sb%d" % e)
+                to = z_sb[2 * f][:, :, x * C2 : (x + 1) * C2]
+            weight = gate_sb[f][:, x * C2 : (x + 1) * C2].unsqueeze(1).to_broadcast([P, PACK, C2])
+            nc.vector.scalar_tensor_tensor(to, z_bank[e][:], -0.5, weight, ALU.mult, ALU.mult)
 
-        def scatter_z(u, which=range(2)):
-            if u >= FIRST_JOINT:
-                f, t = divmod(u, PACK)
-                z_win[f, t] = place([P, (f + 1) * C1], F32, "z_win%d_%d" % (f, t))
-                to = z_win[f, t][:].indirect(offs2_sb[:, entries(f * C1, C1)])
-                if u < FIRST_COPY_UNIT:
-                    nc.vector.tensor_tensor(to, z_sb[u][:], gate_of(f * C1, C1), ALU.mult)
-                else:
-                    nc.vector.tensor_copy(to, z_sb[u][:])
-                return
-            e, x = divmod(u, 2)
+        def scatter_z(e, t, engine):
             f = e // 2
-            for s in which:
-                t = 2 * x + s
-                if (f, t) not in z_win:
-                    z_win[f, t] = place([P, max(2, f + 1) * C1], F32, "z_win%d_%d" % (f, t))
-                to = z_win[f, t][:].indirect(offs2_sb[:, entries(e * C2, C2)])
-                nc.vector.tensor_tensor(to, z_sb[u][:, s, :], gate_of(e * C2, C2), ALU.mult)
+            count = C2 if f < BY_EXPERT else C1
+            if (f, t) not in z_win:
+                z_win[f, t] = place([P, (f + 1) * C1], F32, "z_win%d_%d" % (f, t))
+            scatter_on(engine, z_win[f, t][:].indirect(offs2_sb[:, entries(e * C2, count)]), z_sb[e][:, t, :])
 
-        def tanh_of(f, ts):
-            if ts.start == 0:
-                tanh_sb[f] = place([P, PACK, C1], F32, "tanh%d" % f)
-            nc.scalar.activation(out=tanh_sb[f][:, ts, :], in_=a_sb[f][:, ts, :], func=ACT.Tanh, scale=0.5, bias=no_bias[:])
-
-        def silu_of(f, ts):
-            if ts.start == 0:
-                silu_sb[f] = place([P, PACK, C1], F32, "silu%d" % f)
-            nc.scalar.activation(out=silu_sb[f][:, ts, :], in_=a_sb[f][:, ts, :], func=ACT.Silu, scale=-1.0, bias=no_bias[:])
-
-        def scattered(f, t):
-            return z_win[f, t][:, f * C1 : (f + 1) * C1]
-
-        def first_factors(x):
-            tanh_sb[0, x] = place([P, 2, C1], F32, "tanh0_%d" % x)
-            nc.scalar.activation(out=tanh_sb[0, x][:], in_=a_sb[0, x][:], func=ACT.Tanh, scale=0.5, bias=no_bias[:])
-            silu_sb[0, x] = place([P, 2, C1], F32, "silu0_%d" % x)
-            nc.scalar.activation(out=silu_sb[0, x][:], in_=a_sb[0, x][:], func=ACT.Silu, scale=-1.0, bias=no_bias[:])
-
-        def first_products(x):
-            if x == 0:
-                planes[0] = place([P, PACK, C1], BF16, "planes0")
-            half = [place([P, C1], F32, "half0_%d" % (2 * x + s)) for s in range(2)]
-            for s in range(2):
-                nc.vector.scalar_tensor_tensor(half[s][:], tanh_sb[0, x][:, s, :], 1.0, scattered(0, 2 * x + s), ALU.add, ALU.mult)
-            for s in range(2):
-                nc.vector.scalar_tensor_tensor(
-                    planes[0][:, 2 * x + s, :], silu_sb[0, x][:, s, :], 1.0, half[s][:], ALU.subtract, ALU.mult
+        def factors(f):
+            for x in range(2):
+                tanh_sb[f, x] = place([P, 2, C1], F32, "tanh%d_%d" % (f, x))
+                nc.scalar.activation(
+                    out=tanh_sb[f, x][:], in_=a_sb[f][:, 2 * x : 2 * x + 2, :], func=ACT.Tanh, scale=0.5, bias=no_bias[:]
+                )
+            for x in range(2):
+                silu_sb[f, x] = place([P, 2, C1], F32, "silu%d_%d" % (f, x))
+                nc.scalar.activation(
+                    out=silu_sb[f, x][:], in_=a_sb[f][:, 2 * x : 2 * x + 2, :], func=ACT.Silu, scale=-1.0, bias=no_bias[:]
                 )
 
-        def plus_factor(f):
-            plus[f] = place([P, PACK, C1], F32, "plus%d" % f)
-            nc.scalar.activation(out=plus[f][:], in_=tanh_sb[f][:], func=ACT.Identity, bias=one[:])
+        def first_product(f, t):
+            x, s = divmod(t, 2)
+            if s == 0:
+                half_sb[f, x] = place([P, 2, C1], F32, "half%d_%d" % (f, x))
+            nc.vector.scalar_tensor_tensor(
+                half_sb[f, x][:, s, :], tanh_sb[f, x][:, s, :], 1.0, z_win[f, t][:, f * C1 : (f + 1) * C1], ALU.add, ALU.mult
+            )
 
-        def minus_factor(f):
-            minus[f] = place([P, PACK, C1], F32, "minus%d" % f)
-            nc.scalar.activation(out=minus[f][:], in_=silu_sb[f][:], func=ACT.Identity, bias=minus_one[:])
-
-        def half_product(f, x):
-            half_sb[f, x] = place([P, 2, C1], F32, "half%d_%d" % (f, x))
-            for s in range(2):
-                t = 2 * x + s
-                nc.gpsimd.tensor_tensor(half_sb[f, x][:, s, :], plus[f][:, t, :], scattered(f, t), ALU.mult)
-
-        def last_product(f):
-            planes[f] = place([P, PACK, C1], BF16, "planes%d" % f)
-            for x in range(2):
-                ts = slice(2 * x, 2 * x + 2)
-                nc.gpsimd.tensor_tensor(planes[f][:, ts, :], minus[f][:, ts, :], half_sb[f, x][:], ALU.mult)
-
-        def whole_products(f):
-            half_sb[f] = place([P, PACK, C1], F32, "half%d" % f)
-            for t in range(PACK):
-                nc.gpsimd.tensor_tensor(half_sb[f][:, t, :], plus[f][:, t, :], scattered(f, t), ALU.mult)
-            planes[f] = place([P, PACK, C1], BF16, "planes%d" % f)
-            nc.gpsimd.tensor_tensor(planes[f][:], minus[f][:], half_sb[f][:], ALU.mult)
+        def second_product(f, x):
+            if x == 0:
+                planes[f] = place([P, PACK, C1], BF16, "planes%d" % f)
+            nc.vector.scalar_tensor_tensor(
+                planes[f][:, 2 * x : 2 * x + 2, :], silu_sb[f, x][:], 1.0, half_sb[f, x][:], ALU.subtract, ALU.mult
+            )
 
         def interleave_da(f):
             da_bf[f] = place([P, C1, PACK], BF16, "da_bf%d" % f)
-            nc.scalar.copy(
+            nc.vector.tensor_copy(
                 out=da_bf[f][:].rearrange("q (c i) t -> q c t i", i=PACK),
                 in_=planes[f][:].rearrange("q t (c i) -> q c t i", i=PACK),
             )
@@ -302,18 +199,12 @@ def tile_moe_hib_silu_kernel(
             nc.vector.quantize_mx(
                 out=da_c[f][:].bitcast(FP8X4), scales=da_s[f][:], in_=da_bf[f][:].rearrange("q j t -> q (j t)")
             )
-
-        def group_product(f):
             for c in range(ROW_TILES):
-                if f > 0:
-                    dx_bank[f, c] = psum.tile([P, C1], F32, name="bank")[:]
-                else:
-                    if c % 2 == 0:
-                        both = psum.tile([P, 2, C1], F32, name="bank")
-                    dx_bank[f, c] = both[:, c % 2, :]
+                if c % 2 == 0:
+                    dx_bank[f, c // 2] = psum.tile([P, 2, C1], F32, name="bank")
                 ks = slice(c * P, (c + 1) * P)
                 nc.tensor.matmul_mx(
-                    out=dx_bank[f, c],
+                    out=dx_bank[f, c // 2][:, c % 2, :],
                     lhsT=wgt_w[f][:, ks].bitcast(FP8X4),
                     lhsT_scale=wgt_s[SCALE_ROWS * f : P, ks],
                     rhs=da_c[f][:].bitcast(FP8X4),
@@ -322,14 +213,14 @@ def tile_moe_hib_silu_kernel(
                     stop=True,
                 )
 
-        def fetch_dx(f, c):
-            dx_sb[f, c] = place([P, C1], F32, "dx%d_%d" % (f, c))
-            nc.scalar.copy(out=dx_sb[f, c][:], in_=dx_bank[f, c])
+        def fetch_dx(f, b, engine):
+            dx_sb[f, b] = place([P, 2, C1], F32, "dx%d_%d" % (f, b))
+            copy_on(engine, dx_sb[f, b][:], dx_bank[f, b][:])
 
-        def scatter_dx(f, c):
+        def scatter_dx(f, c, engine):
             if f == 0:
                 out_sb[c] = place([P, T], F32, "out_sb%d" % c)
-            nc.vector.tensor_copy(out_sb[c][:].indirect(offs_sb[:, entries(f * C1, C1)]), dx_sb[f, c][:])
+            scatter_on(engine, out_sb[c][:].indirect(offs_sb[:, entries(f * C1, C1)]), dx_sb[f, c // 2][:, c % 2, :])
             if f == G - 1:
                 nc.sync.dma_start(out=out[c * P : (c + 1) * P, :], in_=out_sb[c][:])
 
@@ -339,28 +230,19 @@ def tile_moe_hib_silu_kernel(
         for q in range(QUADRANTS):
             rows_q = dy_scales[0, SCALE_ROWS * q : SCALE_ROWS * (q + 1), :].bitcast(I32)
             (nc.sync, nc.scalar)[q // 2].dma_start(
-                out=dy_s[QUADRANT * q : QUADRANT * (q + 1), 0 : T // 4], in_=rows_q.partition_broadcast(QUADRANT // SCALE_ROWS)
+                out=dy_s[QUADRANT * q : QUADRANT * (q + 1), :], in_=rows_q.partition_broadcast(QUADRANT // SCALE_ROWS)
             )
-        load_half_wet(0, 0)
+        load_a(0)
         nc.sync.dma_start(out=dy_w[:], in_=dy_words[0].rearrange("p t d -> p (t d)").bitcast(I32))
+        load_half_wet(0, 0)
         load_half_wet(0, 1)
         nc.sync.dma_start(offs2_sb[:], offs2)
         load_gate(0)
-        load_half_wet(1, 0)
-        load_half_wet(1, 1)
-        load_half_wet(2, 0)
-        load_half_wet(2, 1)
-        load_wet(3)
-        load_first_a(0)
-        load_gate(1)
-        load_wet(4)
-        load_wet(5)
-        load_first_a(1)
-        load_gate(2)
-        load_wet(6)
-        load_wet(7)
-        load_gate(3)
         load_a(1)
+        load_wet(1)
+        load_wet(2)
+        load_gate(1)
+        load_wet(3)
         for q in range(QUADRANTS):
             nc.sync.dma_start(
                 out=wgt_s[QUADRANT * q : QUADRANT * q + G * SCALE_ROWS, :].bitcast(I32),
@@ -368,127 +250,70 @@ def tile_moe_hib_silu_kernel(
             )
         load_wgt(0)
         nc.sync.dma_start(offs_sb[:], offs)
-        load_a(2)
-        load_wgt(1)
-        load_a(3)
-        load_wgt(2)
-        load_wgt(3)
+        for f in range(2, G):
+            load_wet(2 * f)
+            load_wet(2 * f + 1)
+            load_a(f)
+            load_gate(f)
+            load_wgt(f - 1)
+        load_wgt(G - 1)
 
         nc.vector.memset(zero[:], 0.0)
         nc.scalar.activation(out=no_bias[:], in_=zero[:], func=ACT.Silu)
 
-        nc.vector.memset(dy_s[:, T // 4 :], 0)
-        gather_scales()
-        round_wet(0, ms=slice(0, P // 2))
-        round_wet(1)
+        gather_scales(0)
         gather_words(0)
-        round_wet(0, on_vector=True, ms=slice(P // 2, P))
+        factors(0)
+        round_half_wet(0, 0, "scalar")
+        round_half_wet(0, 1, "vector")
+        gather_scales(1)
         quantize_wet(0)
-        quantize_wet(1)
         gather_words(1)
+        factors(1)
+        for e in range(2 * BY_EXPERT):
+            fetch_z(e)
+            for t in range(PACK):
+                scatter_z(e, t, "scalar")
+            if e + 1 < 2 * BY_EXPERT:
+                round_wet(e + 1)
+                if e < 2:
+                    gather_scales(e + 2)
+                quantize_wet(e + 1)
+                if e < 2:
+                    gather_words(e + 2)
+            if e + 2 == 2 * BY_EXPERT:
+                first_product(0, 0)
+                first_product(0, 1)
 
-        low, high, all_planes = slice(0, 2), slice(2, PACK), slice(0, PACK)
-        expert_product(0)
-        fetch_z(0)
-        round_wet(2)
-        round_wet(3, ms=slice(0, P // 2))
-        expert_product(1)
-        fetch_z(1)
-        round_wet(3, ms=slice(P // 2, P))
-        scatter_z(0)
-        quantize_wet(2)
-        scatter_z(1, [0])
-        scatter_z(1, [1])
-        quantize_wet(3)
-
-        early, late = slice(0, P // 2), slice(P // 2, P)
-        expert_product(2)
-        round_wet(4, ms=early)
-        fetch_z(2)
-        round_wet(5, ms=early)
-        round_wet(4, ms=late)
-        scatter_z(2)
-        quantize_wet(4)
-        expert_product(3)
-        fetch_z(3)
-        round_wet(5, ms=late)
-        round_wet(6)
-        first_factors(0)
-        scatter_z(3)
-        quantize_wet(5)
-        quantize_wet(6)
-        first_products(0)
-        for u in range(FIRST_JOINT, FIRST_COPY_UNIT):
-            coming = u + AHEAD + 1
-            if u % 2 == 0:
-                pair = (4 + u // 2 % 2, 6 + u // 2 % 2) if u < 2 * FIRST_JOINT else (u, u + 1)
-                for v in pair:
-                    expert_product(v)
-            fetch_z(u)
-            if coming < UNITS:
-                round_wet(coming)
-            if u == PRODUCT_STEPS[1]:
-                first_factors(1)
-            if u == INTERLEAVE_STEP:
-                interleave_da(0)
-            if u in TANH_HALF_STEPS:
-                tanh_of(1, (low, high)[TANH_HALF_STEPS.index(u)])
-            scatter_z(u)
-            if u == QUANTISE_STEP:
-                quantize_da(0)
-            if coming < UNITS:
-                quantize_wet(coming)
-            if u == PRODUCT_STEPS[1]:
-                first_products(1)
-
-        plus_factor(1)
-        group_product(0)
-        fetch_dx(0, 0)
-        silu_of(1, all_planes)
-        fetch_dx(0, 1)
-        fetch_dx(0, 2)
-        minus_factor(1)
-        whole_products(1)
-        for u in range(FIRST_COPY_UNIT, UNITS):
-            expert_product(u)
-        for u in range(FIRST_COPY_UNIT, UNITS):
-            fetch_z(u)
-        for u in range(FIRST_COPY_UNIT, UNITS):
-            scatter_z(u)
-        scatter_dx(0, 0)
-
-        last = ROW_TILES - 1
-        for f in range(1, G):
-            following = f + 1 < G
-            if f == 1:
-                tanh_of(2, all_planes)
-            else:
-                for c in range(last):
-                    fetch_dx(f - 1, c)
-            if following:
-                if f == 1:
-                    silu_of(2, all_planes)
-                plus_factor(f + 1)
-                if f == 2:
-                    silu_of(3, all_planes)
-                half_product(f + 1, 0)
-            if f == 1:
-                minus_factor(2)
+        for f in range(G):
+            coming = f + 1 < G and f + 1 >= BY_EXPERT
+            last = f == G - 1
+            if coming:
+                round_wet(2 * f + 2)
+                round_wet(2 * f + 3)
+                quantize_wet(2 * f + 2)
+                quantize_wet(2 * f + 3)
+            if last:
+                scatter_z(2 * f, PACK - 1, "vector")
+            for t in range(2 if f == 0 else 0, PACK):
+                first_product(f, t)
+            second_product(f, 0)
+            second_product(f, 1)
+            if BY_EXPERT <= f + 1 < G:
+                factors(f + 1)
+            if coming:
+                fetch_z(2 * f + 2)
             interleave_da(f)
-            fetch_dx(f - 1, last)
-            if f == 2:
-                minus_factor(3)
-            if f == 1:
-                tanh_of(3, all_planes)
-            for c in range(1 if f == 1 else 0, last):
-                scatter_dx(f - 1, c)
+            if coming:
+                fetch_z(2 * f + 3)
+                for t in range(PACK - 1 if f + 2 == G else PACK):
+                    scatter_z(2 * f + 2, t, "scalar")
             quantize_da(f)
-            if following:
-                half_product(f + 1, 1)
-                last_product(f + 1)
-            scatter_dx(f - 1, last)
-            group_product(f)
-        for c in range(ROW_TILES):
-            fetch_dx(G - 1, c)
-        for c in range(ROW_TILES):
-            scatter_dx(G - 1, c)
+            if f > 0:
+                scatter_dx(f - 1, 1, "scalar" if last else "vector")
+            fetch_dx(f, 0, "vector")
+            fetch_dx(f, 1, "scalar")
+            scatter_dx(f, 0, "vector")
+            scatter_dx(f, 2, "scalar")
+            scatter_dx(f, 3, "scalar")
+        scatter_dx(G - 1, 1, "vector")

@@ -28,16 +28,33 @@ FLOPS = 2 * 2 * W * W * T
 BY_EXPERT = 2
 
 TAKES_PLACE_OF = {
-    **{"grouped%d" % e: "grouped%d" % (e % 2) for e in range(E)},
-    **{"wet_c%d" % e: "wet_c%d" % (e % 2) for e in range(E)},
-    **{"wet_s%d" % e: "wet_s%d" % (e % 2) for e in range(E)},
+    "wet_c2": "wet_c1",
+    "wet_c3": "raw0_0",
+    **{"wet_s%d" % e: "wet_s%d" % (e % 2) for e in range(2 * BY_EXPERT)},
     **{"z_win%d_%d" % (f, t): "z_win%d_%d" % (f % 2, t) for f in range(G) for t in range(PACK)},
-    **{"%s%d_%d" % (name, f, x): "%s1_%d" % (name, x) for name in ("tanh", "silu") for f in range(1, G) for x in range(2)},
-    **{"half%d_%d" % (f, x): "half1_%d" % x for f in range(1, G) for x in range(2)},
-    "half0_0": "raw3",
+    **{"%s%d_%d" % (name, f, x): "%s%d_%d" % (name, f % 2, x) for name in ("tanh", "silu") for f in range(G) for x in range(2)},
+    "slot_w1": "raw0_1",
+    "slot_w2": "wet_c0",
+    "slot_w3": "grouped1",
+    "grouped2": "grouped0",
+    "grouped3": "raw1",
+    "half0": "raw3",
+    "da_bf0": "grouped0",
+    "grouped4": "grouped0",
+    "da_c0": "raw1",
+    "grouped5": "raw1",
+    "pair_c2": "raw5",
+    "half1": "raw1",
+    "da_bf1": "raw2",
+    "grouped6": "raw2",
+    "da_c1": "raw4",
+    "grouped7": "raw4",
+    "pair_c3": "raw7",
+    "half2": "raw4",
+    "half3": "z_plane3_3",
     **{"planes%d" % f: "planes0" for f in range(G)},
-    **{"da_bf%d" % f: "da_bf0" for f in range(G)},
-    **{"dx%d_%d" % (f, b): "dx%d_%d" % (f % 2, b) for f in range(G) for b in range(2)},
+    **{"dx%d_%d" % (f, b): "dx%d_%d" % (f % 2, b) for f in range(2) for b in (0, 2)},
+    **{"z_plane3_%d" % t: "z_plane2_%d" % t for t in range(PACK - 1)},
 }
 
 
@@ -64,7 +81,7 @@ def tile_moe_hib_silu_kernel(
         gate_sb = [held.tile([P, C1], F32, name="gate%d" % f, align_bytes=64) for f in range(G)]
         raw, grouped, wet_c, wet_s, slot_w, slot_s, z_sb, z_win, z_bank = {}, {}, {}, {}, {}, {}, {}, {}, {}
         a_sb, tanh_sb, silu_sb, half_sb, planes, da_bf, da_c, da_s = {}, {}, {}, {}, {}, {}, {}, {}
-        dx_sb, out_sb, dx_bank = {}, {}, {}
+        dx_sb, out_sb, dx_bank, pair, plane_bank, z_plane = {}, {}, {}, {}, {}, {}
 
         def entries(first, count):
             return slice(first // LIST, (first + count) // LIST)
@@ -107,6 +124,46 @@ def tile_moe_hib_silu_kernel(
                 in_=raw[e][:].rearrange("p j (m t) -> p m j t", t=PACK),
             )
 
+        def round_on_gpsimd(e):
+            grouped[e] = place([P, PACK, P, PACK], BF16, "grouped%d" % e)
+            to = grouped[e][:].rearrange("p t m j -> p m t j")
+            src = raw[e][:].rearrange("p j (m t) -> p m t j", t=PACK)
+            nc.gpsimd.tensor_scalar(to, src, 1.0, 0.0, ALU.mult, ALU.add)
+
+        def quantize_pair(f):
+            codes = place([P, 2 * W], U32, "pair_c%d" % f)
+            scales = place([P, 2 * W], U8, "pair_s%d" % f)
+            for x in (1, 0):
+                columns = slice(x * W, (x + 1) * W)
+                nc.vector.quantize_mx(
+                    out=codes[:, columns].bitcast(FP8X4),
+                    scales=scales[:, columns],
+                    in_=grouped[2 * f + x][:].rearrange("p t m j -> p (t m j)"),
+                )
+            for t in range(PACK):
+                if t % 2 == 0:
+                    bank = psum.tile([P, 2, C1], F32, name="bank")
+                plane_bank[f, t] = bank[:, t % 2, :]
+                for x in range(2):
+                    columns = slice(x * W + t * P, x * W + (t + 1) * P)
+                    nc.tensor.matmul_mx(
+                        out=bank[:, t % 2, x * C2 : (x + 1) * C2],
+                        lhsT=codes[:, columns].bitcast(FP8X4),
+                        lhsT_scale=scales[:, columns],
+                        rhs=slot_w[f][:, x * C2 : (x + 1) * C2].bitcast(FP8X4),
+                        rhs_scale=slot_s[f][:, x * C2 : (x + 1) * C2],
+                        start=True,
+                        stop=True,
+                    )
+
+        def fetch_plane(f, t):
+            z_plane[f, t] = place([P, C1], F32, "z_plane%d_%d" % (f, t))
+            nc.vector.scalar_tensor_tensor(z_plane[f, t][:], plane_bank[f, t], -0.5, gate_sb[f][:], ALU.mult, ALU.mult)
+
+        def scatter_plane(f, t, engine):
+            z_win[f, t] = place([P, (f + 1) * C1], F32, "z_win%d_%d" % (f, t))
+            scatter_on(engine, z_win[f, t][:].indirect(offs2_sb[:, entries(f * C1, C1)]), z_plane[f, t][:])
+
         def round_half_wet(e, h, engine):
             if h == 0:
                 grouped[e] = place([P, PACK, P, PACK], BF16, "grouped%d" % e)
@@ -142,22 +199,16 @@ def tile_moe_hib_silu_kernel(
 
         def fetch_z(e):
             f, x = divmod(e, 2)
-            if f < BY_EXPERT:
-                z_sb[e] = place([P, PACK, C2], F32, "z_sb%d" % e)
-                to = z_sb[e][:]
-            else:
-                if x == 0:
-                    z_sb[e] = place([P, PACK, C1], F32, "z_sb%d" % e)
-                to = z_sb[2 * f][:, :, x * C2 : (x + 1) * C2]
+            z_sb[e] = place([P, PACK, C2], F32, "z_sb%d" % e)
+            to = z_sb[e][:]
             weight = gate_sb[f][:, x * C2 : (x + 1) * C2].unsqueeze(1).to_broadcast([P, PACK, C2])
             nc.vector.scalar_tensor_tensor(to, z_bank[e][:], -0.5, weight, ALU.mult, ALU.mult)
 
         def scatter_z(e, t, engine):
             f = e // 2
-            count = C2 if f < BY_EXPERT else C1
             if (f, t) not in z_win:
                 z_win[f, t] = place([P, (f + 1) * C1], F32, "z_win%d_%d" % (f, t))
-            scatter_on(engine, z_win[f, t][:].indirect(offs2_sb[:, entries(e * C2, count)]), z_sb[e][:, t, :])
+            scatter_on(engine, z_win[f, t][:].indirect(offs2_sb[:, entries(e * C2, C2)]), z_sb[e][:, t, :])
 
         def factors(f):
             for x in range(2):
@@ -173,17 +224,17 @@ def tile_moe_hib_silu_kernel(
 
         def first_product(f, t):
             x, s = divmod(t, 2)
-            if s == 0:
-                half_sb[f, x] = place([P, 2, C1], F32, "half%d_%d" % (f, x))
+            if f not in half_sb:
+                half_sb[f] = place([P, PACK, C1], F32, "half%d" % f)
             nc.vector.scalar_tensor_tensor(
-                half_sb[f, x][:, s, :], tanh_sb[f, x][:, s, :], 1.0, z_win[f, t][:, f * C1 : (f + 1) * C1], ALU.add, ALU.mult
+                half_sb[f][:, t, :], tanh_sb[f, x][:, s, :], 1.0, z_win[f, t][:, f * C1 : (f + 1) * C1], ALU.add, ALU.mult
             )
 
         def second_product(f, x):
             if x == 0:
                 planes[f] = place([P, PACK, C1], BF16, "planes%d" % f)
             nc.vector.scalar_tensor_tensor(
-                planes[f][:, 2 * x : 2 * x + 2, :], silu_sb[f, x][:], 1.0, half_sb[f, x][:], ALU.subtract, ALU.mult
+                planes[f][:, 2 * x : 2 * x + 2, :], silu_sb[f, x][:], 1.0, half_sb[f][:, 2 * x : 2 * x + 2, :], ALU.subtract, ALU.mult
             )
 
         def interleave_da(f):
@@ -213,14 +264,17 @@ def tile_moe_hib_silu_kernel(
                     stop=True,
                 )
 
-        def fetch_dx(f, b, engine):
-            dx_sb[f, b] = place([P, 2, C1], F32, "dx%d_%d" % (f, b))
-            copy_on(engine, dx_sb[f, b][:], dx_bank[f, b][:])
+        def fetch_dx(f, first, count, engine):
+            tile = place([P, count, C1], F32, "dx%d_%d" % (f, first))
+            copy_on(engine, tile[:], dx_bank[f, first // 2][:, first % 2 : first % 2 + count, :])
+            for c in range(count):
+                dx_sb[f, first + c] = tile[:, c, :]
 
-        def scatter_dx(f, c, engine):
-            if f == 0:
+        def scatter_dx(f, c, engine, slots=slice(0, C1)):
+            if c not in out_sb:
                 out_sb[c] = place([P, T], F32, "out_sb%d" % c)
-            scatter_on(engine, out_sb[c][:].indirect(offs_sb[:, entries(f * C1, C1)]), dx_sb[f, c // 2][:, c % 2, :])
+            listed = entries(f * C1 + slots.start, slots.stop - slots.start)
+            scatter_on(engine, out_sb[c][:].indirect(offs_sb[:, listed]), dx_sb[f, c][:, slots])
             if f == G - 1:
                 nc.sync.dma_start(out=out[c * P : (c + 1) * P, :], in_=out_sb[c][:])
 
@@ -232,14 +286,14 @@ def tile_moe_hib_silu_kernel(
             (nc.sync, nc.scalar)[q // 2].dma_start(
                 out=dy_s[QUADRANT * q : QUADRANT * (q + 1), :], in_=rows_q.partition_broadcast(QUADRANT // SCALE_ROWS)
             )
-        load_a(0)
-        nc.sync.dma_start(out=dy_w[:], in_=dy_words[0].rearrange("p t d -> p (t d)").bitcast(I32))
         load_half_wet(0, 0)
         load_half_wet(0, 1)
-        nc.sync.dma_start(offs2_sb[:], offs2)
+        nc.sync.dma_start(out=dy_w[:], in_=dy_words[0].rearrange("p t d -> p (t d)").bitcast(I32))
         load_gate(0)
-        load_a(1)
+        nc.sync.dma_start(offs2_sb[:], offs2)
+        load_a(0)
         load_wet(1)
+        load_a(1)
         load_wet(2)
         load_gate(1)
         load_wet(3)
@@ -261,59 +315,97 @@ def tile_moe_hib_silu_kernel(
         nc.vector.memset(zero[:], 0.0)
         nc.scalar.activation(out=no_bias[:], in_=zero[:], func=ACT.Silu)
 
-        gather_scales(0)
-        gather_words(0)
-        factors(0)
+        for f in range(G):
+            gather_scales(f)
         round_half_wet(0, 0, "scalar")
-        round_half_wet(0, 1, "vector")
-        gather_scales(1)
+        round_half_wet(0, 1, "scalar")
+        gather_words(0)
         quantize_wet(0)
         gather_words(1)
+        fetch_z(0)
+        for t in range(PACK):
+            scatter_z(0, t, "scalar")
+        factors(0)
+        gather_words(2)
+        round_wet(1)
+        quantize_wet(1)
+        gather_words(3)
+        fetch_z(1)
+        for t in range(PACK):
+            scatter_z(1, t, "scalar")
         factors(1)
-        for e in range(2 * BY_EXPERT):
-            fetch_z(e)
-            for t in range(PACK):
-                scatter_z(e, t, "scalar")
-            if e + 1 < 2 * BY_EXPERT:
-                round_wet(e + 1)
-                if e < 2:
-                    gather_scales(e + 2)
-                quantize_wet(e + 1)
-                if e < 2:
-                    gather_words(e + 2)
-            if e + 2 == 2 * BY_EXPERT:
-                first_product(0, 0)
-                first_product(0, 1)
+        round_wet(2)
+        quantize_wet(2)
+        round_wet(3)
+        fetch_z(2)
+        for t in range(PACK - 1):
+            scatter_z(2, t, "scalar")
+        quantize_wet(3)
+        for t in range(PACK):
+            first_product(0, t)
+        second_product(0, 0)
+        second_product(0, 1)
+        fetch_z(3)
+        for t in range(PACK - 1):
+            scatter_z(3, t, "scalar")
+        interleave_da(0)
+        scatter_z(2, PACK - 1, "vector")
+        quantize_da(0)
+        scatter_z(3, PACK - 1, "vector")
 
-        for f in range(G):
-            coming = f + 1 < G and f + 1 >= BY_EXPERT
-            last = f == G - 1
-            if coming:
-                round_wet(2 * f + 2)
-                round_wet(2 * f + 3)
-                quantize_wet(2 * f + 2)
-                quantize_wet(2 * f + 3)
-            if last:
-                scatter_z(2 * f, PACK - 1, "vector")
-            for t in range(2 if f == 0 else 0, PACK):
-                first_product(f, t)
-            second_product(f, 0)
-            second_product(f, 1)
-            if BY_EXPERT <= f + 1 < G:
-                factors(f + 1)
-            if coming:
-                fetch_z(2 * f + 2)
-            interleave_da(f)
-            if coming:
-                fetch_z(2 * f + 3)
-                for t in range(PACK - 1 if f + 2 == G else PACK):
-                    scatter_z(2 * f + 2, t, "scalar")
-            quantize_da(f)
-            if f > 0:
-                scatter_dx(f - 1, 1, "scalar" if last else "vector")
-            fetch_dx(f, 0, "vector")
-            fetch_dx(f, 1, "scalar")
+        for f in range(2):
+            round_on_gpsimd(2 * f + 4)
+            round_on_gpsimd(2 * f + 5)
+            factors(f + 2)
+            fetch_dx(f, 0, 2, "vector")
+            fetch_dx(f, 2, 2, "vector")
             scatter_dx(f, 0, "vector")
-            scatter_dx(f, 2, "scalar")
+            scatter_dx(f, 1, "vector")
+            if f == 0:
+                scatter_dx(f, 2, "scalar")
+            else:
+                scatter_dx(f, 2, "vector", slice(0, C2))
             scatter_dx(f, 3, "scalar")
-        scatter_dx(G - 1, 1, "vector")
+            if f == 1:
+                scatter_dx(f, 2, "scalar", slice(C2, C1))
+            quantize_pair(f + 2)
+            first_product(f + 1, 0)
+            first_product(f + 1, 1)
+            fetch_plane(f + 2, 0)
+            scatter_plane(f + 2, 0, "scalar")
+            first_product(f + 1, 2)
+            first_product(f + 1, 3)
+            second_product(f + 1, 0)
+            second_product(f + 1, 1)
+            fetch_plane(f + 2, 1)
+            scatter_plane(f + 2, 1, "scalar")
+            interleave_da(f + 1)
+            fetch_plane(f + 2, 3 if f == 1 else 2)
+            quantize_da(f + 1)
+            fetch_plane(f + 2, 2 if f == 1 else 3)
+            scatter_plane(f + 2, 2, "scalar")
+            scatter_plane(f + 2, 3, "vector" if f == 1 else "scalar")
+
+        fetch_dx(2, 0, 1, "vector")
+        scatter_dx(2, 0, "scalar")
+        for t in (0, 1, 3):
+            first_product(3, t)
+        second_product(3, 0)
+        first_product(3, 2)
+        fetch_dx(2, 1, 1, "vector")
+        scatter_dx(2, 1, "scalar")
+        second_product(3, 1)
+        fetch_dx(2, 2, 1, "vector")
+        scatter_dx(2, 2, "scalar")
+        interleave_da(3)
+        fetch_dx(2, 3, 1, "vector")
+        quantize_da(3)
+        scatter_dx(2, 3, "vector")
+        fetch_dx(3, 0, 1, "scalar")
+        fetch_dx(3, 1, 1, "scalar")
+        fetch_dx(3, 2, 1, "vector")
+        fetch_dx(3, 3, 1, "vector")
+        scatter_dx(3, 0, "scalar")
+        scatter_dx(3, 1, "scalar")
+        scatter_dx(3, 2, "vector")
+        scatter_dx(3, 3, "vector")

@@ -28,31 +28,35 @@ FLOPS = 2 * 2 * W * W * T
 BY_EXPERT = 2
 
 TAKES_PLACE_OF = {
-    "wet_c2": "wet_c1",
-    "wet_c3": "raw0_0",
+    "wet_c2": "wet_c0",
+    "wet_c3": "wet_c1",
     **{"wet_s%d" % e: "wet_s%d" % (e % 2) for e in range(2 * BY_EXPERT)},
-    **{"z_win%d_%d" % (f, t): "z_win%d_%d" % (f % 2, t) for f in range(G) for t in range(PACK)},
-    **{"%s%d_%d" % (name, f, x): "%s%d_%d" % (name, f % 2, x) for name in ("tanh", "silu") for f in range(G) for x in range(2)},
-    "slot_w1": "raw0_1",
-    "slot_w2": "wet_c0",
-    "slot_w3": "grouped1",
-    "grouped2": "grouped0",
+    **{"z_win%d_%d" % (f, t): "z_win%d_%d" % (f % 2, t) for f in range(G) for t in range(PACK - 1)},
+    **{"sig%d" % f: "sig%d" % (f % 2) for f in range(G)},
+    "slot_w3": "grouped0",
+    "z_win0_3": "grouped1",
+    "z_win2_3": "grouped1",
+    "grouped2": "raw0",
+    "bend0": "raw2",
     "grouped3": "raw1",
     "half0": "raw3",
-    "da_bf0": "grouped0",
-    "grouped4": "grouped0",
+    "z_win1_3": "raw3",
+    "z_win3_3": "raw3",
+    "da_bf0": "raw0",
+    "grouped4": "raw0",
     "da_c0": "raw1",
     "grouped5": "raw1",
     "pair_c2": "raw5",
-    "half1": "raw1",
+    "bend1": "raw1",
     "da_bf1": "raw2",
     "grouped6": "raw2",
     "da_c1": "raw4",
     "grouped7": "raw4",
     "pair_c3": "raw7",
-    "half2": "raw4",
+    "bend2": "raw4",
+    "bend3": "raw4",
+    "half2": "half1",
     "half3": "z_plane3_3",
-    **{"planes%d" % f: "planes0" for f in range(G)},
     **{"dx%d_%d" % (f, b): "dx%d_%d" % (f % 2, b) for f in range(2) for b in (0, 2)},
     **{"z_plane3_%d" % t: "z_plane2_%d" % t for t in range(PACK - 1)},
 }
@@ -80,7 +84,7 @@ def tile_moe_hib_silu_kernel(
         wgt_w = [held.tile([P, W], I32, name="wgt_w%d" % f, align_bytes=64) for f in range(G)]
         gate_sb = [held.tile([P, C1], F32, name="gate%d" % f, align_bytes=64) for f in range(G)]
         raw, grouped, wet_c, wet_s, slot_w, slot_s, z_sb, z_win, z_bank = {}, {}, {}, {}, {}, {}, {}, {}, {}
-        a_sb, tanh_sb, silu_sb, half_sb, planes, da_bf, da_c, da_s = {}, {}, {}, {}, {}, {}, {}, {}
+        a_sb, sig, bend, half_sb, da_bf, da_c, da_s = {}, {}, {}, {}, {}, {}, {}
         dx_sb, out_sb, dx_bank, pair, plane_bank, z_plane = {}, {}, {}, {}, {}, {}
 
         def entries(first, count):
@@ -89,11 +93,6 @@ def tile_moe_hib_silu_kernel(
         def load_wet(e):
             raw[e] = place([P, PACK, W], F32, "raw%d" % e)
             nc.sync.dma_start(out=raw[e][:], in_=wet[e].rearrange("(p j) i -> p j i", j=PACK))
-
-        def load_half_wet(e, h):
-            raw[e, h] = place([P, PACK, W // 2], F32, "raw%d_%d" % (e, h))
-            columns = slice(h * W // 2, (h + 1) * W // 2)
-            nc.sync.dma_start(out=raw[e, h][:], in_=wet[e].rearrange("(p j) i -> p j i", j=PACK)[:, :, columns])
 
         def load_gate(f):
             nc.sync.dma_start(out=gate_sb[f][:], in_=gate[:, f * C1 : (f + 1) * C1])
@@ -126,8 +125,8 @@ def tile_moe_hib_silu_kernel(
 
         def round_on_gpsimd(e):
             grouped[e] = place([P, PACK, P, PACK], BF16, "grouped%d" % e)
-            to = grouped[e][:].rearrange("p t m j -> p m t j")
-            src = raw[e][:].rearrange("p j (m t) -> p m t j", t=PACK)
+            to = grouped[e][:].rearrange("p t m j -> p m j t")
+            src = raw[e][:].rearrange("p j (m t) -> p m j t", t=PACK)
             nc.gpsimd.tensor_scalar(to, src, 1.0, 0.0, ALU.mult, ALU.add)
 
         def quantize_pair(f):
@@ -158,7 +157,7 @@ def tile_moe_hib_silu_kernel(
 
         def fetch_plane(f, t):
             z_plane[f, t] = place([P, C1], F32, "z_plane%d_%d" % (f, t))
-            nc.vector.scalar_tensor_tensor(z_plane[f, t][:], plane_bank[f, t], -0.5, gate_sb[f][:], ALU.mult, ALU.mult)
+            nc.vector.scalar_tensor_tensor(z_plane[f, t][:], plane_bank[f, t], -1.0, gate_sb[f][:], ALU.mult, ALU.mult)
 
         def scatter_plane(f, t, engine):
             z_win[f, t] = place([P, (f + 1) * C1], F32, "z_win%d_%d" % (f, t))
@@ -168,7 +167,8 @@ def tile_moe_hib_silu_kernel(
             if h == 0:
                 grouped[e] = place([P, PACK, P, PACK], BF16, "grouped%d" % e)
             to = grouped[e][:].rearrange("p t m j -> p m j t")[:, h * P // 2 : (h + 1) * P // 2]
-            copy_on(engine, to, raw[e, h][:].rearrange("p j (m t) -> p m j t", t=PACK))
+            src = raw[e][:].rearrange("p j (m t) -> p m j t", t=PACK)[:, h * P // 2 : (h + 1) * P // 2]
+            copy_on(engine, to, src)
 
         def quantize_wet(e):
             wet_c[e] = place([P, W], U32, "wet_c%d" % e)
@@ -202,46 +202,38 @@ def tile_moe_hib_silu_kernel(
             z_sb[e] = place([P, PACK, C2], F32, "z_sb%d" % e)
             to = z_sb[e][:]
             weight = gate_sb[f][:, x * C2 : (x + 1) * C2].unsqueeze(1).to_broadcast([P, PACK, C2])
-            nc.vector.scalar_tensor_tensor(to, z_bank[e][:], -0.5, weight, ALU.mult, ALU.mult)
+            nc.vector.scalar_tensor_tensor(to, z_bank[e][:], -1.0, weight, ALU.mult, ALU.mult)
 
         def scatter_z(e, t, engine):
             f = e // 2
             if (f, t) not in z_win:
-                z_win[f, t] = place([P, (f + 1) * C1], F32, "z_win%d_%d" % (f, t))
+                z_win[f, t] = place([P, max(2, f + 1) * C1], F32, "z_win%d_%d" % (f, t))
             scatter_on(engine, z_win[f, t][:].indirect(offs2_sb[:, entries(e * C2, C2)]), z_sb[e][:, t, :])
 
-        def factors(f):
-            for x in range(2):
-                tanh_sb[f, x] = place([P, 2, C1], F32, "tanh%d_%d" % (f, x))
-                nc.scalar.activation(
-                    out=tanh_sb[f, x][:], in_=a_sb[f][:, 2 * x : 2 * x + 2, :], func=ACT.Tanh, scale=0.5, bias=no_bias[:]
-                )
-            for x in range(2):
-                silu_sb[f, x] = place([P, 2, C1], F32, "silu%d_%d" % (f, x))
-                nc.scalar.activation(
-                    out=silu_sb[f, x][:], in_=a_sb[f][:, 2 * x : 2 * x + 2, :], func=ACT.Silu, scale=-1.0, bias=no_bias[:]
-                )
+        def sigmoid_of(f):
+            sig[f] = place([P, PACK, C1], F32, "sig%d" % f)
+            nc.scalar.activation(out=sig[f][:], in_=a_sb[f][:], func=ACT.Sigmoid, bias=no_bias[:])
+
+        def bend_of(f, x):
+            if x == 0:
+                bend[f] = place([P, PACK, C1], F32, "bend%d" % f)
+            ts = slice(2 * x, 2 * x + 2)
+            nc.vector.scalar_tensor_tensor(bend[f][:, ts, :], sig[f][:, ts, :], 1.0, a_sb[f][:, ts, :], ALU.subtract, ALU.mult)
 
         def first_product(f, t):
-            x, s = divmod(t, 2)
             if f not in half_sb:
                 half_sb[f] = place([P, PACK, C1], F32, "half%d" % f)
             nc.vector.scalar_tensor_tensor(
-                half_sb[f][:, t, :], tanh_sb[f, x][:, s, :], 1.0, z_win[f, t][:, f * C1 : (f + 1) * C1], ALU.add, ALU.mult
+                half_sb[f][:, t, :], bend[f][:, t, :], 1.0, z_win[f, t][:, f * C1 : (f + 1) * C1], ALU.subtract, ALU.mult
             )
 
-        def second_product(f, x):
-            if x == 0:
-                planes[f] = place([P, PACK, C1], BF16, "planes%d" % f)
-            nc.vector.scalar_tensor_tensor(
-                planes[f][:, 2 * x : 2 * x + 2, :], silu_sb[f, x][:], 1.0, half_sb[f][:, 2 * x : 2 * x + 2, :], ALU.subtract, ALU.mult
-            )
-
-        def interleave_da(f):
+        def second_product(f):
             da_bf[f] = place([P, C1, PACK], BF16, "da_bf%d" % f)
-            nc.vector.tensor_copy(
-                out=da_bf[f][:].rearrange("q (c i) t -> q c t i", i=PACK),
-                in_=planes[f][:].rearrange("q t (c i) -> q c t i", i=PACK),
+            nc.vector.tensor_tensor(
+                da_bf[f][:].rearrange("q (c i) t -> q c t i", i=PACK),
+                sig[f][:].rearrange("q t (c i) -> q c t i", i=PACK),
+                half_sb[f][:].rearrange("q t (c i) -> q c t i", i=PACK),
+                ALU.mult,
             )
 
         def quantize_da(f):
@@ -286,14 +278,12 @@ def tile_moe_hib_silu_kernel(
             (nc.sync, nc.scalar)[q // 2].dma_start(
                 out=dy_s[QUADRANT * q : QUADRANT * (q + 1), :], in_=rows_q.partition_broadcast(QUADRANT // SCALE_ROWS)
             )
-        load_half_wet(0, 0)
-        load_half_wet(0, 1)
         nc.sync.dma_start(out=dy_w[:], in_=dy_words[0].rearrange("p t d -> p (t d)").bitcast(I32))
+        load_wet(0)
         load_gate(0)
         nc.sync.dma_start(offs2_sb[:], offs2)
-        load_a(0)
         load_wet(1)
-        load_a(1)
+        load_a(0)
         load_wet(2)
         load_gate(1)
         load_wet(3)
@@ -304,6 +294,7 @@ def tile_moe_hib_silu_kernel(
             )
         load_wgt(0)
         nc.sync.dma_start(offs_sb[:], offs)
+        load_a(1)
         for f in range(2, G):
             load_wet(2 * f)
             load_wet(2 * f + 1)
@@ -312,43 +303,43 @@ def tile_moe_hib_silu_kernel(
             load_wgt(f - 1)
         load_wgt(G - 1)
 
-        nc.vector.memset(zero[:], 0.0)
-        nc.scalar.activation(out=no_bias[:], in_=zero[:], func=ACT.Silu)
+        nc.vector.memset(zero[:], -128.0)
+        nc.scalar.activation(out=no_bias[:], in_=zero[:], func=ACT.Sigmoid)
 
         for f in range(G):
             gather_scales(f)
+        for f in range(G - 1):
+            gather_words(f)
         round_half_wet(0, 0, "scalar")
-        round_half_wet(0, 1, "scalar")
-        gather_words(0)
+        round_half_wet(0, 1, "vector")
         quantize_wet(0)
-        gather_words(1)
+        gather_words(G - 1)
         fetch_z(0)
-        for t in range(PACK):
+        for t in range(PACK - 1):
             scatter_z(0, t, "scalar")
-        factors(0)
-        gather_words(2)
+        sigmoid_of(0)
         round_wet(1)
         quantize_wet(1)
-        gather_words(3)
+        scatter_z(0, PACK - 1, "vector")
         fetch_z(1)
         for t in range(PACK):
             scatter_z(1, t, "scalar")
-        factors(1)
         round_wet(2)
+        bend_of(0, 0)
         quantize_wet(2)
         round_wet(3)
         fetch_z(2)
         for t in range(PACK - 1):
             scatter_z(2, t, "scalar")
+        bend_of(0, 1)
         quantize_wet(3)
         for t in range(PACK):
             first_product(0, t)
-        second_product(0, 0)
-        second_product(0, 1)
         fetch_z(3)
         for t in range(PACK - 1):
             scatter_z(3, t, "scalar")
-        interleave_da(0)
+        sigmoid_of(1)
+        second_product(0)
         scatter_z(2, PACK - 1, "vector")
         quantize_da(0)
         scatter_z(3, PACK - 1, "vector")
@@ -356,7 +347,7 @@ def tile_moe_hib_silu_kernel(
         for f in range(2):
             round_on_gpsimd(2 * f + 4)
             round_on_gpsimd(2 * f + 5)
-            factors(f + 2)
+            sigmoid_of(f + 2)
             fetch_dx(f, 0, 2, "vector")
             fetch_dx(f, 2, 2, "vector")
             scatter_dx(f, 0, "vector")
@@ -369,17 +360,15 @@ def tile_moe_hib_silu_kernel(
             if f == 1:
                 scatter_dx(f, 2, "scalar", slice(C2, C1))
             quantize_pair(f + 2)
-            first_product(f + 1, 0)
-            first_product(f + 1, 1)
+            bend_of(f + 1, 0)
             fetch_plane(f + 2, 0)
             scatter_plane(f + 2, 0, "scalar")
-            first_product(f + 1, 2)
-            first_product(f + 1, 3)
-            second_product(f + 1, 0)
-            second_product(f + 1, 1)
+            bend_of(f + 1, 1)
+            for t in range(PACK):
+                first_product(f + 1, t)
             fetch_plane(f + 2, 1)
             scatter_plane(f + 2, 1, "scalar")
-            interleave_da(f + 1)
+            second_product(f + 1)
             fetch_plane(f + 2, 3 if f == 1 else 2)
             quantize_da(f + 1)
             fetch_plane(f + 2, 2 if f == 1 else 3)
@@ -388,16 +377,15 @@ def tile_moe_hib_silu_kernel(
 
         fetch_dx(2, 0, 1, "vector")
         scatter_dx(2, 0, "scalar")
-        for t in (0, 1, 3):
-            first_product(3, t)
-        second_product(3, 0)
-        first_product(3, 2)
+        bend_of(3, 0)
+        bend_of(3, 1)
         fetch_dx(2, 1, 1, "vector")
         scatter_dx(2, 1, "scalar")
-        second_product(3, 1)
+        for t in (0, 1, 3, 2):
+            first_product(3, t)
         fetch_dx(2, 2, 1, "vector")
         scatter_dx(2, 2, "scalar")
-        interleave_da(3)
+        second_product(3)
         fetch_dx(2, 3, 1, "vector")
         quantize_da(3)
         scatter_dx(2, 3, "vector")

@@ -33,32 +33,35 @@ TAKES_PLACE_OF = {
     **{"wet_s%d" % e: "wet_s%d" % (e % 2) for e in range(2 * BY_EXPERT)},
     **{"z_win%d_%d" % (f, t): "z_win%d_%d" % (f % 2, t) for f in range(G) for t in range(PACK - 1)},
     **{"sig%d" % f: "sig%d" % (f % 2) for f in range(G)},
-    "slot_w3": "grouped0",
-    "z_win0_3": "grouped1",
-    "z_win2_3": "grouped1",
-    "grouped2": "raw0",
-    "bend0": "raw2",
-    "grouped3": "raw1",
-    "half0": "raw3",
-    "z_win1_3": "raw3",
-    "z_win3_3": "raw3",
-    "da_bf0": "raw0",
-    "grouped4": "raw0",
-    "da_c0": "raw1",
-    "grouped5": "raw1",
+    **{"grouped%d_%d" % (e, x): "grouped%d_%d" % (e % 2, x) for e in range(2 * BY_EXPERT) for x in range(2)},
+    "slot_w1": "raw0",
+    "bend0": "grouped1_0",
+    "slot_w2": "grouped1_0",
+    "half0": "raw1",
+    "z_win1_3": "raw1",
+    "da_bf0": "grouped0_0",
+    "grouped5": "grouped0_0",
     "pair_c2": "raw5",
-    "bend1": "raw1",
-    "da_bf1": "raw2",
-    "grouped6": "raw2",
+    "bend1": "grouped0_0",
+    "dx0_3_0": "grouped0_0",
+    "half1": "raw2",
+    "z_win2_3": "raw2",
+    "da_bf1": "raw3",
+    "grouped6_0": "raw3",
     "da_c1": "raw4",
     "grouped7": "raw4",
+    "grouped6_1": "grouped4_1",
     "pair_c3": "raw7",
     "bend2": "raw4",
-    "bend3": "raw4",
-    "half2": "half1",
-    "half3": "z_plane3_3",
-    **{"dx%d_%d" % (f, b): "dx%d_%d" % (f % 2, b) for f in range(2) for b in (0, 2)},
-    **{"z_plane3_%d" % t: "z_plane2_%d" % t for t in range(PACK - 1)},
+    "dx1_2_0": "raw4",
+    "half2": "grouped0_0",
+    "bend3": "grouped0_0",
+    "dx1_3_0": "grouped0_0",
+    "z_win3_3": "raw1",
+    "half3": "raw6",
+    "dx2_2_0": "raw6",
+    "dx2_3_128": "da_c3",
+    **{"z_plane3_%d" % t: "z_plane2_%d" % t for t in range(PACK)},
 }
 
 
@@ -82,7 +85,7 @@ def tile_moe_hib_silu_kernel(
         no_bias = held.tile([P, 1], F32, name="no_bias")
         wgt_s = held.tile([P, W], U8, name="wgt_s", align_bytes=64)
         wgt_w = [held.tile([P, W], I32, name="wgt_w%d" % f, align_bytes=64) for f in range(G)]
-        gate_sb = [held.tile([P, C1], F32, name="gate%d" % f, align_bytes=64) for f in range(G)]
+        gate_sb = {}
         raw, grouped, wet_c, wet_s, slot_w, slot_s, z_sb, z_win, z_bank = {}, {}, {}, {}, {}, {}, {}, {}, {}
         a_sb, sig, bend, half_sb, da_bf, da_c, da_s = {}, {}, {}, {}, {}, {}, {}
         dx_sb, out_sb, dx_bank, pair, plane_bank, z_plane = {}, {}, {}, {}, {}, {}
@@ -94,15 +97,20 @@ def tile_moe_hib_silu_kernel(
             raw[e] = place([P, PACK, W], F32, "raw%d" % e)
             nc.sync.dma_start(out=raw[e][:], in_=wet[e].rearrange("(p j) i -> p j i", j=PACK))
 
-        def load_gate(f):
-            nc.sync.dma_start(out=gate_sb[f][:], in_=gate[:, f * C1 : (f + 1) * C1])
+        def load_gate(first, count):
+            tile = place([P, count * C2], F32, "gate%d" % first)
+            nc.sync.dma_start(out=tile[:], in_=gate[:, first * C2 : (first + count) * C2])
+            gate_sb[first, count] = tile[:]
 
         def load_wgt(f):
             nc.sync.dma_start(out=wgt_w[f][:], in_=wgt_words[f, 0].rearrange("p k d -> p (k d)").bitcast(I32))
 
-        def load_a(f):
-            a_sb[f] = place([P, PACK, C1], F32, "a%d" % f)
-            nc.sync.dma_start(out=a_sb[f][:], in_=a.rearrange("(q t) j -> q t j", t=PACK)[:, :, f * C1 : (f + 1) * C1])
+        def load_a(f, pairs=(0, 1)):
+            tile = place([P, 2 * len(pairs), C1], F32, "a%d_%d" % (f, pairs[0]))
+            ts = slice(2 * pairs[0], 2 * pairs[-1] + 2)
+            nc.sync.dma_start(out=tile[:], in_=a.rearrange("(q t) j -> q t j", t=PACK)[:, ts, f * C1 : (f + 1) * C1])
+            for x in pairs:
+                a_sb[f, x] = tile[:, 2 * (x - pairs[0]) : 2 * (x - pairs[0]) + 2, :]
 
         def copy_on(engine, to, src):
             if engine == "vector":
@@ -116,28 +124,31 @@ def tile_moe_hib_silu_kernel(
             else:
                 nc.scalar.activation(out=to, in_=src, func=ACT.Copy)
 
-        def round_wet(e):
-            grouped[e] = place([P, PACK, P, PACK], BF16, "grouped%d" % e)
-            nc.vector.tensor_copy(
-                out=grouped[e][:].rearrange("p t m j -> p m j t"),
-                in_=raw[e][:].rearrange("p j (m t) -> p m j t", t=PACK),
-            )
-
         def round_on_gpsimd(e):
             grouped[e] = place([P, PACK, P, PACK], BF16, "grouped%d" % e)
             to = grouped[e][:].rearrange("p t m j -> p m j t")
             src = raw[e][:].rearrange("p j (m t) -> p m j t", t=PACK)
             nc.gpsimd.tensor_scalar(to, src, 1.0, 0.0, ALU.mult, ALU.add)
 
+        def round_planes(e, x, engine):
+            grouped[e, x] = place([P, 2, P, PACK], BF16, "grouped%d_%d" % (e, x))
+            to = grouped[e, x][:].rearrange("p t m j -> p m j t")
+            src = raw[e][:].rearrange("p j (m t) -> p m j t", t=PACK)[:, :, :, 2 * x : 2 * x + 2]
+            if engine != "gpsimd":
+                copy_on(engine, to, src)
+            else:
+                nc.gpsimd.tensor_scalar(to, src, 1.0, 0.0, ALU.mult, ALU.add)
+
         def quantize_pair(f):
             codes = place([P, 2 * W], U32, "pair_c%d" % f)
             scales = place([P, 2 * W], U8, "pair_s%d" % f)
-            for x in (1, 0):
-                columns = slice(x * W, (x + 1) * W)
+            pieces = [(W, grouped[2 * f + 1]), (0, grouped[2 * f, 0]), (W // 2, grouped[2 * f, 1])]
+            for first, piece in pieces:
+                columns = slice(first, first + piece.shape[1] * P)
                 nc.vector.quantize_mx(
                     out=codes[:, columns].bitcast(FP8X4),
                     scales=scales[:, columns],
-                    in_=grouped[2 * f + x][:].rearrange("p t m j -> p (t m j)"),
+                    in_=piece[:].rearrange("p t m j -> p (t m j)"),
                 )
             for t in range(PACK):
                 if t % 2 == 0:
@@ -157,25 +168,24 @@ def tile_moe_hib_silu_kernel(
 
         def fetch_plane(f, t):
             z_plane[f, t] = place([P, C1], F32, "z_plane%d_%d" % (f, t))
-            nc.vector.scalar_tensor_tensor(z_plane[f, t][:], plane_bank[f, t], -1.0, gate_sb[f][:], ALU.mult, ALU.mult)
+            nc.vector.scalar_tensor_tensor(z_plane[f, t][:], plane_bank[f, t], -1.0, gate_sb[2 * f, 2], ALU.mult, ALU.mult)
 
         def scatter_plane(f, t, engine):
             z_win[f, t] = place([P, (f + 1) * C1], F32, "z_win%d_%d" % (f, t))
             scatter_on(engine, z_win[f, t][:].indirect(offs2_sb[:, entries(f * C1, C1)]), z_plane[f, t][:])
 
-        def round_half_wet(e, h, engine):
-            if h == 0:
-                grouped[e] = place([P, PACK, P, PACK], BF16, "grouped%d" % e)
-            to = grouped[e][:].rearrange("p t m j -> p m j t")[:, h * P // 2 : (h + 1) * P // 2]
-            src = raw[e][:].rearrange("p j (m t) -> p m j t", t=PACK)[:, h * P // 2 : (h + 1) * P // 2]
-            copy_on(engine, to, src)
-
-        def quantize_wet(e):
-            wet_c[e] = place([P, W], U32, "wet_c%d" % e)
-            wet_s[e] = place([P, W], U8, "wet_s%d" % e)
+        def quantize_planes(e, x):
+            if x == 0:
+                wet_c[e] = place([P, W], U32, "wet_c%d" % e)
+                wet_s[e] = place([P, W], U8, "wet_s%d" % e)
+            columns = slice(x * W // 2, (x + 1) * W // 2)
             nc.vector.quantize_mx(
-                out=wet_c[e][:].bitcast(FP8X4), scales=wet_s[e][:], in_=grouped[e][:].rearrange("p t m j -> p (t m j)")
+                out=wet_c[e][:, columns].bitcast(FP8X4),
+                scales=wet_s[e][:, columns],
+                in_=grouped[e, x][:].rearrange("p t m j -> p (t m j)"),
             )
+
+        def expert_product(e):
             z_bank[e] = psum.tile([P, PACK, C2], F32, name="bank")
             f, x = divmod(e, 2)
             for t in range(PACK):
@@ -193,15 +203,16 @@ def tile_moe_hib_silu_kernel(
             slot_s[f] = place([P, C1], U8, "slot_s%d" % f)
             nc.vector.tensor_copy(slot_s[f][:], dy_s[:].bitcast(U8).indirect(dst_sb[:, entries(f * C1, C1)]))
 
-        def gather_words(f):
-            slot_w[f] = place([P, C1], U32, "slot_w%d" % f)
-            nc.vector.tensor_copy(slot_w[f][:], dy_w[:].bitcast(U32).indirect(dst_sb[:, entries(f * C1, C1)]))
+        def gather_words(first, count):
+            tile = place([P, count * C1], U32, "slot_w%d" % first)
+            nc.vector.tensor_copy(tile[:], dy_w[:].bitcast(U32).indirect(dst_sb[:, entries(first * C1, count * C1)]))
+            for x in range(count):
+                slot_w[first + x] = tile[:, x * C1 : (x + 1) * C1]
 
         def fetch_z(e):
-            f, x = divmod(e, 2)
             z_sb[e] = place([P, PACK, C2], F32, "z_sb%d" % e)
             to = z_sb[e][:]
-            weight = gate_sb[f][:, x * C2 : (x + 1) * C2].unsqueeze(1).to_broadcast([P, PACK, C2])
+            weight = gate_sb[e, 1].unsqueeze(1).to_broadcast([P, PACK, C2])
             nc.vector.scalar_tensor_tensor(to, z_bank[e][:], -1.0, weight, ALU.mult, ALU.mult)
 
         def scatter_z(e, t, engine):
@@ -210,15 +221,16 @@ def tile_moe_hib_silu_kernel(
                 z_win[f, t] = place([P, max(2, f + 1) * C1], F32, "z_win%d_%d" % (f, t))
             scatter_on(engine, z_win[f, t][:].indirect(offs2_sb[:, entries(e * C2, C2)]), z_sb[e][:, t, :])
 
-        def sigmoid_of(f):
-            sig[f] = place([P, PACK, C1], F32, "sig%d" % f)
-            nc.scalar.activation(out=sig[f][:], in_=a_sb[f][:], func=ACT.Sigmoid, bias=no_bias[:])
+        def sigmoid_of(f, x):
+            if x == 0:
+                sig[f] = place([P, PACK, C1], F32, "sig%d" % f)
+            nc.scalar.activation(out=sig[f][:, 2 * x : 2 * x + 2, :], in_=a_sb[f, x], func=ACT.Sigmoid, bias=no_bias[:])
 
         def bend_of(f, x):
             if x == 0:
                 bend[f] = place([P, PACK, C1], F32, "bend%d" % f)
             ts = slice(2 * x, 2 * x + 2)
-            nc.vector.scalar_tensor_tensor(bend[f][:, ts, :], sig[f][:, ts, :], 1.0, a_sb[f][:, ts, :], ALU.subtract, ALU.mult)
+            nc.vector.scalar_tensor_tensor(bend[f][:, ts, :], sig[f][:, ts, :], 1.0, a_sb[f, x], ALU.subtract, ALU.mult)
 
         def first_product(f, t):
             if f not in half_sb:
@@ -229,7 +241,7 @@ def tile_moe_hib_silu_kernel(
 
         def second_product(f):
             da_bf[f] = place([P, C1, PACK], BF16, "da_bf%d" % f)
-            nc.vector.tensor_tensor(
+            nc.gpsimd.tensor_tensor(
                 da_bf[f][:].rearrange("q (c i) t -> q c t i", i=PACK),
                 sig[f][:].rearrange("q t (c i) -> q c t i", i=PACK),
                 half_sb[f][:].rearrange("q t (c i) -> q c t i", i=PACK),
@@ -256,19 +268,20 @@ def tile_moe_hib_silu_kernel(
                     stop=True,
                 )
 
-        def fetch_dx(f, first, count, engine):
-            tile = place([P, count, C1], F32, "dx%d_%d" % (f, first))
-            copy_on(engine, tile[:], dx_bank[f, first // 2][:, first % 2 : first % 2 + count, :])
+        def fetch_dx(f, first, count, engine, slots=slice(0, C1)):
+            tile = place([P, count, slots.stop - slots.start], F32, "dx%d_%d_%d" % (f, first, slots.start))
+            copy_on(engine, tile[:], dx_bank[f, first // 2][:, first % 2 : first % 2 + count, slots])
             for c in range(count):
-                dx_sb[f, first + c] = tile[:, c, :]
+                dx_sb[f, first + c, slots.start] = tile[:, c, :]
 
         def scatter_dx(f, c, engine, slots=slice(0, C1)):
             if c not in out_sb:
                 out_sb[c] = place([P, T], F32, "out_sb%d" % c)
             listed = entries(f * C1 + slots.start, slots.stop - slots.start)
-            scatter_on(engine, out_sb[c][:].indirect(offs_sb[:, listed]), dx_sb[f, c][:, slots])
+            scatter_on(engine, out_sb[c][:].indirect(offs_sb[:, listed]), dx_sb[f, c, slots.start])
             if f == G - 1:
-                nc.sync.dma_start(out=out[c * P : (c + 1) * P, :], in_=out_sb[c][:])
+                queue = nc.scalar if c == 1 else nc.sync
+                queue.dma_start(out=out[c * P : (c + 1) * P, :], in_=out_sb[c][:])
 
         nc.gpsimd.memset(wgt_s[:].bitcast(I32), 0)
 
@@ -278,15 +291,20 @@ def tile_moe_hib_silu_kernel(
             (nc.sync, nc.scalar)[q // 2].dma_start(
                 out=dy_s[QUADRANT * q : QUADRANT * (q + 1), :], in_=rows_q.partition_broadcast(QUADRANT // SCALE_ROWS)
             )
-        nc.sync.dma_start(out=dy_w[:], in_=dy_words[0].rearrange("p t d -> p (t d)").bitcast(I32))
         load_wet(0)
-        load_gate(0)
+        nc.sync.dma_start(out=dy_w[:], in_=dy_words[0].rearrange("p t d -> p (t d)").bitcast(I32))
+        load_gate(0, 1)
         nc.sync.dma_start(offs2_sb[:], offs2)
         load_wet(1)
-        load_a(0)
         load_wet(2)
-        load_gate(1)
+        load_gate(1, 1)
+        load_a(0, (0,))
         load_wet(3)
+        load_a(0, (1,))
+        load_gate(2, 1)
+        load_gate(3, 1)
+        load_a(1)
+        load_wet(4)
         for q in range(QUADRANTS):
             nc.sync.dma_start(
                 out=wgt_s[QUADRANT * q : QUADRANT * q + G * SCALE_ROWS, :].bitcast(I32),
@@ -294,71 +312,79 @@ def tile_moe_hib_silu_kernel(
             )
         load_wgt(0)
         nc.sync.dma_start(offs_sb[:], offs)
-        load_a(1)
-        for f in range(2, G):
-            load_wet(2 * f)
-            load_wet(2 * f + 1)
-            load_a(f)
-            load_gate(f)
-            load_wgt(f - 1)
-        load_wgt(G - 1)
+        load_wet(5)
+        load_gate(4, 2)
+        load_a(2)
+        load_wet(6)
+        load_wgt(1)
+        load_wet(7)
+        load_gate(6, 2)
+        load_a(3)
+        load_wgt(2)
+        load_wgt(3)
 
         nc.vector.memset(zero[:], -128.0)
         nc.scalar.activation(out=no_bias[:], in_=zero[:], func=ACT.Sigmoid)
 
         for f in range(G):
             gather_scales(f)
-        for f in range(G - 1):
-            gather_words(f)
-        round_half_wet(0, 0, "scalar")
-        round_half_wet(0, 1, "vector")
-        quantize_wet(0)
-        gather_words(G - 1)
+        round_planes(0, 1, "scalar")
+        round_planes(0, 0, "vector")
+        gather_words(0, 1)
+        quantize_planes(0, 0)
+        quantize_planes(0, 1)
+        expert_product(0)
+        gather_words(1, 1)
         fetch_z(0)
-        for t in range(PACK - 1):
-            scatter_z(0, t, "scalar")
-        sigmoid_of(0)
-        round_wet(1)
-        quantize_wet(1)
-        scatter_z(0, PACK - 1, "vector")
-        fetch_z(1)
         for t in range(PACK):
-            scatter_z(1, t, "scalar")
-        round_wet(2)
+            scatter_z(0, t, "scalar")
+        sigmoid_of(0, 0)
+        for e in range(1, 2 * BY_EXPERT):
+            round_planes(e, 0, "vector")
+            if e > 1:
+                fetch_z(e - 1)
+                for t in range(PACK if e == 2 else PACK - 1):
+                    scatter_z(e - 1, t, "scalar")
+            round_planes(e, 1, "vector")
+            quantize_planes(e, 0)
+            if e == 2:
+                sigmoid_of(0, 1)
+            quantize_planes(e, 1)
+            expert_product(e)
+        sigmoid_of(1, 0)
+        sigmoid_of(1, 1)
         bend_of(0, 0)
-        quantize_wet(2)
-        round_wet(3)
-        fetch_z(2)
-        for t in range(PACK - 1):
-            scatter_z(2, t, "scalar")
         bend_of(0, 1)
-        quantize_wet(3)
         for t in range(PACK):
             first_product(0, t)
-        fetch_z(3)
-        for t in range(PACK - 1):
-            scatter_z(3, t, "scalar")
-        sigmoid_of(1)
         second_product(0)
-        scatter_z(2, PACK - 1, "vector")
+        fetch_z(3)
+        gather_words(2, 2)
+        scatter_z(3, 0, "scalar")
+        scatter_z(3, 1, "scalar")
+        scatter_z(3, 2, "vector")
+        round_planes(4, 0, "scalar")
+        round_planes(4, 1, "scalar")
         quantize_da(0)
-        scatter_z(3, PACK - 1, "vector")
+        scatter_z(2, PACK - 1, "vector")
 
         for f in range(2):
-            round_on_gpsimd(2 * f + 4)
+            if f == 1:
+                round_planes(2 * f + 4, 0, "gpsimd")
+                round_planes(2 * f + 4, 1, "scalar")
             round_on_gpsimd(2 * f + 5)
-            sigmoid_of(f + 2)
-            fetch_dx(f, 0, 2, "vector")
-            fetch_dx(f, 2, 2, "vector")
-            scatter_dx(f, 0, "vector")
-            scatter_dx(f, 1, "vector")
+            sigmoid_of(f + 2, 0)
+            sigmoid_of(f + 2, 1)
+            fetch_dx(f, 0, 1, "vector")
+            fetch_dx(f, 1, 1, "vector")
+            if f == 0:
+                scatter_z(3, PACK - 1, "vector")
+            if f == 0:
+                fetch_dx(f, 2, 1, "vector")
+            scatter_dx(f, 0, "scalar" if f == 0 else "vector")
+            scatter_dx(f, 1, "scalar")
             if f == 0:
                 scatter_dx(f, 2, "scalar")
-            else:
-                scatter_dx(f, 2, "vector", slice(0, C2))
-            scatter_dx(f, 3, "scalar")
-            if f == 1:
-                scatter_dx(f, 2, "scalar", slice(C2, C1))
             quantize_pair(f + 2)
             bend_of(f + 1, 0)
             fetch_plane(f + 2, 0)
@@ -366,34 +392,49 @@ def tile_moe_hib_silu_kernel(
             bend_of(f + 1, 1)
             for t in range(PACK):
                 first_product(f + 1, t)
-            fetch_plane(f + 2, 1)
-            scatter_plane(f + 2, 1, "scalar")
             second_product(f + 1)
-            fetch_plane(f + 2, 3 if f == 1 else 2)
-            quantize_da(f + 1)
-            fetch_plane(f + 2, 2 if f == 1 else 3)
+            fetch_plane(f + 2, 1)
+            fetch_plane(f + 2, 2)
+            if f == 0:
+                fetch_dx(f, 3, 1, "vector")
+            fetch_plane(f + 2, 3)
+            if f == 1:
+                fetch_dx(f, 2, 1, "vector")
+            scatter_plane(f + 2, 1, "scalar")
             scatter_plane(f + 2, 2, "scalar")
-            scatter_plane(f + 2, 3, "vector" if f == 1 else "scalar")
+            if f == 0:
+                scatter_dx(f, 3, "vector")
+                quantize_da(f + 1)
+                scatter_plane(f + 2, 3, "vector")
+            else:
+                scatter_dx(f, 2, "scalar")
+                scatter_plane(f + 2, 3, "vector")
+                quantize_da(f + 1)
 
-        fetch_dx(2, 0, 1, "vector")
-        scatter_dx(2, 0, "scalar")
         bend_of(3, 0)
         bend_of(3, 1)
-        fetch_dx(2, 1, 1, "vector")
+        fetch_dx(2, 0, 1, "scalar")
+        fetch_dx(2, 1, 1, "scalar")
+        scatter_dx(2, 0, "scalar")
         scatter_dx(2, 1, "scalar")
         for t in (0, 1, 3, 2):
             first_product(3, t)
-        fetch_dx(2, 2, 1, "vector")
-        scatter_dx(2, 2, "scalar")
         second_product(3)
-        fetch_dx(2, 3, 1, "vector")
+        low, high = slice(0, C2), slice(C2, C1)
+        fetch_dx(2, 3, 1, "vector", low)
+        fetch_dx(1, 3, 1, "vector")
+        scatter_dx(2, 3, "vector", low)
+        scatter_dx(1, 3, "vector")
+        fetch_dx(2, 2, 1, "vector")
         quantize_da(3)
-        scatter_dx(2, 3, "vector")
+        scatter_dx(2, 2, "vector")
         fetch_dx(3, 0, 1, "scalar")
         fetch_dx(3, 1, 1, "scalar")
         fetch_dx(3, 2, 1, "vector")
         fetch_dx(3, 3, 1, "vector")
+        fetch_dx(2, 3, 1, "vector", high)
         scatter_dx(3, 0, "scalar")
-        scatter_dx(3, 1, "scalar")
         scatter_dx(3, 2, "vector")
+        scatter_dx(3, 1, "scalar")
+        scatter_dx(2, 3, "vector", high)
         scatter_dx(3, 3, "vector")

@@ -16,7 +16,7 @@ P = 128
 PACK = 4
 T = 1024
 G, C1 = 4, 256
-E, C2 = 8, 128
+C2 = 128
 W = 512
 ROW_TILES = W // P
 LIST = 16
@@ -25,44 +25,34 @@ SCALE_ROWS = 4
 BANKS = 8
 FLOPS = 2 * 2 * W * W * T
 
-BY_EXPERT = 2
+SINGLE_EXPERTS = 4
+LAST_PLANE = PACK - 1
 
-TAKES_PLACE_OF = {
-    "wet_c2": "wet_c0",
-    "wet_c3": "wet_c1",
-    **{"wet_s%d" % e: "wet_s%d" % (e % 2) for e in range(2 * BY_EXPERT)},
-    **{"z_win%d_%d" % (f, t): "z_win%d_%d" % (f % 2, t) for f in range(G) for t in range(PACK - 1)},
-    **{"sig%d" % f: "sig%d" % (f % 2) for f in range(G)},
-    **{"grouped%d_%d" % (e, x): "grouped%d_%d" % (e % 2, x) for e in range(2 * BY_EXPERT) for x in range(2)},
-    "slot_w1": "raw0",
-    "bend0": "grouped1_0",
-    "slot_w2": "grouped1_0",
-    "half0": "raw1",
-    "z_win1_3": "raw1",
-    "da_bf0": "grouped0_0",
-    "grouped5": "grouped0_0",
-    "pair_c2": "raw5",
-    "bend1": "grouped0_0",
-    "dx0_3_0": "grouped0_0",
-    "half1": "raw2",
-    "z_win2_3": "raw2",
-    "da_bf1": "raw3",
-    "grouped6_0": "raw3",
-    "da_c1": "raw4",
-    "grouped7": "raw4",
-    "grouped6_1": "grouped4_1",
-    "pair_c3": "raw7",
-    "bend2": "raw4",
-    "dx1_2_0": "raw4",
-    "half2": "grouped0_0",
-    "bend3": "grouped0_0",
-    "dx1_3_0": "grouped0_0",
-    "z_win3_3": "raw1",
-    "half3": "raw6",
-    "dx2_2_0": "raw6",
-    "dx2_3_128": "da_c3",
-    **{"z_plane3_%d" % t: "z_plane2_%d" % t for t in range(PACK)},
-}
+CHAINS = (
+    ("raw0", "slot_w1"),
+    ("grouped1_0", "grouped3_0", "bend0", "slot_w2"),
+    ("raw1", "half0", "z_win1_3", "z_win3_3"),
+    ("raw2", "half1", "z_win2_3"),
+    ("grouped0_0", "grouped2_0", "da_bf0", "grouped5", "bend1", "dx0_3_0", "half2", "bend3", "dx1_3_0"),
+    ("raw3", "da_bf1", "grouped6_0"),
+    ("raw4", "da_c1", "grouped7", "bend2", "dx1_2_0"),
+    ("raw5", "pair_c2"),
+    ("raw7", "pair_c3"),
+    ("raw6", "half3", "dx2_2_0"),
+    ("da_c3", "dx2_3_128"),
+    ("sig0", "sig2"),
+    ("sig1", "sig3"),
+    ("grouped0_1", "grouped2_1"),
+    ("grouped1_1", "grouped3_1"),
+    ("grouped4_1", "grouped6_1"),
+    ("wet_c0", "wet_c2"),
+    ("wet_c1", "wet_c3"),
+    ("wet_s0", "wet_s2"),
+    ("wet_s1", "wet_s3"),
+    *(("z_win%d_%d" % (f, t), "z_win%d_%d" % (f + 2, t)) for f in range(2) for t in range(LAST_PLANE)),
+    *(("z_plane2_%d" % t, "z_plane3_%d" % t) for t in range(PACK)),
+)
+PLACE_OF = {name: chain[0] for chain in CHAINS for name in chain}
 
 
 def tile_moe_hib_silu_kernel(
@@ -74,21 +64,20 @@ def tile_moe_hib_silu_kernel(
         psum = ctx.enter_context(tc.psum_pool(name="psum", bufs=BANKS))
 
         def place(shape, dtype, name):
-            return held.tile(shape, dtype, name=name, tag=TAKES_PLACE_OF.get(name, name), align_bytes=64)
+            return held.tile(shape, dtype, name=name, tag=PLACE_OF.get(name, name), align_bytes=64)
 
         offs_sb = held.tile([P, T // LIST], U16, name="offs_sb")
         offs2_sb = held.tile([P, T // LIST], U16, name="offs2_sb")
         dst_sb = held.tile([P, T // LIST], U16, name="dst_sb")
         dy_w = held.tile([P, T], I32, name="dy_w", align_bytes=64)
         dy_s = held.tile([P, T // 4], I32, name="dy_s", align_bytes=64)
-        zero = held.tile([P, 1], F32, name="zero")
+        far_left = held.tile([P, 1], F32, name="far_left")
         no_bias = held.tile([P, 1], F32, name="no_bias")
         wgt_s = held.tile([P, W], U8, name="wgt_s", align_bytes=64)
         wgt_w = [held.tile([P, W], I32, name="wgt_w%d" % f, align_bytes=64) for f in range(G)]
-        gate_sb = {}
-        raw, grouped, wet_c, wet_s, slot_w, slot_s, z_sb, z_win, z_bank = {}, {}, {}, {}, {}, {}, {}, {}, {}
-        a_sb, sig, bend, half_sb, da_bf, da_c, da_s = {}, {}, {}, {}, {}, {}, {}
-        dx_sb, out_sb, dx_bank, pair, plane_bank, z_plane = {}, {}, {}, {}, {}, {}
+        raw, grouped, wet_c, wet_s, slot_w, slot_s, gate_sb = {}, {}, {}, {}, {}, {}, {}
+        z_bank, z_sb, plane_bank, z_plane, z_win = {}, {}, {}, {}, {}
+        a_sb, sig, bend, half_sb, da_bf, dx_bank, dx_sb, out_sb = {}, {}, {}, {}, {}, {}, {}, {}
 
         def entries(first, count):
             return slice(first // LIST, (first + count) // LIST)
@@ -134,12 +123,12 @@ def tile_moe_hib_silu_kernel(
             grouped[e, x] = place([P, 2, P, PACK], BF16, "grouped%d_%d" % (e, x))
             to = grouped[e, x][:].rearrange("p t m j -> p m j t")
             src = raw[e][:].rearrange("p j (m t) -> p m j t", t=PACK)[:, :, :, 2 * x : 2 * x + 2]
-            if engine != "gpsimd":
-                copy_on(engine, to, src)
-            else:
+            if engine == "gpsimd":
                 nc.gpsimd.tensor_scalar(to, src, 1.0, 0.0, ALU.mult, ALU.add)
+            else:
+                copy_on(engine, to, src)
 
-        def quantize_pair(f):
+        def multiply_pair(f):
             codes = place([P, 2 * W], U32, "pair_c%d" % f)
             scales = place([P, 2 * W], U8, "pair_s%d" % f)
             pieces = [(W, grouped[2 * f + 1]), (0, grouped[2 * f, 0]), (W // 2, grouped[2 * f, 1])]
@@ -211,9 +200,8 @@ def tile_moe_hib_silu_kernel(
 
         def fetch_z(e):
             z_sb[e] = place([P, PACK, C2], F32, "z_sb%d" % e)
-            to = z_sb[e][:]
             weight = gate_sb[e, 1].unsqueeze(1).to_broadcast([P, PACK, C2])
-            nc.vector.scalar_tensor_tensor(to, z_bank[e][:], -1.0, weight, ALU.mult, ALU.mult)
+            nc.vector.scalar_tensor_tensor(z_sb[e][:], z_bank[e][:], -1.0, weight, ALU.mult, ALU.mult)
 
         def scatter_z(e, t, engine):
             f = e // 2
@@ -232,14 +220,14 @@ def tile_moe_hib_silu_kernel(
             ts = slice(2 * x, 2 * x + 2)
             nc.vector.scalar_tensor_tensor(bend[f][:, ts, :], sig[f][:, ts, :], 1.0, a_sb[f, x], ALU.subtract, ALU.mult)
 
-        def first_product(f, t):
+        def half_of(f, t):
             if f not in half_sb:
                 half_sb[f] = place([P, PACK, C1], F32, "half%d" % f)
             nc.vector.scalar_tensor_tensor(
                 half_sb[f][:, t, :], bend[f][:, t, :], 1.0, z_win[f, t][:, f * C1 : (f + 1) * C1], ALU.subtract, ALU.mult
             )
 
-        def second_product(f):
+        def da_of(f):
             da_bf[f] = place([P, C1, PACK], BF16, "da_bf%d" % f)
             nc.gpsimd.tensor_tensor(
                 da_bf[f][:].rearrange("q (c i) t -> q c t i", i=PACK),
@@ -248,11 +236,11 @@ def tile_moe_hib_silu_kernel(
                 ALU.mult,
             )
 
-        def quantize_da(f):
-            da_c[f] = place([P, C1], U32, "da_c%d" % f)
-            da_s[f] = place([P, C1], U8, "da_s%d" % f)
+        def multiply_da(f):
+            codes = place([P, C1], U32, "da_c%d" % f)
+            scales = place([P, C1], U8, "da_s%d" % f)
             nc.vector.quantize_mx(
-                out=da_c[f][:].bitcast(FP8X4), scales=da_s[f][:], in_=da_bf[f][:].rearrange("q j t -> q (j t)")
+                out=codes[:].bitcast(FP8X4), scales=scales[:], in_=da_bf[f][:].rearrange("q j t -> q (j t)")
             )
             for c in range(ROW_TILES):
                 if c % 2 == 0:
@@ -262,17 +250,16 @@ def tile_moe_hib_silu_kernel(
                     out=dx_bank[f, c // 2][:, c % 2, :],
                     lhsT=wgt_w[f][:, ks].bitcast(FP8X4),
                     lhsT_scale=wgt_s[SCALE_ROWS * f : P, ks],
-                    rhs=da_c[f][:].bitcast(FP8X4),
-                    rhs_scale=da_s[f][:],
+                    rhs=codes[:].bitcast(FP8X4),
+                    rhs_scale=scales[:],
                     start=True,
                     stop=True,
                 )
 
-        def fetch_dx(f, first, count, engine, slots=slice(0, C1)):
-            tile = place([P, count, slots.stop - slots.start], F32, "dx%d_%d_%d" % (f, first, slots.start))
-            copy_on(engine, tile[:], dx_bank[f, first // 2][:, first % 2 : first % 2 + count, slots])
-            for c in range(count):
-                dx_sb[f, first + c, slots.start] = tile[:, c, :]
+        def fetch_dx(f, c, engine, slots=slice(0, C1)):
+            tile = place([P, 1, slots.stop - slots.start], F32, "dx%d_%d_%d" % (f, c, slots.start))
+            copy_on(engine, tile[:], dx_bank[f, c // 2][:, c % 2 : c % 2 + 1, slots])
+            dx_sb[f, c, slots.start] = tile[:, 0, :]
 
         def scatter_dx(f, c, engine, slots=slice(0, C1)):
             if c not in out_sb:
@@ -280,8 +267,22 @@ def tile_moe_hib_silu_kernel(
             listed = entries(f * C1 + slots.start, slots.stop - slots.start)
             scatter_on(engine, out_sb[c][:].indirect(offs_sb[:, listed]), dx_sb[f, c, slots.start])
             if f == G - 1:
-                queue = nc.scalar if c == 1 else nc.sync
-                queue.dma_start(out=out[c * P : (c + 1) * P, :], in_=out_sb[c][:])
+                rows = slice(c * P, (c + 1) * P)
+                if c == ROW_TILES - 1:
+                    nc.sync.dma_start(out=out[rows, 0 : T // 2], in_=out_sb[c][:, 0 : T // 2])
+                    nc.scalar.dma_start(out=out[rows, T // 2 : T], in_=out_sb[c][:, T // 2 : T])
+                else:
+                    (nc.scalar if c == 1 else nc.sync).dma_start(out=out[rows, :], in_=out_sb[c][:])
+
+        def port_run(f):
+            multiply_pair(f + 1)
+            bend_of(f, 0)
+            fetch_plane(f + 1, 0)
+            scatter_plane(f + 1, 0, "scalar")
+            bend_of(f, 1)
+            for t in range(PACK):
+                half_of(f, t)
+            da_of(f)
 
         nc.gpsimd.memset(wgt_s[:].bitcast(I32), 0)
 
@@ -323,8 +324,8 @@ def tile_moe_hib_silu_kernel(
         load_wgt(2)
         load_wgt(3)
 
-        nc.vector.memset(zero[:], -128.0)
-        nc.scalar.activation(out=no_bias[:], in_=zero[:], func=ACT.Sigmoid)
+        nc.vector.memset(far_left[:], -128.0)
+        nc.scalar.activation(out=no_bias[:], in_=far_left[:], func=ACT.Sigmoid)
 
         for f in range(G):
             gather_scales(f)
@@ -339,11 +340,12 @@ def tile_moe_hib_silu_kernel(
         for t in range(PACK):
             scatter_z(0, t, "scalar")
         sigmoid_of(0, 0)
-        for e in range(1, 2 * BY_EXPERT):
+
+        for e in range(1, SINGLE_EXPERTS):
             round_planes(e, 0, "vector")
             if e > 1:
                 fetch_z(e - 1)
-                for t in range(PACK if e == 2 else PACK - 1):
+                for t in range(PACK if e - 1 < 2 else LAST_PLANE):
                     scatter_z(e - 1, t, "scalar")
             round_planes(e, 1, "vector")
             quantize_planes(e, 0)
@@ -356,8 +358,9 @@ def tile_moe_hib_silu_kernel(
         bend_of(0, 0)
         bend_of(0, 1)
         for t in range(PACK):
-            first_product(0, t)
-        second_product(0)
+            half_of(0, t)
+        da_of(0)
+
         fetch_z(3)
         gather_words(2, 2)
         scatter_z(3, 0, "scalar")
@@ -365,74 +368,75 @@ def tile_moe_hib_silu_kernel(
         scatter_z(3, 2, "vector")
         round_planes(4, 0, "scalar")
         round_planes(4, 1, "scalar")
-        quantize_da(0)
-        scatter_z(2, PACK - 1, "vector")
+        multiply_da(0)
 
-        for f in range(2):
-            if f == 1:
-                round_planes(2 * f + 4, 0, "gpsimd")
-                round_planes(2 * f + 4, 1, "scalar")
-            round_on_gpsimd(2 * f + 5)
-            sigmoid_of(f + 2, 0)
-            sigmoid_of(f + 2, 1)
-            fetch_dx(f, 0, 1, "vector")
-            fetch_dx(f, 1, 1, "vector")
-            if f == 0:
-                scatter_z(3, PACK - 1, "vector")
-            if f == 0:
-                fetch_dx(f, 2, 1, "vector")
-            scatter_dx(f, 0, "scalar" if f == 0 else "vector")
-            scatter_dx(f, 1, "scalar")
-            if f == 0:
-                scatter_dx(f, 2, "scalar")
-            quantize_pair(f + 2)
-            bend_of(f + 1, 0)
-            fetch_plane(f + 2, 0)
-            scatter_plane(f + 2, 0, "scalar")
-            bend_of(f + 1, 1)
-            for t in range(PACK):
-                first_product(f + 1, t)
-            second_product(f + 1)
-            fetch_plane(f + 2, 1)
-            fetch_plane(f + 2, 2)
-            if f == 0:
-                fetch_dx(f, 3, 1, "vector")
-            fetch_plane(f + 2, 3)
-            if f == 1:
-                fetch_dx(f, 2, 1, "vector")
-            scatter_plane(f + 2, 1, "scalar")
-            scatter_plane(f + 2, 2, "scalar")
-            if f == 0:
-                scatter_dx(f, 3, "vector")
-                quantize_da(f + 1)
-                scatter_plane(f + 2, 3, "vector")
-            else:
-                scatter_dx(f, 2, "scalar")
-                scatter_plane(f + 2, 3, "vector")
-                quantize_da(f + 1)
+        scatter_z(2, LAST_PLANE, "vector")
+        round_on_gpsimd(5)
+        sigmoid_of(2, 0)
+        sigmoid_of(2, 1)
+        fetch_dx(0, 0, "vector")
+        fetch_dx(0, 1, "vector")
+        scatter_z(3, LAST_PLANE, "vector")
+        fetch_dx(0, 2, "vector")
+        for c in range(ROW_TILES - 1):
+            scatter_dx(0, c, "scalar")
+        port_run(1)
+
+        fetch_plane(2, 1)
+        fetch_plane(2, 2)
+        fetch_dx(0, 3, "vector")
+        fetch_plane(2, LAST_PLANE)
+        scatter_plane(2, 1, "scalar")
+        scatter_plane(2, 2, "scalar")
+        scatter_dx(0, 3, "vector")
+        multiply_da(1)
+
+        scatter_plane(2, LAST_PLANE, "vector")
+        round_planes(6, 0, "gpsimd")
+        round_planes(6, 1, "scalar")
+        round_on_gpsimd(7)
+        sigmoid_of(3, 0)
+        sigmoid_of(3, 1)
+        fetch_dx(1, 0, "vector")
+        fetch_dx(1, 1, "vector")
+        scatter_dx(1, 0, "vector")
+        scatter_dx(1, 1, "scalar")
+        port_run(2)
+
+        fetch_plane(3, 1)
+        fetch_plane(3, 2)
+        fetch_plane(3, LAST_PLANE)
+        fetch_dx(1, 2, "vector")
+        scatter_plane(3, 1, "scalar")
+        scatter_plane(3, 2, "scalar")
+        scatter_dx(1, 2, "scalar")
+        scatter_plane(3, LAST_PLANE, "vector")
+        multiply_da(2)
 
         bend_of(3, 0)
         bend_of(3, 1)
-        fetch_dx(2, 0, 1, "scalar")
-        fetch_dx(2, 1, 1, "scalar")
+        fetch_dx(2, 0, "scalar")
+        fetch_dx(2, 1, "scalar")
         scatter_dx(2, 0, "scalar")
         scatter_dx(2, 1, "scalar")
-        for t in (0, 1, 3, 2):
-            first_product(3, t)
-        second_product(3)
-        low, high = slice(0, C2), slice(C2, C1)
-        fetch_dx(2, 3, 1, "vector", low)
-        fetch_dx(1, 3, 1, "vector")
+        for t in (0, 1, LAST_PLANE, 2):
+            half_of(3, t)
+        da_of(3)
+
+        low, high = slice(0, C1 // 2), slice(C1 // 2, C1)
+        fetch_dx(2, 3, "vector", low)
+        fetch_dx(1, 3, "vector")
         scatter_dx(2, 3, "vector", low)
         scatter_dx(1, 3, "vector")
-        fetch_dx(2, 2, 1, "vector")
-        quantize_da(3)
+        fetch_dx(2, 2, "vector")
+        multiply_da(3)
         scatter_dx(2, 2, "vector")
-        fetch_dx(3, 0, 1, "scalar")
-        fetch_dx(3, 1, 1, "scalar")
-        fetch_dx(3, 2, 1, "vector")
-        fetch_dx(3, 3, 1, "vector")
-        fetch_dx(2, 3, 1, "vector", high)
+
+        fetch_dx(3, 0, "scalar")
+        fetch_dx(3, 1, "scalar")
+        fetch_dx(3, 2, "vector")
+        fetch_dx(3, 3, "vector")
+        fetch_dx(2, 3, "vector", high)
         scatter_dx(3, 0, "scalar")
         scatter_dx(3, 2, "vector")
         scatter_dx(3, 1, "scalar")

from contextlib import ExitStack

import concourse.mybir as mybir

F32 = mybir.dt.float32
BF16 = mybir.dt.bfloat16
I32 = mybir.dt.int32
U32 = mybir.dt.uint32
U16 = mybir.dt.uint16
U8 = mybir.dt.uint8
FP8X4 = mybir.dt.float8_e4m3fn_x4
ACT = mybir.ActivationFunctionType
ALU = mybir.AluOpType

P = 128
PACK = 4
T = 1024
G, C1 = 4, 256
C2 = 128
W = 512
ROW_TILES = W // P
LIST = 16
QUADRANTS, QUADRANT = 4, 32
SCALE_ROWS = 4
BANKS = 8
FLOPS = 2 * 2 * W * W * T

SINGLE_EXPERTS = 4
LAST_PLANE = PACK - 1

CHAINS = (
    ("raw0", "slot_w1"),
    ("grouped1_0", "grouped3_0", "bend0", "slot_w2"),
    ("raw1", "half0", "z_win1_3", "z_win3_3"),
    ("raw2", "half1", "z_win2_3"),
    ("grouped0_0", "grouped2_0", "da_bf0", "grouped5", "bend1", "dx0_3_0", "half2", "bend3", "dx1_3_0"),
    ("raw3", "da_bf1", "grouped6_0"),
    ("raw4", "da_c1", "grouped7", "bend2", "dx1_2_0"),
    ("raw5", "pair_c2"),
    ("raw7", "pair_c3"),
    ("raw6", "half3", "dx2_2_0"),
    ("da_c3", "dx2_3_128"),
    ("sig0", "sig2"),
    ("sig1", "sig3"),
    ("grouped0_1", "grouped2_1"),
    ("grouped1_1", "grouped3_1"),
    ("grouped4_1", "grouped6_1"),
    ("wet_c0", "wet_c2"),
    ("wet_c1", "wet_c3"),
    ("wet_s0", "wet_s2"),
    ("wet_s1", "wet_s3"),
    *(("z_win%d_%d" % (f, t), "z_win%d_%d" % (f + 2, t)) for f in range(2) for t in range(LAST_PLANE)),
    *(("z_plane2_%d" % t, "z_plane3_%d" % t) for t in range(PACK)),
)
PLACE_OF = {name: chain[0] for chain in CHAINS for name in chain}


def tile_moe_hib_silu_kernel(
    tc, dy_words, dy_scales, wet, wgt_words, wgt_scales, a, gate, offs, offs2, dst, out
):
    nc = tc.nc
    with ExitStack() as ctx:
        held = ctx.enter_context(tc.tile_pool(name="held", bufs=1))
        psum = ctx.enter_context(tc.psum_pool(name="psum", bufs=BANKS))

        def place(shape, dtype, name):
            return held.tile(shape, dtype, name=name, tag=PLACE_OF.get(name, name), align_bytes=64)

        offs_sb = held.tile([P, T // LIST], U16, name="offs_sb")
        offs2_sb = held.tile([P, T // LIST], U16, name="offs2_sb")
        dst_sb = held.tile([P, T // LIST], U16, name="dst_sb")
        dy_w = held.tile([P, T], I32, name="dy_w", align_bytes=64)
        dy_s = held.tile([P, T // 4], I32, name="dy_s", align_bytes=64)
        far_left = held.tile([P, 1], F32, name="far_left")
        no_bias = held.tile([P, 1], F32, name="no_bias")
        wgt_s = held.tile([P, W], U8, name="wgt_s", align_bytes=64)
        wgt_w = [held.tile([P, W], I32, name="wgt_w%d" % f, align_bytes=64) for f in range(G)]
        raw, grouped, wet_c, wet_s, slot_w, slot_s, gate_sb = {}, {}, {}, {}, {}, {}, {}
        z_bank, z_sb, plane_bank, z_plane, z_win = {}, {}, {}, {}, {}
        a_sb, sig, bend, half_sb, da_bf, dx_bank, dx_sb, out_sb = {}, {}, {}, {}, {}, {}, {}, {}

        def entries(first, count):
            return slice(first // LIST, (first + count) // LIST)

        def load_wet(e):
            raw[e] = place([P, PACK, W], F32, "raw%d" % e)
            nc.sync.dma_start(out=raw[e][:], in_=wet[e].rearrange("(p j) i -> p j i", j=PACK))

        def load_gate(first, count):
            tile = place([P, count * C2], F32, "gate%d" % first)
            nc.sync.dma_start(out=tile[:], in_=gate[:, first * C2 : (first + count) * C2])
            gate_sb[first, count] = tile[:]

        def load_wgt(f):
            nc.sync.dma_start(out=wgt_w[f][:], in_=wgt_words[f, 0].rearrange("p k d -> p (k d)").bitcast(I32))

        def load_a(f, pairs=(0, 1)):
            tile = place([P, 2 * len(pairs), C1], F32, "a%d_%d" % (f, pairs[0]))
            ts = slice(2 * pairs[0], 2 * pairs[-1] + 2)
            nc.sync.dma_start(out=tile[:], in_=a.rearrange("(q t) j -> q t j", t=PACK)[:, ts, f * C1 : (f + 1) * C1])
            for x in pairs:
                a_sb[f, x] = tile[:, 2 * (x - pairs[0]) : 2 * (x - pairs[0]) + 2, :]

        def copy_on(engine, to, src):
            if engine == "vector":
                nc.vector.tensor_copy(out=to, in_=src)
            else:
                nc.scalar.copy(out=to, in_=src)

        def scatter_on(engine, to, src):
            if engine == "vector":
                nc.vector.tensor_copy(to, src)
            else:
                nc.scalar.activation(out=to, in_=src, func=ACT.Copy)

        def round_on_gpsimd(e):
            grouped[e] = place([P, PACK, P, PACK], BF16, "grouped%d" % e)
            to = grouped[e][:].rearrange("p t m j -> p m j t")
            src = raw[e][:].rearrange("p j (m t) -> p m j t", t=PACK)
            nc.gpsimd.tensor_scalar(to, src, 1.0, 0.0, ALU.mult, ALU.add)

        def round_planes(e, x, engine):
            grouped[e, x] = place([P, 2, P, PACK], BF16, "grouped%d_%d" % (e, x))
            to = grouped[e, x][:].rearrange("p t m j -> p m j t")
            src = raw[e][:].rearrange("p j (m t) -> p m j t", t=PACK)[:, :, :, 2 * x : 2 * x + 2]
            if engine == "gpsimd":
                nc.gpsimd.tensor_scalar(to, src, 1.0, 0.0, ALU.mult, ALU.add)
            else:
                copy_on(engine, to, src)

        def multiply_pair(f):
            codes = place([P, 2 * W], U32, "pair_c%d" % f)
            scales = place([P, 2 * W], U8, "pair_s%d" % f)
            pieces = [(W, grouped[2 * f + 1]), (0, grouped[2 * f, 0]), (W // 2, grouped[2 * f, 1])]
            for first, piece in pieces:
                columns = slice(first, first + piece.shape[1] * P)
                nc.vector.quantize_mx(
                    out=codes[:, columns].bitcast(FP8X4),
                    scales=scales[:, columns],
                    in_=piece[:].rearrange("p t m j -> p (t m j)"),
                )
            for t in range(PACK):
                if t % 2 == 0:
                    bank = psum.tile([P, 2, C1], F32, name="bank")
                plane_bank[f, t] = bank[:, t % 2, :]
                for x in range(2):
                    columns = slice(x * W + t * P, x * W + (t + 1) * P)
                    nc.tensor.matmul_mx(
                        out=bank[:, t % 2, x * C2 : (x + 1) * C2],
                        lhsT=codes[:, columns].bitcast(FP8X4),
                        lhsT_scale=scales[:, columns],
                        rhs=slot_w[f][:, x * C2 : (x + 1) * C2].bitcast(FP8X4),
                        rhs_scale=slot_s[f][:, x * C2 : (x + 1) * C2],
                        start=True,
                        stop=True,
                    )

        def fetch_plane(f, t):
            z_plane[f, t] = place([P, C1], F32, "z_plane%d_%d" % (f, t))
            nc.vector.scalar_tensor_tensor(z_plane[f, t][:], plane_bank[f, t], -1.0, gate_sb[2 * f, 2], ALU.mult, ALU.mult)

        def scatter_plane(f, t, engine):
            z_win[f, t] = place([P, (f + 1) * C1], F32, "z_win%d_%d" % (f, t))
            scatter_on(engine, z_win[f, t][:].indirect(offs2_sb[:, entries(f * C1, C1)]), z_plane[f, t][:])

        def quantize_planes(e, x):
            if x == 0:
                wet_c[e] = place([P, W], U32, "wet_c%d" % e)
                wet_s[e] = place([P, W], U8, "wet_s%d" % e)
            columns = slice(x * W // 2, (x + 1) * W // 2)
            nc.vector.quantize_mx(
                out=wet_c[e][:, columns].bitcast(FP8X4),
                scales=wet_s[e][:, columns],
                in_=grouped[e, x][:].rearrange("p t m j -> p (t m j)"),
            )

        def expert_product(e):
            z_bank[e] = psum.tile([P, PACK, C2], F32, name="bank")
            f, x = divmod(e, 2)
            for t in range(PACK):
                nc.tensor.matmul_mx(
                    out=z_bank[e][:, t, :],
                    lhsT=wet_c[e][:, t * P : (t + 1) * P].bitcast(FP8X4),
                    lhsT_scale=wet_s[e][:, t * P : (t + 1) * P],
                    rhs=slot_w[f][:, x * C2 : (x + 1) * C2].bitcast(FP8X4),
                    rhs_scale=slot_s[f][:, x * C2 : (x + 1) * C2],
                    start=True,
                    stop=True,
                )

        def gather_scales(f):
            slot_s[f] = place([P, C1], U8, "slot_s%d" % f)
            nc.vector.tensor_copy(slot_s[f][:], dy_s[:].bitcast(U8).indirect(dst_sb[:, entries(f * C1, C1)]))

        def gather_words(first, count):
            tile = place([P, count * C1], U32, "slot_w%d" % first)
            nc.vector.tensor_copy(tile[:], dy_w[:].bitcast(U32).indirect(dst_sb[:, entries(first * C1, count * C1)]))
            for x in range(count):
                slot_w[first + x] = tile[:, x * C1 : (x + 1) * C1]

        def fetch_z(e):
            z_sb[e] = place([P, PACK, C2], F32, "z_sb%d" % e)
            weight = gate_sb[e, 1].unsqueeze(1).to_broadcast([P, PACK, C2])
            nc.vector.scalar_tensor_tensor(z_sb[e][:], z_bank[e][:], -1.0, weight, ALU.mult, ALU.mult)

        def scatter_z(e, t, engine):
            f = e // 2
            if (f, t) not in z_win:
                z_win[f, t] = place([P, max(2, f + 1) * C1], F32, "z_win%d_%d" % (f, t))
            scatter_on(engine, z_win[f, t][:].indirect(offs2_sb[:, entries(e * C2, C2)]), z_sb[e][:, t, :])

        def sigmoid_of(f, x):
            if x == 0:
                sig[f] = place([P, PACK, C1], F32, "sig%d" % f)
            nc.scalar.activation(out=sig[f][:, 2 * x : 2 * x + 2, :], in_=a_sb[f, x], func=ACT.Sigmoid, bias=no_bias[:])

        def bend_of(f, x):
            if x == 0:
                bend[f] = place([P, PACK, C1], F32, "bend%d" % f)
            ts = slice(2 * x, 2 * x + 2)
            nc.vector.scalar_tensor_tensor(bend[f][:, ts, :], sig[f][:, ts, :], 1.0, a_sb[f, x], ALU.subtract, ALU.mult)

        def half_of(f, t):
            if f not in half_sb:
                half_sb[f] = place([P, PACK, C1], F32, "half%d" % f)
            nc.vector.scalar_tensor_tensor(
                half_sb[f][:, t, :], bend[f][:, t, :], 1.0, z_win[f, t][:, f * C1 : (f + 1) * C1], ALU.subtract, ALU.mult
            )

        def da_of(f):
            da_bf[f] = place([P, C1, PACK], BF16, "da_bf%d" % f)
            nc.gpsimd.tensor_tensor(
                da_bf[f][:].rearrange("q (c i) t -> q c t i", i=PACK),
                sig[f][:].rearrange("q t (c i) -> q c t i", i=PACK),
                half_sb[f][:].rearrange("q t (c i) -> q c t i", i=PACK),
                ALU.mult,
            )

        def multiply_da(f):
            codes = place([P, C1], U32, "da_c%d" % f)
            scales = place([P, C1], U8, "da_s%d" % f)
            nc.vector.quantize_mx(
                out=codes[:].bitcast(FP8X4), scales=scales[:], in_=da_bf[f][:].rearrange("q j t -> q (j t)")
            )
            for c in range(ROW_TILES):
                if c % 2 == 0:
                    dx_bank[f, c // 2] = psum.tile([P, 2, C1], F32, name="bank")
                ks = slice(c * P, (c + 1) * P)
                nc.tensor.matmul_mx(
                    out=dx_bank[f, c // 2][:, c % 2, :],
                    lhsT=wgt_w[f][:, ks].bitcast(FP8X4),
                    lhsT_scale=wgt_s[SCALE_ROWS * f : P, ks],
                    rhs=codes[:].bitcast(FP8X4),
                    rhs_scale=scales[:],
                    start=True,
                    stop=True,
                )

        def fetch_dx(f, c, engine, slots=slice(0, C1)):
            tile = place([P, 1, slots.stop - slots.start], F32, "dx%d_%d_%d" % (f, c, slots.start))
            copy_on(engine, tile[:], dx_bank[f, c // 2][:, c % 2 : c % 2 + 1, slots])
            dx_sb[f, c, slots.start] = tile[:, 0, :]

        def scatter_dx(f, c, engine, slots=slice(0, C1)):
            if c not in out_sb:
                out_sb[c] = place([P, T], F32, "out_sb%d" % c)
            listed = entries(f * C1 + slots.start, slots.stop - slots.start)
            scatter_on(engine, out_sb[c][:].indirect(offs_sb[:, listed]), dx_sb[f, c, slots.start])
            if f == G - 1:
                rows = slice(c * P, (c + 1) * P)
                if c == ROW_TILES - 1:
                    nc.sync.dma_start(out=out[rows, 0 : T // 2], in_=out_sb[c][:, 0 : T // 2])
                    nc.scalar.dma_start(out=out[rows, T // 2 : T], in_=out_sb[c][:, T // 2 : T])
                else:
                    (nc.scalar if c == 1 else nc.sync).dma_start(out=out[rows, :], in_=out_sb[c][:])

        def port_run(f):
            multiply_pair(f + 1)
            bend_of(f, 0)
            fetch_plane(f + 1, 0)
            scatter_plane(f + 1, 0, "scalar")
            bend_of(f, 1)
            for t in range(PACK):
                half_of(f, t)
            da_of(f)

        nc.gpsimd.memset(wgt_s[:].bitcast(I32), 0)

        nc.sync.dma_start(dst_sb[:], dst)
        for q in range(QUADRANTS):
            rows_q = dy_scales[0, SCALE_ROWS * q : SCALE_ROWS * (q + 1), :].bitcast(I32)
            (nc.sync, nc.scalar)[q // 2].dma_start(
                out=dy_s[QUADRANT * q : QUADRANT * (q + 1), :], in_=rows_q.partition_broadcast(QUADRANT // SCALE_ROWS)
            )
        load_wet(0)
        nc.sync.dma_start(out=dy_w[:], in_=dy_words[0].rearrange("p t d -> p (t d)").bitcast(I32))
        load_gate(0, 1)
        nc.sync.dma_start(offs2_sb[:], offs2)
        load_wet(1)
        load_wet(2)
        load_gate(1, 1)
        load_a(0, (0,))
        load_wet(3)
        load_a(0, (1,))
        load_gate(2, 1)
        load_gate(3, 1)
        load_a(1)
        load_wet(4)
        for q in range(QUADRANTS):
            nc.sync.dma_start(
                out=wgt_s[QUADRANT * q : QUADRANT * q + G * SCALE_ROWS, :].bitcast(I32),
                in_=wgt_scales[:, 0, SCALE_ROWS * q : SCALE_ROWS * (q + 1), :].bitcast(I32),
            )
        load_wgt(0)
        nc.sync.dma_start(offs_sb[:], offs)
        load_wet(5)
        load_gate(4, 2)
        load_a(2)
        load_wet(6)
        load_wgt(1)
        load_wet(7)
        load_gate(6, 2)
        load_a(3)
        load_wgt(2)
        load_wgt(3)

        nc.vector.memset(far_left[:], -128.0)
        nc.scalar.activation(out=no_bias[:], in_=far_left[:], func=ACT.Sigmoid)

        for f in range(G):
            gather_scales(f)
        round_planes(0, 1, "scalar")
        round_planes(0, 0, "vector")
        gather_words(0, 1)
        quantize_planes(0, 0)
        quantize_planes(0, 1)
        expert_product(0)
        gather_words(1, 1)
        fetch_z(0)
        for t in range(PACK):
            scatter_z(0, t, "scalar")
        sigmoid_of(0, 0)

        for e in range(1, SINGLE_EXPERTS):
            round_planes(e, 0, "vector")
            if e > 1:
                fetch_z(e - 1)
                for t in range(PACK if e - 1 < 2 else LAST_PLANE):
                    scatter_z(e - 1, t, "scalar")
            round_planes(e, 1, "vector")
            quantize_planes(e, 0)
            if e == 2:
                sigmoid_of(0, 1)
            quantize_planes(e, 1)
            expert_product(e)
        sigmoid_of(1, 0)
        sigmoid_of(1, 1)
        bend_of(0, 0)
        bend_of(0, 1)
        for t in range(PACK):
            half_of(0, t)
        da_of(0)

        fetch_z(3)
        gather_words(2, 2)
        scatter_z(3, 0, "scalar")
        scatter_z(3, 1, "scalar")
        scatter_z(3, 2, "vector")
        round_planes(4, 0, "scalar")
        round_planes(4, 1, "scalar")
        multiply_da(0)

        scatter_z(2, LAST_PLANE, "vector")
        round_on_gpsimd(5)
        sigmoid_of(2, 0)
        sigmoid_of(2, 1)
        fetch_dx(0, 0, "vector")
        fetch_dx(0, 1, "vector")
        scatter_z(3, LAST_PLANE, "vector")
        fetch_dx(0, 2, "vector")
        for c in range(ROW_TILES - 1):
            scatter_dx(0, c, "scalar")
        port_run(1)

        fetch_plane(2, 1)
        fetch_plane(2, 2)
        fetch_dx(0, 3, "vector")
        fetch_plane(2, LAST_PLANE)
        scatter_plane(2, 1, "scalar")
        scatter_plane(2, 2, "scalar")
        scatter_dx(0, 3, "vector")
        multiply_da(1)

        scatter_plane(2, LAST_PLANE, "vector")
        round_planes(6, 0, "gpsimd")
        round_planes(6, 1, "scalar")
        round_on_gpsimd(7)
        sigmoid_of(3, 0)
        sigmoid_of(3, 1)
        fetch_dx(1, 0, "vector")
        fetch_dx(1, 1, "vector")
        scatter_dx(1, 0, "vector")
        scatter_dx(1, 1, "scalar")
        port_run(2)

        fetch_plane(3, 1)
        fetch_plane(3, 2)
        fetch_plane(3, LAST_PLANE)
        fetch_dx(1, 2, "vector")
        scatter_plane(3, 1, "scalar")
        scatter_plane(3, 2, "scalar")
        scatter_dx(1, 2, "scalar")
        scatter_plane(3, LAST_PLANE, "vector")
        multiply_da(2)

        bend_of(3, 0)
        bend_of(3, 1)
        fetch_dx(2, 0, "scalar")
        fetch_dx(2, 1, "scalar")
        scatter_dx(2, 0, "scalar")
        scatter_dx(2, 1, "scalar")
        for t in (0, 1, LAST_PLANE, 2):
            half_of(3, t)
        da_of(3)

        low, high = slice(0, C1 // 2), slice(C1 // 2, C1)
        fetch_dx(2, 3, "vector", low)
        fetch_dx(1, 3, "vector")
        scatter_dx(2, 3, "vector", low)
        scatter_dx(1, 3, "vector")
        fetch_dx(2, 2, "vector")
        multiply_da(3)
        scatter_dx(2, 2, "vector")

        fetch_dx(3, 0, "scalar")
        fetch_dx(3, 1, "scalar")
        fetch_dx(3, 2, "vector")
        fetch_dx(3, 3, "vector")
        fetch_dx(2, 3, "vector", high)
        scatter_dx(3, 0, "scalar")
        scatter_dx(3, 2, "vector")
        scatter_dx(3, 1, "scalar")
        scatter_dx(2, 3, "vector", high)
        scatter_dx(3, 3, "vector")
